import numpy as np, ml_dtypes
CORES = [9,25,41,57]
N = 4
BF = ml_dtypes.bfloat16
def gentries(a):
    return np.ascontiguousarray(a.reshape(8, 16, -1).transpose(0, 2, 1)).reshape(8, -1)
def gtable(e):
    e = np.asarray(e); return np.ascontiguousarray(e.reshape(8, -1, 16).transpose(0, 2, 1)).reshape(128, -1).astype(np.int32)
I, V, G, M, RO = 1536, 769, 256, 2048, 2
def grow(J):
    T = J.shape[0]; ar = np.arange(T); ch = np.zeros((T, 2 * I), np.int64); free = np.zeros((T, I + 1), np.int64); free[:, 1] = 1
    for t in range(1, I):
        j = J[:, t]; ch[ar, free[ar, j]] = t; free[ar, j] = 2 * t; free[:, t + 1] = 2 * t + 1
    ch[ar[:, None], free] = I + np.arange(I + 1)[None, :]
    return ch.reshape(T, I, 2)
def trees(rng, kind, lab):
    T = N * 8; k = kind.reshape(T, 1); t = np.arange(I)[None, :]; r = rng.random((T, I))
    level = t + 1 - 2 ** (np.frexp((t + 1).astype(np.float64))[1].astype(np.int64) - 1)
    J = np.where(k == 0, (r * (t + 1)).astype(np.int64), np.where(k == 1, t - np.minimum((4 * r).astype(np.int64), t), np.where(k == 2, t, level)))
    ch = grow(J); b = lab.reshape(T, 1); s = np.arange(I + 1)[None, :]
    pi = np.where(b == 0, np.argsort(rng.random((T, I)), axis=1), np.where(b == 1, t, I - 1 - t))
    lf = I + np.where(b == 0, np.argsort(rng.random((T, I + 1)), axis=1), np.where(b == 1, s, I - s))
    c = np.take_along_axis(np.concatenate([pi, lf], axis=1), ch.reshape(T, 2 * I), 1).reshape(T, I, 2)
    c = np.where(rng.random((T, I, 1)) < 0.5, c[:, :, ::-1], c)
    o = np.zeros_like(c); o[np.arange(T)[:, None], pi] = c
    return o[:, :, 0].reshape(N, 8, I), o[:, :, 1].reshape(N, 8, I)
def parts(rng):
    size = rng.random((N, 8, 1, I + V)); size[..., :I] = 0.4 + 0.6 * size[..., :I]
    h = np.minimum((256 * size * rng.random((N, 8, 16, I + V))).astype(np.int64), 255)
    return h, rng.integers(-50, 51, (N, 8, 16, V)), rng.integers(0, V, (N, 8, N - 1, G))
def pack(h, v, tr, s):
    return {"h0": np.ascontiguousarray(h.reshape(N, 128, I + V)).astype(np.int32), "vel": np.ascontiguousarray(v.reshape(N, 128, V)).astype(np.int32),
            "kl": np.stack([gtable(a) for a in tr[0]]), "kr": np.stack([gtable(a) for a in tr[1]]), "sl": np.stack([gtable(a.reshape(8, -1)) for a in s])}
def setup_inputs(rng):
    h, v, s = parts(rng)
    return pack(h, v, trees(rng, rng.integers(0, 2, (N, 8)), np.zeros((N, 8), np.int64)), s)
def setup_inputs_ties(rng):
    h, v, s = parts(rng)
    h[:, ::2] = 8 * rng.integers(0, 4, (N, 4, 1, I + V)); h[:, ::2, :, :I] += 16
    v[:, ::2] = 8 * rng.integers(-1, 2, (N, 4, 1, V))
    h[:, 1::2] = 100 + (rng.random((N, 4, 16, I + V)) < 0.0625); v[:, 1::2] = rng.integers(-1, 2, (N, 4, 1, V))
    return pack(h, v, trees(rng, rng.integers(0, 4, (N, 8)), rng.integers(0, 3, (N, 8))), s)
def setup_inputs_chain(rng):
    h, v, s = parts(rng)
    kind = np.tile(np.array([2, 3, 2, 1, 2, 3, 2, 0]), (N, 1)); lab = rng.integers(0, 3, (N, 8)); lab[:, 0] = np.arange(N) % 3; lab[:, 4] = (np.arange(N) + 1) % 3
    for g in (0, 4): h[:, g, :, :I] = 255; h[:, g, :, I:] = 0
    lab[:, 2] = 1 + np.arange(N) % 2; node = np.arange(I)[None, :]
    depth = np.where(lab[:, 2:3] == 1, node, I - 1 - node)
    h[:, 2, :, :I] = rng.integers(0, 128, (N, 16, I)) + 128 * (depth % 2)[:, None, :]; h[:, 2, :, I:] = 0
    return pack(h, v, trees(rng, kind, lab), s)
def setup_inputs_edge(rng):
    h, v, s = parts(rng)
    h = 255 * (rng.random(h.shape) < rng.random((N, 8, 1, I + V))).astype(np.int64); h[:, 3, :, :I] = 255; h[:, 3, :, I:] = 0
    v = 127 * rng.integers(-1, 2, v.shape); s[:, ::2] = (V - 1) * rng.integers(0, 2, (N, 4, N - 1, G))
    lab = rng.integers(1, 3, (N, 8)); lab[:, 0] = 1; lab[:, 1] = 2
    tr = trees(rng, rng.integers(0, 4, (N, 8)), lab)
    c = np.stack([tr[0][0, 0], tr[1][0, 0]], axis=1)
    w = int(c[0][c[0] != 1][0]); low = np.concatenate([np.array([w]), c[1], c[w:w + 1].reshape(-1)]); low = low[low < I + V]
    h[0, 0][:, low] = 0; h[0, 0][:, 1] = 255
    return pack(h, v, tr, s)
def setup_inputs_alike(rng):
    h, v, s = parts(rng); kl, kr = trees(rng, np.zeros((N, 8), np.int64), np.zeros((N, 8), np.int64))
    kl[:] = kl[:, :1]; kr[:] = kr[:, :1]
    g = rng.permutation(8); h[:, g[0], :, :I] = 0; h[:, g[1:3]] = h[:, g[1:3], :1]
    s = rng.choice(np.array([0, V - 1, V // 2, 3]), s.shape)
    return pack(h, v, (kl, kr), s)
def setup_inputs_spread(rng):
    h, v, s = parts(rng)
    h = np.minimum((np.exp2(1 + 8 * rng.random((N, 8, 1, I + V))) * rng.random(h.shape)).astype(np.int64), 255)
    v = np.minimum((np.exp2(7 * rng.random((N, 8, 1, V))) * rng.random(v.shape)).astype(np.int64), 127) * (2 * rng.integers(0, 2, v.shape) - 1)
    return pack(h, v, trees(rng, rng.integers(0, 4, (N, 8)), np.zeros((N, 8), np.int64)), s)
def check_inputs(d):
    bad = []
    for k, lo, hi in (("h0", 0, 255), ("vel", -127, 127), ("kl", 0, 2 * I), ("kr", 0, 2 * I), ("sl", 0, V - 1)):
        if np.min(d[k]) < lo or np.max(d[k]) > hi: bad.append("range of " + k)
    if bad: return bad
    for q in range(N):
        c = np.concatenate([gentries(d["kl"][q]), gentries(d["kr"][q])], axis=1).astype(np.int64); o = np.sort(c, axis=1)
        if np.any(o[:, 1:] == o[:, :-1]):
            bad.append("children all differ"); break
        up = np.tile(np.arange(2 * I + 1), (8, 1)); np.put_along_axis(up, c, np.tile(np.arange(I), (8, 2)), 1)
        for i in range(13): up = np.take_along_axis(up, up, 1)
        if np.any(up != up[:, :1]):
            bad.append("one tree"); break
    return bad
def reference(h0, vel, kl, kr, sl):
    E = 2 * I + 1; at = np.arange(I)
    H = np.zeros((N, 8, 16, E), np.int64); H[..., :I + V] = h0.reshape(N, 8, 16, I + V)
    v = vel.astype(np.int64).reshape(N, 8, 16, V); s = np.stack([gentries(a) for a in sl]).astype(np.int64).reshape(N, 8, N - 1, G)
    K = np.stack([np.stack([gentries(kl[q]), gentries(kr[q])], axis=1) for q in range(N)]).astype(np.int64)
    for rnd in range(RO):
        for q in range(N):
            for d in range(1, N):
                o = (q - d) % N; j = I + V + (d - 1) * G
                H[q, :, :, j:j + G] = np.take_along_axis(H[o, :, :, I:I + V], s[o, :, d - 1][:, None, :], 2)
        hc = [np.take_along_axis(H, K[:, :, a][:, :, None, :], 3) for a in (0, 1)]
        best = np.zeros((N, 8, I), np.int64); ca = np.zeros_like(best); cb = np.zeros_like(best)
        for a in (0, 1):
            inner = K[:, :, a] < I; u = np.where(inner, K[:, :, a], 0); su = np.add.reduce(hc[a], axis=2)
            for b in (0, 1):
                z = np.take_along_axis(K[:, :, 1 - b], u, 2)
                gain = su - np.add.reduce(np.maximum(hc[1 - a], np.take_along_axis(H, z[:, :, None, :], 3)), axis=2)
                more = inner & (gain > best); best = np.where(more, gain, best); ca = np.where(more, a, ca); cb = np.where(more, b, cb)
        key = np.full((N, 8, E + 1), -1, np.int64); key[..., :I] = np.where(best > 0, M * best + at, -1)
        par = np.full((N, 8, E), E, np.int64)
        for a in (0, 1): np.put_along_axis(par, K[:, :, a], np.tile(at, (N, 8, 1)), 2)
        near = np.take_along_axis(key, par[..., :I], 2)
        for a in (0, 1): near = np.maximum(near, np.take_along_axis(key, K[:, :, a], 2))
        q, g, n = np.nonzero(key[..., :I] > near); a = ca[q, g, n]; b = cb[q, g, n]
        u = K[q, g, a, n]; w = K[q, g, 1 - a, n]; x = K[q, g, b, u]
        K[q, g, 1 - a, n] = x; K[q, g, b, u] = w
        new = np.maximum(np.take_along_axis(H, K[:, :, 0][:, :, None, :], 3), np.take_along_axis(H, K[:, :, 1][:, :, None, :], 3))
        H[..., I:I + V] = np.minimum(np.maximum(H[..., I:I + V] + v, 0), 255); H[..., :I] = new
    return {"yh": H[..., :I + V].reshape(N, 128, I + V).astype(np.float32), "yk": K.reshape(N, 8, 2 * I).astype(np.float32)}

@@ -1,0 +1,507 @@
+from concourse.bass import DstId, RemoteDMATransfer
+from concourse.mybir import AluOpType, ActivationFunctionType
+
+NI, NV, NG = 1536, 769, 256
+SH = 7
+DUM = NI + SH
+GH = NI + NV + SH
+WID = GH + 3 * NG
+
+SCRATCH = {
+    "KI": ("sbuf", [128, 2, 96], "int32"), "SLI": ("sbuf", [128, 48], "int32"),
+    "HLI": ("sbuf", [128, NV], "int32"), "HII": ("sbuf", [128, NI], "int32"), "VI": ("sbuf", [128, NV], "int32"),
+    "VB": ("sbuf", [128, NV], "bfloat16"), "YT": ("sbuf", [128, NV], "float32"),
+    "H0": ("sbuf", [128, WID], "bfloat16"), "H1": ("sbuf", [128, WID], "bfloat16"),
+    "GS0": ("sbuf", [128, 3 * NG], "bfloat16"), "GS1": ("sbuf", [128, 3 * NG], "bfloat16"),
+    "W1": ("sbuf", [128, WID], "bfloat16"), "W2": ("sbuf", [128, WID], "float32"),
+    "W2B": ("sbuf", [128, DUM + 1], "bfloat16"), "SRC": ("sbuf", [128, NI], "float32"),
+    "WB": ("sbuf", [128, DUM + 1], "float32"), "VV": ("sbuf", [128, DUM + 1], "float32"),
+    "CW": ("sbuf", [128, DUM + 1], "bfloat16"), "WD": ("sbuf", [128, DUM + 1], "bfloat16"),
+    "HS": ("sbuf", [128, NI], "bfloat16"), "M1": ("sbuf", [128, NI], "bfloat16"), "M2": ("sbuf", [128, NI], "bfloat16"),
+    "TB": ("sbuf", [128, NI], "float32"), "GB": ("sbuf", [128, NI], "bfloat16"), "DP": ("sbuf", [128, NI], "bfloat16"),
+    "OUT": ("sbuf", [128, NI + NV], "float32"),
+    "LA": ("sbuf", [128, 4, 96], "int32"), "LB": ("sbuf", [128, 4, 96], "int32"), "LC": ("sbuf", [128, 2, 96], "int32"),
+    "HI": ("sbuf", [128, 4, 96], "int32"), "LO": ("sbuf", [128, 4, 96], "int32"),
+    "Y7": ("sbuf", [128, 2, 96], "int32"), "IO": ("sbuf", [128, 2, 96], "int32"),
+    "TM": ("sbuf", [128, 32, 96], "float32"),
+    "OF": ("sbuf", [128, 16 * 96], "uint16"),
+    "LI": ("sbuf", [128, 2], "int32"), "COL": ("sbuf", [128, 5], "float32"),
+    "XX": ("sbuf", [128, 768], "bfloat16"), "YY": ("sbuf", [128, 24, 32], "bfloat16"),
+    "XT": ("sbuf", [128, 192], "float32"), "YK": ("sbuf", [128, 6, 32], "float32"), "YC": ("sbuf", [128, 192], "float32"),
+    "UU": ("sbuf", [128, 8, 10, 16], "bfloat16"), "BB": ("sbuf", [128, 2, 8, 16], "bfloat16"),
+    "FF": ("sbuf", [128, 8, 8, 2], "float32"), "MC": ("sbuf", [128, 2, 8, 16], "bfloat16"),
+    "AW": ("sbuf", [128, 3, 8, 16], "bfloat16"),
+    "ID": ("sbuf", [128, 128], "bfloat16"), "ZZ": ("sbuf", [128, 7, 144], "bfloat16"),
+}
+for _k in range(6):
+    SCRATCH["P%d" % _k] = ("psum", [128, 8, 64], "float32")
+SCRATCH["P6"] = ("psum", [128, 512], "float32")
+SCRATCH["P7"] = ("psum", [128, 512], "float32")
+
+SEMAPHORES = ["sv", "sa", "st", "sg", "arr0", "arr1", "sent"] + ["d%d" % _k for _k in range(16)]
+
+
+def rank_program(g, core, T, topo):
+    rank = T.rank_of(core)
+    if rank is None:
+        return
+    A = AluOpType
+    F = ActivationFunctionType
+    n_ranks = len(T.cores)
+    eng = {"v": g.vector, "a": g.scalar, "t": g.tensor, "g": g, "s": g.sync}
+    qsem = {"v": "sv", "a": "sa", "t": "st", "g": "sg"}
+    total = {}
+    waited = {q: {} for q in eng}
+    lastw, readers = {}, {}
+    ndma = [0]
+
+    def sync(q, reads, writes):
+        need = {}
+        deps = [lastw[k] for k in list(reads) + list(writes) if k in lastw]
+        for k in writes:
+            deps += readers.get(k, [])
+        for s, c in deps:
+            if q == "t" and s == "st":
+                continue
+            need[s] = max(need.get(s, 0), c)
+        for s, c in need.items():
+            if waited[q].get(s, 0) < c:
+                eng[q].wait_ge(T.sem[s], c)
+                waited[q][s] = c
+
+    def done(tok, reads, writes):
+        for k in reads:
+            readers.setdefault(k, []).append(tok)
+        for k in writes:
+            lastw[k] = tok
+            readers[k] = []
+
+    def op(q, call, reads, writes):
+        writes = list(writes) + [k for k in reads if k[0] == "P" and k[1:].isdigit()]
+        sync(q, reads, writes)
+        s = qsem[q]
+        call().then_inc(T.sem[s], 1)
+        total[s] = total.get(s, 0) + 1
+        done((s, total[s]), reads, writes)
+
+    def dma(q, out, in_, reads, writes):
+        sync(q, reads, writes)
+        s = "d%d" % ndma[0]
+        ndma[0] += 1
+        eng[q].dma_start(out, in_).then_inc(T.sem[s], 16)
+        total[s] = 16
+        done((s, 16), reads, writes)
+
+    V, S_, PE = g.vector, g.scalar, g.tensor
+
+    def ts(out, in0, s1, s2, o0, o1, reads, writes):
+        if o1 is None:
+            op("v", lambda: V.tensor_scalar(out, in0, s1, None, o0), reads, writes)
+        else:
+            op("v", lambda: V.tensor_scalar(out, in0, s1, s2, o0, o1), reads, writes)
+
+    def tt(out, a, b, o, reads, writes):
+        op("v", lambda: V.tensor_tensor(out, a, b, o), reads, writes)
+
+    def cp(out, in_, reads, writes):
+        op("v", lambda: V.tensor_copy(out, in_), reads, writes)
+
+    def fill(ap, val, writes):
+        op("v", lambda: V.memset(ap, val), [], writes)
+
+    def act(out, in_, func, reads, writes, bias=None, scale=None):
+        kw = {}
+        if bias is not None:
+            kw["bias"] = bias
+        if scale is not None:
+            kw["scale"] = scale
+        op("a", lambda: S_.activation(out, in_, func, **kw), reads, writes)
+
+    def mms(lst, reads, writes):
+        def run():
+            ins = None
+            for out, lhs, rhs, st, sp in lst:
+                ins = PE.matmul(out, lhs, rhs, st, sp)
+            return ins
+        op("t", run, reads, writes)
+
+    def aff(ap, pattern, base, val, key, cmp=None, mult=1):
+        ks = key if isinstance(key, list) else [key]
+        op("g", lambda: g.affine_select(ap, ap, pattern, cmp or A.not_equal, float(val), base, mult), ks, ks)
+
+    def gfill(ap, n, val, writes):
+        op("g", lambda: g.iota(ap, [[0, n]], val, 0, allow_small_or_imprecise_dtypes=True), [], writes)
+
+    def keys(name, n):
+        return ["%s_%d" % (name, i) for i in range(n)]
+
+    PS = [T["P%d" % k] for k in range(8)]
+    O_H = [0, 2, 4]
+    O_S = [6, 8]
+    O_SIB, O_PAR, O_GP, O_SL = [10, 11], [12, 13], 14, 15
+
+    def off(slot, c0=0, c1=96):
+        return T.OF[:, slot * 96 + c0: slot * 96 + c1]
+
+    def okey(slot):
+        return "OF%d" % slot
+
+    def fld(bank, f, n=1):
+        return PS[bank][:, 96 * f: 96 * (f + n)]
+
+    def extract(bank, f, zset, src, c0, reads, first=True, last=True, part=(0, 96)):
+        a, b = part
+        mms([(PS[bank][:, 96 * f + a:96 * f + b], T.ZZ[:, zset, 15 - r:143 - r], src[:, c0 + 16 * a + r:c0 + 16 * b:16],
+              first and r == 0, last and r == 15) for r in range(16)], reads + ["ZZ%d" % zset], ["P%d" % bank])
+
+    def from_y(bank, k, t, mode):
+        return [(PS[bank][:, :, 16 * cl:16 * cl + 16], T.UU[:, 4 * t + cl, 1 - g0:9 - g0, :],
+                 T.YY[:, 8 * k:8 * k + 8, 16 * g0:16 * g0 + 16],
+                 (mode == "alone" and g0 == 0) or (mode == "open" and cl + g0 == 0), mode == "alone" and g0 == 1)
+                for cl in range(4) for g0 in range(2)]
+
+    def digits(LS, lname, l0, l1):
+        rk = ["%s%d" % (lname, l) for l in range(l0, l1)]
+        ts(T.HI[:, l0:l1, :], LS[:, l0:l1, :], 6, None, A.arith_shift_right, None, rk, ["HI%d" % l0])
+        ts(T.LO[:, l0:l1, :], LS[:, l0:l1, :], 63, None, A.bitwise_and, None, rk, ["LO%d" % l0])
+        for l in range(l0, l1):
+            cp(T.XX[:, 2 * l::8], T.HI[:, l, :], ["HI%d" % l0], ["XX%d" % (2 * l)])
+        for l in range(l0, l1):
+            cp(T.XX[:, 2 * l + 1::8], T.LO[:, l, :], ["LO%d" % l0], ["XX%d" % (2 * l + 1)])
+
+    XK = ["XX%d" % f for f in range(8)]
+
+    def turn():
+        op("v", lambda: V.transpose(T.YY[:], T.XX[:]), XK, ["YY"])
+
+    def send(src, skey, dst, sem):
+        sync("g", [skey], [])
+        trs = []
+        for d in range(1, n_ranks):
+            peer = T.cores[(rank + d) % n_ranks]
+            e = topo.engines(core, peer)
+            pick = [0, 2, 1][d - 1]
+            m = (1 << e[pick]) | (1 << e[pick + len(e) // 2])
+            rid, pid, _ = topo.addr(peer)
+            trs.append(RemoteDMATransfer(dst_ids=[DstId(rid=rid, pnc=pid)], dma_engine_mask=m, remote_sem=T.sem[sem],
+                                         src=src[:, (d - 1) * NG:d * NG], dst=dst[:, GH + (d - 1) * NG:GH + d * NG]))
+        g.remote_dma_fused(trs, local_sem=T.sem.sent)
+        total["sent"] = total.get("sent", 0) + 2 * (n_ranks - 1)
+
+    def tm(i, n=1):
+        return T.TM[:, i, :] if n == 1 else T.TM[:, i:i + n, :]
+
+    def pt(bank, i):
+        return PS[bank][:, 2 * i:2 * i + 2, 0:48]
+
+    for r in range(2):
+        total["arr%d" % r] = 2 * (n_ranks - 1)
+        lastw["HG%d" % r] = ("arr%d" % r, 2 * (n_ranks - 1))
+
+    dma("s", T.KI[:, 0, :], T.kl[:], [], ["KI0"])
+    dma("a", T.KI[:, 1, :], T.kr[:], [], ["KI1"])
+    dma("s", T.HLI[:], T.h0[:, NI:NI + NV], [], ["HLI"])
+    dma("a", T.SLI[:], T.sl[:], [], ["SLI"])
+    dma("s", T.HII[:], T.h0[:, 0:NI], [], ["HII"])
+    dma("s", T.VI[:], T.vel[:], [], ["VI"])
+
+    op("g", lambda: g.iota(T.LI[:, 0:1], [[0, 1]], 0, 1), [], ["LI0"])
+    op("g", lambda: g.iota(T.IO[:], [[0, 2], [16, 96]], SH, 0), [], ["IO"])
+    fill(T.UU[:], 0.0, ["UU0", "UU1"])
+    fill(T.W1[:, 0:DUM + 1], 0.0, ["W1"])
+    pu = [[-8, 4], [-32, 4]]
+    aff(T.UU[:, 0:4, 1:9:2, 8:12], pu + [[-1, 4]], -4, 1 / 256, "UU0")
+    aff(T.UU[:, 0:4, 1:9:2, 1], pu, -1, 1 / 256, "UU0")
+    aff(T.UU[:, 0:4, 1:9:2, 0], pu, 0, -1 / 256, "UU0")
+    act(T.W2[:, 0:DUM + 1], T.W1[:, 0:DUM + 1], F.Silu, ["W1"], ["W2"])
+    ts(T.LI[:, 1:2], T.LI[:, 0:1], 15, None, A.bitwise_and, None, ["LI0"], ["LI1"])
+    cp(T.COL[:, 0:1], T.LI[:, 1:2], ["LI1"], ["LANE"])
+    fill(T.XX[:, 2::8], 0.0, ["XX2"])
+    ts(T.Y7[:], T.IO[:], T.COL[:, 0:1], None, A.add, None, ["IO", "LANE"], ["Y7"])
+    fill(T.XX[:, 3::8], 0.0, ["XX3"])
+    ts(T.HI[:, 0, :], T.Y7[:, 0, :], 6, None, A.arith_shift_right, None, ["Y7"], ["HI0"])
+    ts(T.LO[:, 0, :], T.Y7[:, 0, :], 63, None, A.bitwise_and, None, ["Y7"], ["LO0"])
+    cp(T.XX[:, 0::8], T.HI[:, 0, :], ["HI0"], ["XX0"])
+    cp(T.XX[:, 1::8], T.LO[:, 0, :], ["LO0"], ["XX1"])
+    pz = [[-16, 8]]
+    zk = ["ZZ%d" % s for s in range(7)]
+
+    def affz(s0, s1, step, lane, val):
+        aff(T.ZZ[:, s0:s1, 15:128:16], [[step, s1 - s0]] + pz, -lane, val, zk[s0:s1])
+    aff(T.UU[:, 4:8, 1:9:2, 10:12], pu + [[-1, 2]], -4, 1 / 256, "UU1")
+    aff(T.UU[:, 4:8, 1:9:2, 8:10], pu + [[-1, 2]], -6, 1 / 256, "UU1")
+    gfill(T.ZZ[:, 0:4, :], 4 * 144, 0, zk[0:4])
+    affz(2, 4, -2, 8, 64)
+    affz(2, 4, -2, 9, 1)
+    affz(0, 2, -2, 1, 1)
+    affz(0, 1, 0, 0, -64)
+    affz(1, 2, 0, 2, 64)
+    gfill(T.H0[:, 0:SH], SH, 0, ["HZ0"])
+
+    ts(T.LA[:, 2:4, :], T.KI[:], float(SH), None, A.add, None, ["KI0", "KI1"], ["LA2", "LA3"])
+    digits(T.LA, "LA", 2, 4)
+    turn()
+    for k in range(3):
+        mms(from_y(k, k, 0, "alone"), ["YY", "UU0"], ["P%d" % k])
+    cp(off(O_SL, 0, 48), T.SLI[:], ["SLI"], [okey(O_SL)])
+    ts(off(O_H[0], 0, 192), T.KI[:], float(SH), None, A.add, None, ["KI0", "KI1"], [okey(O_H[0]), okey(O_H[0] + 1)])
+    cp(T.GS0[:], T.HLI[:].indirect(off(O_SL, 0, 48)), ["HLI", okey(O_SL)], ["GS0"])
+    send(T.GS0, "GS0", T.H0, "arr0")
+    third = [slice(512 * k, 512 * k + 512) for k in range(3)]
+    third7 = [slice(SH + 512 * k, SH + 512 * k + 512) for k in range(3)]
+    quarter = [slice(SH + 384 * b, SH + 384 * b + 384) for b in range(4)]
+    for k in range(3):
+        act(T.SRC[:, third[k]], PS[k][:], F.Identity, ["P%d" % k], ["SRC_%d" % k], bias=64.0, scale=256.0)
+    act(T.W2[:].indirect(off(O_H[0] + 1)), T.SRC[:], F.Silu, keys("SRC", 3) + [okey(O_H[0] + 1)], ["W2"])
+    act(T.W2B[:, SH:DUM], T.W2[:, SH:DUM], F.Copy, ["W2"], ["W2B"])
+    for k in range(3):
+        cp(T.W1[:].indirect(off(O_H[0], 32 * k, 32 * k + 32)), T.SRC[:, third[k]], ["SRC_%d" % k, okey(O_H[0])], ["W1"])
+    cp(T.H0[:, SH:DUM], T.HII[:], ["HII"], keys("HI0", 6))
+    cp(T.H0[:, DUM:GH], T.HLI[:], ["HLI"], ["HL0"])
+    for t in (1, 0):
+        for k in range(3):
+            mms(from_y(3 * t + k, k, t, "open"), ["YY", "UU0", "UU1"], ["P%d" % (3 * t + k)])
+    gfill(T.AW[:], 384, 0, ["AW0", "AW1"])
+    aff(T.AW[:, 0, :, 4], pz, 0, -1 / 32, "AW0")
+    aff(T.AW[:, 0, :, 4], pz, -1, 1 / 2048, "AW0")
+    aff(T.AW[:, 0, :, 4], pz, -5, 31 / 2048, "AW0")
+    gfill(T.BB[:], 256, 0, ["BB"])
+    gfill(T.BB[:, 0, :, 4:12], 64, 1, ["BB"])
+    gfill(T.BB[:, 1, :, 4:12], 64, -1, ["BB"])
+    aff(T.BB[:, :, :, 4:12], [[0, 2], [-16, 8], [0, 8]], 0, 0, "BB", A.is_ge)
+    aff(T.BB[:, :, :, 4:12], [[0, 2], [16, 8], [0, 8]], 15, 0, "BB", A.is_ge, -1)
+    gfill(T.H1[:, 0:SH], SH, 0, ["HZ1"])
+    gfill(T.H1[:, NI:DUM], SH, 0, ["HI1_5"])
+    for W, wn in ((T.WB, "WB"), (T.VV, "VV"), (T.CW, "CW"), (T.WD, "WD")):
+        gfill(W[:, 0:SH], SH, 0, [wn + "z"])
+        gfill(W[:, DUM:DUM + 1], 1, 0, [wn + "y"])
+    aff(T.AW[:, 1:3, :, 0:2], [[0, 2]] + pz + [[-1, 2]], 0, 1, "AW1")
+    aff(T.AW[:, 1:3, :, 2:4], [[2, 2]] + pz + [[-1, 2]], -10, 1, "AW1")
+    gfill(T.ID[:], 128, 0, ["ID"])
+    aff(T.ID[:], [[-1, 128]], 0, 1, "ID")
+    gfill(T.FF[:], 128, 0, ["FF"])
+    aff(T.FF[:, :, 3:6, :], pz + [[0, 6]], -7, -256, "FF")
+    aff(T.FF[:, :, 4:6, :], pz + [[-1, 4]], -8, 256, "FF")
+    aff(T.FF[:, :, 3, :], pz + [[-1, 2]], -8, 256, "FF")
+    aff(T.FF[:, :, 3:5, :], pz + [[1, 2], [0, 2]], -6, 512, "FF")
+    aff(T.FF[:, :, 3:5, :], pz + [[-1, 2], [0, 2]], -5, -512, "FF")
+    gfill(T.MC[:], 256, 0, ["MC0", "MC1"])
+    aff(T.MC[:, 0, :, 6:12], pz + [[0, 6]], -4, -256, "MC0")
+    aff(T.MC[:, 1, :, 6:12], pz + [[0, 6]], -4, 256, "MC1")
+    gfill(T.ZZ[:, 4:7, :], 3 * 144, 0, zk[4:7])
+    affz(4, 7, 0, 8, 64)
+    affz(4, 7, 0, 9, 1)
+    affz(4, 6, 0, 6, 64)
+    affz(4, 6, 0, 7, 1)
+    affz(5, 7, 4, 10, -64)
+    affz(5, 7, 4, 11, -1)
+    for f, w in ((0, 1 / 32), (1, 1 / 2048)):
+        aff(T.UU[:, :, 1:9:2, 4], [[0, 2]] + pu, -f, w, ["UU0", "UU1"])
+
+    def each_bank(lhs, src, reads, start, ks=(0, 1, 2)):
+        for k in ks:
+            for t in range(2):
+                mms([(PS[3 * t + k][:], lhs, src[:, third7[k]], start, False)], reads, ["P%d" % (3 * t + k)])
+    extract(7, 0, 3, T.W1, SH, ["W1"], True, False)
+    extract(6, 0, 0, T.W1, SH, ["W1"], True, False)
+    each_bank(T.AW[:, 0], T.W1, ["W1", "AW0"], False, (0,))
+    extract(7, 0, 2, T.W2B, SH, ["W2B"], False, True)
+    cp(T.VB[:], T.VI[:], ["VI"], ["VB"])
+    ts(off(O_SIB[0]), fld(7, 0), -4160.0, None, A.add, None, ["P7"], [okey(O_SIB[0])])
+    ts(T.LA[:, 1, :], fld(7, 0), -4160.0, 0.0, A.add, A.max, ["P7"], ["LA1"])
+    ts(T.COL[:, 1:2], T.COL[:, 0:1], 7.0, 0.25, A.is_ge, A.mult, ["LANE"], ["BA"])
+    ts(T.COL[:, 2:3], T.COL[:, 0:1], 6.0, 0.5, A.is_ge, A.mult, ["LANE"], ["BBI"])
+    ts(T.COL[:, 4:5], T.COL[:, 0:1], 8.0, 256.0, A.is_ge, A.mult, ["LANE"], ["B8"])
+    ts(off(O_S[0], 0, 192), T.LA[:, 2:4, :], float(DUM), None, A.min, None, ["LA2", "LA3"], [okey(O_S[0])])
+    ts(T.COL[:, 3:4], T.COL[:, 2:3], -1024.0, T.COL[:, 4:5], A.mult, A.add, ["BBI", "B8"], ["BD"])
+
+    HALVES = ((7, (0, 512)), (6, (512, NV)))
+
+    def leaves_sum(H, r):
+        for b, (c0, c1) in HALVES:
+            o = PS[b][:, 0:c1 - c0]
+            mms([(o, T.ID[:], H[:, DUM + c0:DUM + c1], True, False), (o, T.ID[:], T.VB[:, c0:c1], False, True)],
+                ["ID", "VB", "HL%d" % r], ["P%d" % b])
+
+    def leaves_cap():
+        for b, (c0, c1) in HALVES:
+            act(T.YT[:, c0:c1], PS[b][:, 0:c1 - c0], F.Relu, ["P%d" % b], ["YT%d" % b], bias=255.0, scale=-1.0)
+
+    def leaves_out(out, key):
+        act(out, T.YT[:], F.Relu, ["YT6", "YT7"], [key], bias=255.0, scale=-1.0)
+
+    for r in range(2):
+        H = [T.H0, T.H1][r]
+        LS, ln = [(T.LA, "LA"), (T.LB, "LB")][r]
+        hk = keys("HI%d" % r, 6) + ["HL%d" % r, "HG%d" % r, "HZ%d" % r]
+        oh, os_, osib, opar = O_H[r], O_S[r], O_SIB[r], O_PAR[r]
+        for i, (c0, c1) in enumerate(((0, 16), (16, 32), (32, 64), (64, 96))):
+            act(T.HS[:, 16 * c0:16 * c1], H[:].indirect(off(osib, c0, c1)), F.Copy, hk + [okey(osib)], ["HS_%d" % i])
+
+        def ids(k):
+            if r == 1:
+                for t in range(2):
+                    mms(from_y(3 * t + k, k, t, "part"), ["YY", "UU0", "UU1"], ["P%d" % (3 * t + k)])
+                return
+            each_bank(T.BB[:, 0], T.H0, keys("HI0", 6) + ["BB"], False, (k,))
+            each_bank(T.AW[:, 0], T.W2B, ["W2B", "AW0"], False, (k,))
+            if k > 0:
+                each_bank(T.AW[:, 0], T.W1, ["W1", "AW0"], False, (k,))
+        ids(0)
+        for k in range(3):
+            pieces = ((0, 16, 0), (16, 32, 1)) if k == 0 else ((32 * k, 32 * k + 32, k + 1),)
+            if k < 2:
+                ids(k + 1)
+            for t, M, mn in ((0, T.M1, "M1"), (1, T.M2, "M2")):
+                for c0, c1, i in pieces:
+                    tt(M[:, 16 * c0:16 * c1], H[:].indirect(off(oh + 1 - t, c0, c1)), T.HS[:, 16 * c0:16 * c1], A.max,
+                       hk + [okey(oh + 1 - t), "HS_%d" % i], ["%s_%d" % (mn, i)])
+                mms([(PS[3 * t + k][:], T.BB[:, 1], M[:, third[k]], False, True)],
+                    ["%s_%d" % (mn, i) for c0, c1, i in pieces] + ["BB"], ["P%d" % (3 * t + k)])
+            act(T.TB[:, third[k]], PS[k][:], F.Relu, ["P%d" % k, "BA"], ["TA_%d" % k], bias=T.COL[:, 1:2])
+            if r == 0 and k == 1:
+                extract(6, 0, 0, T.W2B, SH, ["W2B"], False, True)
+        for k in range(3):
+            tt(T.WB[:, third7[k]], PS[3 + k][:], T.TB[:, third[k]], A.max, ["P%d" % (3 + k), "TA_%d" % k], ["WB_%d" % k])
+        wb = keys("WB", 3) + ["WBz", "WBy"]
+        if r == 0:
+            ts(T.LA[:, 0, :], fld(6, 0), 4032.0, float(DUM), A.add, A.min, ["P6"], ["LA0"])
+            ts(off(opar), fld(6, 0), 4032.0, float(DUM), A.add, A.min, ["P6"], [okey(opar)])
+            for b in range(4):
+                mms([(PS[b][:, 0:6, :], T.AW[:, 1], T.W1[:, quarter[b]], True, False),
+                     (PS[b][:, 0:6, :], T.AW[:, 2], T.W2B[:, quarter[b]], False, False)],
+                    ["AW1", "W1", "W2B"], ["P%d" % b])
+        leaves_sum(H, r)
+        for s in range(2):
+            tt(tm(6 + s), LS[:, 1, :], LS[:, 2 + s, :], A.subtract, [ln + "1", ln + str(2 + s)], ["T6_%d" % s])
+        for i in range(6):
+            act(T.TB[:, 256 * i:256 * i + 256], T.WB[:].indirect(off(os_, 16 * i, 16 * i + 16)), F.Identity,
+                wb + [okey(os_), "BBI"], ["TB_%d" % i], bias=T.COL[:, 2:3])
+        for i in range(6):
+            tt(T.VV[:, SH + 256 * i:SH + 256 * i + 256], T.WB[:].indirect(off(os_ + 1, 16 * i, 16 * i + 16)),
+               T.TB[:, 256 * i:256 * i + 256], A.max, wb + [okey(os_), "TB_%d" % i], ["VV_%d" % i])
+        for k in range(3):
+            act(T.SRC[:, third[k]], T.VV[:, third7[k]], F.Copy, ["VV_%d" % (2 * k), "VV_%d" % (2 * k + 1)], ["VC_%d" % k])
+        vk = keys("VV", 6) + ["VVz", "VVy"]
+        for b in range(4):
+            mms([(PS[b][:, 0:6, :], T.FF[:], T.VV[:, quarter[b]], r == 1, False)],
+                ["VV_%d" % i for i in range(384 * b // 256, (384 * b + 383) // 256 + 1)] + ["FF"], ["P%d" % b])
+        leaves_cap()
+        if r == 0:
+            leaves_out(T.H1[:, DUM:GH], "HL1")
+        else:
+            leaves_out(T.OUT[:, NI:NI + NV], "OUTL")
+            dma("s", T.yh[:, NI:NI + NV], T.OUT[:, NI:NI + NV], ["OUTL"], [])
+        for k in range(3):
+            tt(T.CW[:, third7[k]], T.VV[:].indirect(off(opar, 32 * k, 32 * k + 32)), T.SRC[:, third[k]], A.is_lt,
+               vk + [okey(opar), "VC_%d" % k], ["CW_%d" % k])
+            mms([(PS[k][:, 0:6, :], T.MC[:, 1], T.CW[:, quarter[k]], False, False)], keys("CW", k + 1) + ["MC1"], ["P%d" % k])
+        cw = keys("CW", 3)
+        ck = cw + ["CWz", "CWy"]
+        mms([(PS[3][:, 0:6, :], T.MC[:, 1], T.CW[:, quarter[3]], False, False)], cw + ["MC1"], ["P3"])
+        for b in range(4):
+            c0, c1 = 24 * b, 24 * b + 24
+            o = PS[b][:, 0:6, :]
+            cp(T.M2[:, 16 * c0:16 * c1], T.CW[:].indirect(off(os_ + 1, c0, c1)), ck + [okey(os_)], ["CR_%d" % b])
+            act(T.M1[:, 16 * c0:16 * c1], T.CW[:].indirect(off(os_, c0, c1)), F.Copy, ck + [okey(os_)], ["CL_%d" % b])
+            mms([(o, T.MC[:, 0], T.M2[:, 16 * c0:16 * c1], False, False),
+                 (o, T.MC[:, 0], T.M1[:, 16 * c0:16 * c1], False, True)], ["CR_%d" % b, "CL_%d" % b, "MC0"], ["P%d" % b])
+        for b in range(4):
+            if b % 2:
+                act(T.WD[:, quarter[b]], PS[b][:, 0:6, :], F.Relu, ["P%d" % b, "BD"], ["WD_%d" % b], bias=T.COL[:, 3:4])
+            else:
+                ts(T.WD[:, quarter[b]], PS[b][:, 0:6, :], T.COL[:, 3:4], 0.0, A.add, A.max, ["P%d" % b, "BD"], ["WD_%d" % b])
+        wd = keys("WD", 4) + ["WDz", "WDy"]
+        if r == 0:
+            ts(off(O_SL, 48, 96), T.SLI[:], float(SH), None, A.add, None, ["SLI"], ["OSL1"])
+        act(T.DP[:, 0:768], T.WD[:].indirect(off(opar, 0, 48)), F.Copy, wd + [okey(opar)], ["DP_0"])
+        cp(T.DP[:, 768:NI], T.WD[:].indirect(off(opar, 48, 96)), wd + [okey(opar)], ["DP_1"])
+        dp = keys("DP", 2)
+        extract(6, 0, 6, T.WD, SH, wd)
+        extract(7, 0, 4, T.DP, 0, dp)
+        if r == 0:
+            act(T.GS1[:], T.H1[:, NI:GH].indirect(off(O_SL, 48, 96)), F.Copy, ["HL1", "HI1_5", "OSL1"], ["GS1"])
+            send(T.GS1, "GS1", T.H1, "arr1")
+        ts(pt(4, 0), fld(6, 0), 0.0, None, A.is_le, None, ["P6"], ["P4"])
+        ts(pt(5, 0), fld(6, 0), 0.0, -1.0, A.is_ge, A.mult, ["P6"], ["P5"])
+        for s in range(2):
+            tt(tm(2 + s), pt(4 + s, 0), LS[:, 2 + s, :], A.mult, ["P%d" % (4 + s), ln + str(2 + s)], ["T2_%d" % s])
+        for s in range(2):
+            tt(tm(4 + s), fld(6, 0), tm(2 + s), [A.max, A.min][s], ["P6", "T2_%d" % s], ["T4_%d" % s])
+        if r == 0:
+            extract(6, 3, 0, T.DP, 0, dp)
+            tt(tm(12), T.LA[:, 0, :], LS[:, 1, :], A.subtract, ["LA0", "LA1"], ["T12"])
+        ohn = O_H[r + 1]
+        KN = [[T.LB[:, 2, :], T.LB[:, 3, :]], [T.LC[:, 0, :], T.LC[:, 1, :]]][r]
+        nk = [["LB2", "LB3"], ["LC0", "LC1"]][r]
+        for s in range(2):
+            tt(pt(s, 0), fld(7, 0), LS[:, 2 + s, :], A.is_equal, ["P7", ln + str(2 + s)], ["P%d" % s])
+        for s in range(2):
+            tt(pt(2 + s, 0), pt(s, 0), tm(6 + s), A.mult, ["P%d" % s, "T6_%d" % s], ["P%d" % (2 + s)])
+        for s in range(2):
+            tt(KN[s], pt(2 + s, 0), tm(4 + s), [A.add, A.subtract][s], ["P%d" % (2 + s), "T4_%d" % s], [nk[s]])
+        for s in range(2):
+            cp(off(ohn + s), KN[s], [nk[s]], [okey(ohn + s)])
+        if r == 0:
+            ts(off(O_GP), fld(6, 3), 4032.0, float(DUM), A.add, A.min, ["P6"], [okey(O_GP)])
+            ts(tm(15), fld(7, 0), 0.0, None, A.is_equal, None, ["P7"], ["T15"])
+            cp(tm(9), pt(1, 0), ["P1"], ["T9"])
+            extract(6, 1, 3, T.DP, 0, dp)
+            extract(6, 2, 5, T.DP, 0, dp)
+            extract(6, 4, 1, T.DP, 0, dp)
+            tt(tm(16), pt(0, 0), tm(9), A.add, ["P0", "T9"], ["T16"])
+        else:
+            for t in range(6):
+                ts(T.XT[:, 32 * t:32 * t + 32], T.LC[:, :, t::6], -float(SH), None, A.add, None, nk, ["XT_%d" % t])
+            op("v", lambda: V.transpose(T.YK[:], T.XT[:]), keys("XT", 6), ["YK"])
+        for i in range(6):
+            act(T.HS[:, 256 * i:256 * i + 256], H[:].indirect(off(ohn, 16 * i, 16 * i + 16)), F.Copy, hk + [okey(ohn)],
+                ["HE_%d" % i])
+        if r == 1:
+            for g0 in range(2):
+                act(T.YC[:, 96 * g0:96 * g0 + 96], T.YK[:, :, 16 * g0:16 * g0 + 16], F.Copy, ["YK"], ["YC_%d" % g0])
+            for g0 in range(2):
+                dma("a", T.yk[g0::2, :], T.YC[:, 96 * g0:96 * g0 + 96], ["YC_%d" % g0], [])
+        for i in range(6):
+            o = T.H1[:, SH + 256 * i:SH + 256 * i + 256] if r == 0 else T.OUT[:, 256 * i:256 * i + 256]
+            tt(o, H[:].indirect(off(ohn + 1, 16 * i, 16 * i + 16)), T.HS[:, 256 * i:256 * i + 256], A.max,
+               hk + [okey(ohn + 1), "HE_%d" % i], ["HI1_%d" % i if r == 0 else "OUT_%d" % i])
+            if r == 1 and i in (1, 3, 4, 5):
+                i0 = i - 1 if i < 4 else i
+                dma("s", T.yh[:, 256 * i0:256 * i + 256], T.OUT[:, 256 * i0:256 * i + 256],
+                    ["OUT_%d" % j for j in range(i0, i + 1)], [])
+        if r == 0:
+            for j in range(2):
+                act(T.GB[:, 768 * j:768 * j + 768], T.WD[:].indirect(off(O_GP, 48 * j, 48 * j + 48)), F.Copy,
+                    wd + [okey(O_GP)], ["GB_%d" % j])
+                extract(7, 2, 4, T.GB, 0, ["GB_%d" % j], part=(48 * j, 48 * j + 48))
+                extract(7, 3, 3, T.GB, 0, ["GB_%d" % j], part=(48 * j, 48 * j + 48))
+            tt(tm(17), tm(15), LS[:, 1, :], A.mult, ["T15", "LA1"], ["T17"])
+            tt(tm(18), fld(6, 2), tm(16), A.mult, ["P6", "T16"], ["T18"])
+            tt(pt(4, 1), tm(15), tm(16), A.add, ["T15", "T16"], ["P4"])
+            tt(pt(5, 1), fld(6, 1), tm(17), A.add, ["P6", "T17"], ["P5"])
+            tt(tm(27), pt(4, 1), tm(12), A.mult, ["P4", "T12"], ["T27"])
+            tt(tm(10), fld(6, 3), LS[:, 0, :], A.subtract, ["P6", "LA0"], ["T10"])
+            tt(pt(3, 1), pt(5, 1), tm(18), A.add, ["P5", "T18"], ["P3"])
+            tt(tm(11), fld(6, 4), LS[:, 1, :], A.subtract, ["P6", "LA1"], ["T11"])
+            tt(pt(2, 1), tm(27), LS[:, 1, :], A.add, ["T27", "LA1"], ["P2"])
+            ts(tm(14), tm(10), 4032.0, None, A.add, None, ["T10"], ["T14"])
+            ts(tm(13), tm(11), -4160.0, None, A.add, None, ["T11"], ["T13"])
+            ts(off(O_S[1], 0, 192), T.LB[:, 2:4, :], float(DUM), None, A.min, None, nk, [okey(O_S[1])])
+            digits(T.LB, "LB", 2, 4)
+            tt(PS[4][:, 4:8, 0:48], fld(7, 2, 2), T.Y7[:], A.is_equal, ["P7", "Y7"], ["P4"])
+            tt(tm(24, 2), PS[4][:, 4:8, 0:48], tm(12, 2), A.mult, ["P4", "T12", "T13"], ["T24"])
+            tt(tm(28), pt(4, 2), tm(14), A.mult, ["P4", "T14"], ["T28"])
+            tt(pt(5, 2), pt(3, 1), tm(24), A.add, ["P3", "T24"], ["P5"])
+            tt(tm(30), pt(2, 1), tm(28), A.add, ["P2", "T28"], ["T30"])
+            tt(T.LB[:, 1, :], pt(5, 2), tm(25), A.add, ["P5", "T24"], ["LB1"])
+            ts(T.LB[:, 0, :], tm(30), -2048.0, None, A.add, None, ["T30"], ["LB0"])
+            cp(off(O_SIB[1]), T.LB[:, 1, :], ["LB1"], [okey(O_SIB[1])])
+            each_bank(T.BB[:, 0], T.H1, keys("HI1", 6) + ["BB"], True)
+            digits(T.LB, "LB", 0, 1)
+            turn()
+            cp(off(O_PAR[1]), tm(30), ["T30"], [okey(O_PAR[1])])
+
+    for s, c in total.items():
+        if waited["g"].get(s, 0) < c:
+            g.wait_ge(T.sem[s], c)

@@ -22,7 +22,7 @@ SCRATCH = {
     "OUT": ("sbuf", [128, NI + NV], "float32"),
     "LA": ("sbuf", [128, 4, 96], "int32"), "LB": ("sbuf", [128, 4, 96], "int32"), "LC": ("sbuf", [128, 2, 96], "int32"),
     "HI": ("sbuf", [128, 4, 96], "int32"), "LO": ("sbuf", [128, 4, 96], "int32"),
-    "Y7": ("sbuf", [128, 2, 96], "int32"), "IO": ("sbuf", [128, 2, 96], "int32"),
+    "Y7": ("sbuf", [128, 96], "int32"), "IO": ("sbuf", [128, 96], "int32"),
     "TM": ("sbuf", [128, 32, 96], "float32"),
     "OF": ("sbuf", [128, 16 * 96], "uint16"),
     "LI": ("sbuf", [128, 2], "int32"), "COL": ("sbuf", [128, 5], "float32"),
@@ -55,9 +55,12 @@ def rank_program(g, core, T, topo):
     lastw, readers = {}, {}
     ndma = [0]
 
+    def bank(k):
+        return k[0] == "P" and k[1:].isdigit()
+
     def sync(q, reads, writes):
         need = {}
-        deps = [lastw[k] for k in list(reads) + list(writes) if k in lastw]
+        deps = [lastw[k] for k in list(reads) + list(writes) if k in lastw and not (bank(k) and lastw[k][0] == qsem.get(q))]
         for k in writes:
             deps += readers.get(k, [])
         for s, c in deps:
@@ -77,7 +80,7 @@ def rank_program(g, core, T, topo):
             readers[k] = []
 
     def op(q, call, reads, writes):
-        writes = list(writes) + [k for k in reads if k[0] == "P" and k[1:].isdigit()]
+        writes = list(writes) + [k for k in reads if bank(k)]
         sync(q, reads, writes)
         s = qsem[q]
         call().then_inc(T.sem[s], 1)
@@ -146,16 +149,16 @@ def rank_program(g, core, T, topo):
     def okey(slot):
         return "OF%d" % slot
 
-    def fld(bank, f, n=1):
-        return PS[bank][:, 96 * f: 96 * (f + n)]
+    def fld(b, f, n=1):
+        return PS[b][:, 96 * f: 96 * (f + n)]
 
-    def extract(bank, f, zset, src, c0, reads, first=True, last=True, part=(0, 96)):
-        a, b = part
-        mms([(PS[bank][:, 96 * f + a:96 * f + b], T.ZZ[:, zset, 15 - r:143 - r], src[:, c0 + 16 * a + r:c0 + 16 * b:16],
-              first and r == 0, last and r == 15) for r in range(16)], reads + ["ZZ%d" % zset], ["P%d" % bank])
+    def extract(b, f, zset, src, c0, reads, first=True, last=True, part=(0, 96)):
+        a, e = part
+        mms([(PS[b][:, 96 * f + a:96 * f + e], T.ZZ[:, zset, 15 - r:143 - r], src[:, c0 + 16 * a + r:c0 + 16 * e:16],
+              first and r == 0, last and r == 15) for r in range(16)], reads + ["ZZ%d" % zset], ["P%d" % b])
 
-    def from_y(bank, k, t, mode):
-        return [(PS[bank][:, :, 16 * cl:16 * cl + 16], T.UU[:, 4 * t + cl, 1 - g0:9 - g0, :],
+    def from_y(b, k, t, mode):
+        return [(PS[b][:, :, 16 * cl:16 * cl + 16], T.UU[:, 4 * t + cl, 1 - g0:9 - g0, :],
                  T.YY[:, 8 * k:8 * k + 8, 16 * g0:16 * g0 + 16],
                  (mode == "alone" and g0 == 0) or (mode == "open" and cl + g0 == 0), mode == "alone" and g0 == 1)
                 for cl in range(4) for g0 in range(2)]
@@ -174,29 +177,38 @@ def rank_program(g, core, T, topo):
     def turn():
         op("v", lambda: V.transpose(T.YY[:], T.XX[:]), XK, ["YY"])
 
+    def engines_of(src, dst, d):
+        e = topo.engines(src, dst)
+        h = len(e) // 2
+        return [e[:h], e[h:], e][d - 1]
+
     def send(src, skey, dst, sem):
         sync("g", [skey], [])
         trs = []
         for d in range(1, n_ranks):
             peer = T.cores[(rank + d) % n_ranks]
-            e = topo.engines(core, peer)
-            pick = [0, 2, 1][d - 1]
-            m = (1 << e[pick]) | (1 << e[pick + len(e) // 2])
+            e = engines_of(core, peer, d)
             rid, pid, _ = topo.addr(peer)
-            trs.append(RemoteDMATransfer(dst_ids=[DstId(rid=rid, pnc=pid)], dma_engine_mask=m, remote_sem=T.sem[sem],
-                                         src=src[:, (d - 1) * NG:d * NG], dst=dst[:, GH + (d - 1) * NG:GH + d * NG]))
-        g.remote_dma_fused(trs, local_sem=T.sem.sent)
-        total["sent"] = total.get("sent", 0) + 2 * (n_ranks - 1)
+            trs.append(RemoteDMATransfer(dst_ids=[DstId(rid=rid, pnc=pid)], dma_engine_mask=sum(1 << x for x in e),
+                                         remote_sem=T.sem[sem], src=src[:, (d - 1) * NG:d * NG],
+                                         dst=dst[:, GH + (d - 1) * NG:GH + d * NG]))
+            total["sent"] = total.get("sent", 0) + len(e)
+        g.remote_dma_fused(trs[:2], local_sem=T.sem.sent)
+        g.remote_dma_fused(trs[2:], local_sem=T.sem.sent)
 
     def tm(i, n=1):
         return T.TM[:, i, :] if n == 1 else T.TM[:, i:i + n, :]
 
-    def pt(bank, i):
-        return PS[bank][:, 2 * i:2 * i + 2, 0:48]
+    def pt(b, i):
+        return PS[b][:, 2 * i:2 * i + 2, 0:48]
 
+    def pk(b, i):
+        return ["P%d" % b, "Q%d%d" % (b, i)]
+
+    arrive = sum(len(engines_of(T.cores[(rank - d) % n_ranks], core, d)) for d in range(1, n_ranks))
     for r in range(2):
-        total["arr%d" % r] = 2 * (n_ranks - 1)
-        lastw["HG%d" % r] = ("arr%d" % r, 2 * (n_ranks - 1))
+        total["arr%d" % r] = arrive
+        lastw["HG%d" % r] = ("arr%d" % r, arrive)
 
     dma("s", T.KI[:, 0, :], T.kl[:], [], ["KI0"])
     dma("a", T.KI[:, 1, :], T.kr[:], [], ["KI1"])
@@ -206,7 +218,7 @@ def rank_program(g, core, T, topo):
     dma("s", T.VI[:], T.vel[:], [], ["VI"])
 
     op("g", lambda: g.iota(T.LI[:, 0:1], [[0, 1]], 0, 1), [], ["LI0"])
-    op("g", lambda: g.iota(T.IO[:], [[0, 2], [16, 96]], SH, 0), [], ["IO"])
+    op("g", lambda: g.iota(T.IO[:], [[16, 96]], SH, 0), [], ["IO"])
     fill(T.UU[:], 0.0, ["UU0", "UU1"])
     fill(T.W1[:, 0:DUM + 1], 0.0, ["W1"])
     pu = [[-8, 4], [-32, 4]]
@@ -215,12 +227,15 @@ def rank_program(g, core, T, topo):
     aff(T.UU[:, 0:4, 1:9:2, 0], pu, 0, -1 / 256, "UU0")
     act(T.W2[:, 0:DUM + 1], T.W1[:, 0:DUM + 1], F.Silu, ["W1"], ["W2"])
     ts(T.LI[:, 1:2], T.LI[:, 0:1], 15, None, A.bitwise_and, None, ["LI0"], ["LI1"])
-    cp(T.COL[:, 0:1], T.LI[:, 1:2], ["LI1"], ["LANE"])
     fill(T.XX[:, 2::8], 0.0, ["XX2"])
-    ts(T.Y7[:], T.IO[:], T.COL[:, 0:1], None, A.add, None, ["IO", "LANE"], ["Y7"])
+    cp(T.COL[:, 0:1], T.LI[:, 1:2], ["LI1"], ["LANE"])
     fill(T.XX[:, 3::8], 0.0, ["XX3"])
-    ts(T.HI[:, 0, :], T.Y7[:, 0, :], 6, None, A.arith_shift_right, None, ["Y7"], ["HI0"])
-    ts(T.LO[:, 0, :], T.Y7[:, 0, :], 63, None, A.bitwise_and, None, ["Y7"], ["LO0"])
+    ts(T.Y7[:], T.IO[:], T.COL[:, 0:1], None, A.add, None, ["IO", "LANE"], ["Y7"])
+    ts(T.COL[:, 1:2], T.COL[:, 0:1], 7.0, 0.25, A.is_ge, A.mult, ["LANE"], ["BA"])
+    ts(T.COL[:, 2:3], T.COL[:, 0:1], 6.0, 0.5, A.is_ge, A.mult, ["LANE"], ["BBI"])
+    ts(T.HI[:, 0, :], T.Y7[:], 6, None, A.arith_shift_right, None, ["Y7"], ["HI0"])
+    ts(T.LO[:, 0, :], T.Y7[:], 63, None, A.bitwise_and, None, ["Y7"], ["LO0"])
+    ts(T.COL[:, 4:5], T.COL[:, 0:1], 8.0, 256.0, A.is_ge, A.mult, ["LANE"], ["B8"])
     cp(T.XX[:, 0::8], T.HI[:, 0, :], ["HI0"], ["XX0"])
     cp(T.XX[:, 1::8], T.LO[:, 0, :], ["LO0"], ["XX1"])
     pz = [[-16, 8]]
@@ -233,31 +248,31 @@ def rank_program(g, core, T, topo):
     gfill(T.ZZ[:, 0:4, :], 4 * 144, 0, zk[0:4])
     affz(2, 4, -2, 8, 64)
     affz(2, 4, -2, 9, 1)
-    affz(0, 2, -2, 1, 1)
-    affz(0, 1, 0, 0, -64)
-    affz(1, 2, 0, 2, 64)
     gfill(T.H0[:, 0:SH], SH, 0, ["HZ0"])
 
     ts(T.LA[:, 2:4, :], T.KI[:], float(SH), None, A.add, None, ["KI0", "KI1"], ["LA2", "LA3"])
+    ts(off(O_H[0], 0, 192), T.KI[:], float(SH), None, A.add, None, ["KI0", "KI1"], [okey(O_H[0]), okey(O_H[0] + 1)])
     digits(T.LA, "LA", 2, 4)
+    cp(off(O_SL, 0, 48), T.SLI[:], ["SLI"], [okey(O_SL)])
     turn()
     for k in range(3):
         mms(from_y(k, k, 0, "alone"), ["YY", "UU0"], ["P%d" % k])
-    cp(off(O_SL, 0, 48), T.SLI[:], ["SLI"], [okey(O_SL)])
-    ts(off(O_H[0], 0, 192), T.KI[:], float(SH), None, A.add, None, ["KI0", "KI1"], [okey(O_H[0]), okey(O_H[0] + 1)])
     cp(T.GS0[:], T.HLI[:].indirect(off(O_SL, 0, 48)), ["HLI", okey(O_SL)], ["GS0"])
     send(T.GS0, "GS0", T.H0, "arr0")
     third = [slice(512 * k, 512 * k + 512) for k in range(3)]
     third7 = [slice(SH + 512 * k, SH + 512 * k + 512) for k in range(3)]
-    quarter = [slice(SH + 384 * b, SH + 384 * b + 384) for b in range(4)]
+    QC = [0, 32, 64, 84, 96]
+    quarter = [slice(SH + 16 * QC[b], SH + 16 * QC[b + 1]) for b in range(4)]
+    PQ = [PS[b][:, 0:(QC[b + 1] - QC[b]) // 4, :] for b in range(4)]
     for k in range(3):
         act(T.SRC[:, third[k]], PS[k][:], F.Identity, ["P%d" % k], ["SRC_%d" % k], bias=64.0, scale=256.0)
     act(T.W2[:].indirect(off(O_H[0] + 1)), T.SRC[:], F.Silu, keys("SRC", 3) + [okey(O_H[0] + 1)], ["W2"])
-    act(T.W2B[:, SH:DUM], T.W2[:, SH:DUM], F.Copy, ["W2"], ["W2B"])
-    for k in range(3):
-        cp(T.W1[:].indirect(off(O_H[0], 32 * k, 32 * k + 32)), T.SRC[:, third[k]], ["SRC_%d" % k, okey(O_H[0])], ["W1"])
-    cp(T.H0[:, SH:DUM], T.HII[:], ["HII"], keys("HI0", 6))
+    act(T.W2B[:, SH:SH + 1024], T.W2[:, SH:SH + 1024], F.Copy, ["W2"], ["W2B"])
     cp(T.H0[:, DUM:GH], T.HLI[:], ["HLI"], ["HL0"])
+    cp(T.W1[:].indirect(off(O_H[0])), T.SRC[:], keys("SRC", 3) + [okey(O_H[0])], ["W1"])
+    cp(T.W2B[:, SH + 1024:DUM], T.W2[:, SH + 1024:DUM], ["W2"], ["W2C"])
+    cp(T.H0[:, SH:DUM], T.HII[:], ["HII"], keys("HI0", 6))
+    w2b = ["W2B", "W2C"]
     for t in (1, 0):
         for k in range(3):
             mms(from_y(3 * t + k, k, t, "open"), ["YY", "UU0", "UU1"], ["P%d" % (3 * t + k)])
@@ -270,6 +285,9 @@ def rank_program(g, core, T, topo):
     gfill(T.BB[:, 1, :, 4:12], 64, -1, ["BB"])
     aff(T.BB[:, :, :, 4:12], [[0, 2], [-16, 8], [0, 8]], 0, 0, "BB", A.is_ge)
     aff(T.BB[:, :, :, 4:12], [[0, 2], [16, 8], [0, 8]], 15, 0, "BB", A.is_ge, -1)
+    affz(0, 2, -2, 1, 1)
+    affz(0, 1, 0, 0, -64)
+    affz(1, 2, 0, 2, 64)
     gfill(T.H1[:, 0:SH], SH, 0, ["HZ1"])
     gfill(T.H1[:, NI:DUM], SH, 0, ["HI1_5"])
     for W, wn in ((T.WB, "WB"), (T.VV, "VV"), (T.CW, "CW"), (T.WD, "WD")):
@@ -303,18 +321,17 @@ def rank_program(g, core, T, topo):
             for t in range(2):
                 mms([(PS[3 * t + k][:], lhs, src[:, third7[k]], start, False)], reads, ["P%d" % (3 * t + k)])
     extract(7, 0, 3, T.W1, SH, ["W1"], True, False)
-    extract(6, 0, 0, T.W1, SH, ["W1"], True, False)
     each_bank(T.AW[:, 0], T.W1, ["W1", "AW0"], False, (0,))
-    extract(7, 0, 2, T.W2B, SH, ["W2B"], False, True)
-    cp(T.VB[:], T.VI[:], ["VI"], ["VB"])
+    extract(7, 0, 2, T.W2B, SH, w2b, False, True)
     ts(off(O_SIB[0]), fld(7, 0), -4160.0, None, A.add, None, ["P7"], [okey(O_SIB[0])])
     ts(T.LA[:, 1, :], fld(7, 0), -4160.0, 0.0, A.add, A.max, ["P7"], ["LA1"])
-    ts(T.COL[:, 1:2], T.COL[:, 0:1], 7.0, 0.25, A.is_ge, A.mult, ["LANE"], ["BA"])
-    ts(T.COL[:, 2:3], T.COL[:, 0:1], 6.0, 0.5, A.is_ge, A.mult, ["LANE"], ["BBI"])
-    ts(T.COL[:, 4:5], T.COL[:, 0:1], 8.0, 256.0, A.is_ge, A.mult, ["LANE"], ["B8"])
     ts(off(O_S[0], 0, 192), T.LA[:, 2:4, :], float(DUM), None, A.min, None, ["LA2", "LA3"], [okey(O_S[0])])
     ts(T.COL[:, 3:4], T.COL[:, 2:3], -1024.0, T.COL[:, 4:5], A.mult, A.add, ["BBI", "B8"], ["BD"])
 
+    def sib_less_child(LS, ln):
+        for s in range(2):
+            tt(tm(6 + s), LS[:, 1, :], LS[:, 2 + s, :], A.subtract, [ln + "1", ln + str(2 + s)], ["T6_%d" % s])
+    sib_less_child(T.LA, "LA")
     HALVES = ((7, (0, 512)), (6, (512, NV)))
 
     def leaves_sum(H, r):
@@ -344,7 +361,7 @@ def rank_program(g, core, T, topo):
                     mms(from_y(3 * t + k, k, t, "part"), ["YY", "UU0", "UU1"], ["P%d" % (3 * t + k)])
                 return
             each_bank(T.BB[:, 0], T.H0, keys("HI0", 6) + ["BB"], False, (k,))
-            each_bank(T.AW[:, 0], T.W2B, ["W2B", "AW0"], False, (k,))
+            each_bank(T.AW[:, 0], T.W2B, w2b + ["AW0"], False, (k,))
             if k > 0:
                 each_bank(T.AW[:, 0], T.W1, ["W1", "AW0"], False, (k,))
         ids(0)
@@ -359,33 +376,37 @@ def rank_program(g, core, T, topo):
                 mms([(PS[3 * t + k][:], T.BB[:, 1], M[:, third[k]], False, True)],
                     ["%s_%d" % (mn, i) for c0, c1, i in pieces] + ["BB"], ["P%d" % (3 * t + k)])
             act(T.TB[:, third[k]], PS[k][:], F.Relu, ["P%d" % k, "BA"], ["TA_%d" % k], bias=T.COL[:, 1:2])
-            if r == 0 and k == 1:
-                extract(6, 0, 0, T.W2B, SH, ["W2B"], False, True)
+        if r == 0:
+            extract(6, 0, 0, T.W1, SH, ["W1"], True, False)
+            extract(6, 0, 0, T.W2B, SH, w2b, False, True)
         for k in range(3):
             tt(T.WB[:, third7[k]], PS[3 + k][:], T.TB[:, third[k]], A.max, ["P%d" % (3 + k), "TA_%d" % k], ["WB_%d" % k])
         wb = keys("WB", 3) + ["WBz", "WBy"]
         if r == 0:
-            ts(T.LA[:, 0, :], fld(6, 0), 4032.0, float(DUM), A.add, A.min, ["P6"], ["LA0"])
-            ts(off(opar), fld(6, 0), 4032.0, float(DUM), A.add, A.min, ["P6"], [okey(opar)])
+            cp(T.VB[:], T.VI[:], ["VI"], ["VB"])
             for b in range(4):
-                mms([(PS[b][:, 0:6, :], T.AW[:, 1], T.W1[:, quarter[b]], True, False),
-                     (PS[b][:, 0:6, :], T.AW[:, 2], T.W2B[:, quarter[b]], False, False)],
-                    ["AW1", "W1", "W2B"], ["P%d" % b])
-        leaves_sum(H, r)
-        for s in range(2):
-            tt(tm(6 + s), LS[:, 1, :], LS[:, 2 + s, :], A.subtract, [ln + "1", ln + str(2 + s)], ["T6_%d" % s])
+                mms([(PQ[b], T.AW[:, 1], T.W1[:, quarter[b]], True, False),
+                     (PQ[b], T.AW[:, 2], T.W2B[:, quarter[b]], False, False)], ["AW1", "W1"] + w2b, ["P%d" % b])
+        else:
+            ts(off(opar), T.LB[:, 0, :], 2048.0, None, A.add, None, ["LB0"], [okey(opar)])
+            sib_less_child(LS, ln)
         for i in range(6):
             act(T.TB[:, 256 * i:256 * i + 256], T.WB[:].indirect(off(os_, 16 * i, 16 * i + 16)), F.Identity,
                 wb + [okey(os_), "BBI"], ["TB_%d" % i], bias=T.COL[:, 2:3])
         for i in range(6):
             tt(T.VV[:, SH + 256 * i:SH + 256 * i + 256], T.WB[:].indirect(off(os_ + 1, 16 * i, 16 * i + 16)),
                T.TB[:, 256 * i:256 * i + 256], A.max, wb + [okey(os_), "TB_%d" % i], ["VV_%d" % i])
+            if i == 1:
+                if r == 0:
+                    ts(T.LA[:, 0, :], fld(6, 0), 4032.0, float(DUM), A.add, A.min, ["P6"], ["LA0"])
+                    ts(off(opar), fld(6, 0), 4032.0, float(DUM), A.add, A.min, ["P6"], [okey(opar)])
+                leaves_sum(H, r)
         for k in range(3):
             act(T.SRC[:, third[k]], T.VV[:, third7[k]], F.Copy, ["VV_%d" % (2 * k), "VV_%d" % (2 * k + 1)], ["VC_%d" % k])
         vk = keys("VV", 6) + ["VVz", "VVy"]
         for b in range(4):
-            mms([(PS[b][:, 0:6, :], T.FF[:], T.VV[:, quarter[b]], r == 1, False)],
-                ["VV_%d" % i for i in range(384 * b // 256, (384 * b + 383) // 256 + 1)] + ["FF"], ["P%d" % b])
+            mms([(PQ[b], T.FF[:], T.VV[:, quarter[b]], r == 1, False)],
+                ["VV_%d" % i for i in range(QC[b] // 16, (QC[b + 1] - 1) // 16 + 1)] + ["FF"], ["P%d" % b])
         leaves_cap()
         if r == 0:
             leaves_out(T.H1[:, DUM:GH], "HL1")
@@ -395,67 +416,70 @@ def rank_program(g, core, T, topo):
         for k in range(3):
             tt(T.CW[:, third7[k]], T.VV[:].indirect(off(opar, 32 * k, 32 * k + 32)), T.SRC[:, third[k]], A.is_lt,
                vk + [okey(opar), "VC_%d" % k], ["CW_%d" % k])
-            mms([(PS[k][:, 0:6, :], T.MC[:, 1], T.CW[:, quarter[k]], False, False)], keys("CW", k + 1) + ["MC1"], ["P%d" % k])
+            mms([(PQ[k], T.MC[:, 1], T.CW[:, quarter[k]], False, False)], keys("CW", k + 1) + ["MC1"], ["P%d" % k])
         cw = keys("CW", 3)
         ck = cw + ["CWz", "CWy"]
-        mms([(PS[3][:, 0:6, :], T.MC[:, 1], T.CW[:, quarter[3]], False, False)], cw + ["MC1"], ["P3"])
+        mms([(PQ[3], T.MC[:, 1], T.CW[:, quarter[3]], False, False)], cw + ["MC1"], ["P3"])
         for b in range(4):
-            c0, c1 = 24 * b, 24 * b + 24
-            o = PS[b][:, 0:6, :]
+            c0, c1 = QC[b], QC[b + 1]
             cp(T.M2[:, 16 * c0:16 * c1], T.CW[:].indirect(off(os_ + 1, c0, c1)), ck + [okey(os_)], ["CR_%d" % b])
             act(T.M1[:, 16 * c0:16 * c1], T.CW[:].indirect(off(os_, c0, c1)), F.Copy, ck + [okey(os_)], ["CL_%d" % b])
-            mms([(o, T.MC[:, 0], T.M2[:, 16 * c0:16 * c1], False, False),
-                 (o, T.MC[:, 0], T.M1[:, 16 * c0:16 * c1], False, True)], ["CR_%d" % b, "CL_%d" % b, "MC0"], ["P%d" % b])
+            mms([(PQ[b], T.MC[:, 0], T.M2[:, 16 * c0:16 * c1], False, False),
+                 (PQ[b], T.MC[:, 0], T.M1[:, 16 * c0:16 * c1], False, True)], ["CR_%d" % b, "CL_%d" % b, "MC0"], ["P%d" % b])
         for b in range(4):
             if b % 2:
-                act(T.WD[:, quarter[b]], PS[b][:, 0:6, :], F.Relu, ["P%d" % b, "BD"], ["WD_%d" % b], bias=T.COL[:, 3:4])
+                act(T.WD[:, quarter[b]], PQ[b], F.Relu, ["P%d" % b, "BD"], ["WD_%d" % b], bias=T.COL[:, 3:4])
             else:
-                ts(T.WD[:, quarter[b]], PS[b][:, 0:6, :], T.COL[:, 3:4], 0.0, A.add, A.max, ["P%d" % b, "BD"], ["WD_%d" % b])
+                ts(T.WD[:, quarter[b]], PQ[b], T.COL[:, 3:4], 0.0, A.add, A.max, ["P%d" % b, "BD"], ["WD_%d" % b])
         wd = keys("WD", 4) + ["WDz", "WDy"]
         if r == 0:
             ts(off(O_SL, 48, 96), T.SLI[:], float(SH), None, A.add, None, ["SLI"], ["OSL1"])
-        act(T.DP[:, 0:768], T.WD[:].indirect(off(opar, 0, 48)), F.Copy, wd + [okey(opar)], ["DP_0"])
-        cp(T.DP[:, 768:NI], T.WD[:].indirect(off(opar, 48, 96)), wd + [okey(opar)], ["DP_1"])
-        dp = keys("DP", 2)
+        for j in range(2):
+            c0, c1, c2 = 48 * j, 48 * j + 24, 48 * j + 48
+            act(T.DP[:, 16 * c0:16 * c1], T.WD[:].indirect(off(opar, c0, c1)), F.Copy, wd + [okey(opar)], ["DP_%d" % (2 * j)])
+            cp(T.DP[:, 16 * c1:16 * c2], T.WD[:].indirect(off(opar, c1, c2)), wd + [okey(opar)], ["DP_%d" % (2 * j + 1)])
+        dp = keys("DP", 4)
         extract(6, 0, 6, T.WD, SH, wd)
-        extract(7, 0, 4, T.DP, 0, dp)
+        for j in range(2):
+            extract(7, 0, 4, T.DP, 0, dp[2 * j:2 * j + 2], part=(48 * j, 48 * j + 48))
         if r == 0:
             act(T.GS1[:], T.H1[:, NI:GH].indirect(off(O_SL, 48, 96)), F.Copy, ["HL1", "HI1_5", "OSL1"], ["GS1"])
             send(T.GS1, "GS1", T.H1, "arr1")
-        ts(pt(4, 0), fld(6, 0), 0.0, None, A.is_le, None, ["P6"], ["P4"])
-        ts(pt(5, 0), fld(6, 0), 0.0, -1.0, A.is_ge, A.mult, ["P6"], ["P5"])
+        ts(pt(4, 0), fld(6, 0), 0.0, None, A.is_le, None, ["P6"], pk(4, 0))
+        ts(pt(5, 0), fld(6, 0), 0.0, -1.0, A.is_ge, A.mult, ["P6"], pk(5, 0))
         for s in range(2):
-            tt(tm(2 + s), pt(4 + s, 0), LS[:, 2 + s, :], A.mult, ["P%d" % (4 + s), ln + str(2 + s)], ["T2_%d" % s])
+            tt(tm(2 + s), pt(4 + s, 0), LS[:, 2 + s, :], A.mult, pk(4 + s, 0) + [ln + str(2 + s)], ["T2_%d" % s])
         for s in range(2):
             tt(tm(4 + s), fld(6, 0), tm(2 + s), [A.max, A.min][s], ["P6", "T2_%d" % s], ["T4_%d" % s])
         if r == 0:
             extract(6, 3, 0, T.DP, 0, dp)
-            tt(tm(12), T.LA[:, 0, :], LS[:, 1, :], A.subtract, ["LA0", "LA1"], ["T12"])
         ohn = O_H[r + 1]
         KN = [[T.LB[:, 2, :], T.LB[:, 3, :]], [T.LC[:, 0, :], T.LC[:, 1, :]]][r]
         nk = [["LB2", "LB3"], ["LC0", "LC1"]][r]
         for s in range(2):
-            tt(pt(s, 0), fld(7, 0), LS[:, 2 + s, :], A.is_equal, ["P7", ln + str(2 + s)], ["P%d" % s])
+            tt(pt(s, 0), fld(7, 0), LS[:, 2 + s, :], A.is_equal, ["P7", ln + str(2 + s)], pk(s, 0))
         for s in range(2):
-            tt(pt(2 + s, 0), pt(s, 0), tm(6 + s), A.mult, ["P%d" % s, "T6_%d" % s], ["P%d" % (2 + s)])
+            tt(pt(2 + s, 0), pt(s, 0), tm(6 + s), A.mult, pk(s, 0) + ["T6_%d" % s], pk(2 + s, 0))
         for s in range(2):
-            tt(KN[s], pt(2 + s, 0), tm(4 + s), [A.add, A.subtract][s], ["P%d" % (2 + s), "T4_%d" % s], [nk[s]])
+            tt(KN[s], pt(2 + s, 0), tm(4 + s), [A.add, A.subtract][s], pk(2 + s, 0) + ["T4_%d" % s], [nk[s]])
         for s in range(2):
             cp(off(ohn + s), KN[s], [nk[s]], [okey(ohn + s)])
         if r == 0:
+            cp(tm(9), pt(1, 0), pk(1, 0), ["T9"])
             ts(off(O_GP), fld(6, 3), 4032.0, float(DUM), A.add, A.min, ["P6"], [okey(O_GP)])
             ts(tm(15), fld(7, 0), 0.0, None, A.is_equal, None, ["P7"], ["T15"])
-            cp(tm(9), pt(1, 0), ["P1"], ["T9"])
             extract(6, 1, 3, T.DP, 0, dp)
             extract(6, 2, 5, T.DP, 0, dp)
             extract(6, 4, 1, T.DP, 0, dp)
-            tt(tm(16), pt(0, 0), tm(9), A.add, ["P0", "T9"], ["T16"])
+            tt(tm(16), pt(0, 0), tm(9), A.add, pk(0, 0) + ["T9"], ["T16"])
+            tt(tm(12), T.LA[:, 0, :], LS[:, 1, :], A.subtract, ["LA0", "LA1"], ["T12"])
         else:
             for t in range(6):
                 ts(T.XT[:, 32 * t:32 * t + 32], T.LC[:, :, t::6], -float(SH), None, A.add, None, nk, ["XT_%d" % t])
             op("v", lambda: V.transpose(T.YK[:], T.XT[:]), keys("XT", 6), ["YK"])
+        EC = [0, 16, 32, 48, 64, 80, 96] if r == 0 else [0, 16, 32, 48, 68, 86, 96]
         for i in range(6):
-            act(T.HS[:, 256 * i:256 * i + 256], H[:].indirect(off(ohn, 16 * i, 16 * i + 16)), F.Copy, hk + [okey(ohn)],
+            act(T.HS[:, 16 * EC[i]:16 * EC[i + 1]], H[:].indirect(off(ohn, EC[i], EC[i + 1])), F.Copy, hk + [okey(ohn)],
                 ["HE_%d" % i])
         if r == 1:
             for g0 in range(2):
@@ -463,44 +487,46 @@ def rank_program(g, core, T, topo):
             for g0 in range(2):
                 dma("a", T.yk[g0::2, :], T.YC[:, 96 * g0:96 * g0 + 96], ["YC_%d" % g0], [])
         for i in range(6):
-            o = T.H1[:, SH + 256 * i:SH + 256 * i + 256] if r == 0 else T.OUT[:, 256 * i:256 * i + 256]
-            tt(o, H[:].indirect(off(ohn + 1, 16 * i, 16 * i + 16)), T.HS[:, 256 * i:256 * i + 256], A.max,
+            c0, c1 = 16 * EC[i], 16 * EC[i + 1]
+            o = T.H1[:, SH + c0:SH + c1] if r == 0 else T.OUT[:, c0:c1]
+            tt(o, H[:].indirect(off(ohn + 1, EC[i], EC[i + 1])), T.HS[:, c0:c1], A.max,
                hk + [okey(ohn + 1), "HE_%d" % i], ["HI1_%d" % i if r == 0 else "OUT_%d" % i])
             if r == 1 and i in (1, 3, 4, 5):
                 i0 = i - 1 if i < 4 else i
-                dma("s", T.yh[:, 256 * i0:256 * i + 256], T.OUT[:, 256 * i0:256 * i + 256],
-                    ["OUT_%d" % j for j in range(i0, i + 1)], [])
+                dma("s", T.yh[:, 16 * EC[i0]:c1], T.OUT[:, 16 * EC[i0]:c1], ["OUT_%d" % j for j in range(i0, i + 1)], [])
         if r == 0:
             for j in range(2):
                 act(T.GB[:, 768 * j:768 * j + 768], T.WD[:].indirect(off(O_GP, 48 * j, 48 * j + 48)), F.Copy,
                     wd + [okey(O_GP)], ["GB_%d" % j])
                 extract(7, 2, 4, T.GB, 0, ["GB_%d" % j], part=(48 * j, 48 * j + 48))
-                extract(7, 3, 3, T.GB, 0, ["GB_%d" % j], part=(48 * j, 48 * j + 48))
             tt(tm(17), tm(15), LS[:, 1, :], A.mult, ["T15", "LA1"], ["T17"])
             tt(tm(18), fld(6, 2), tm(16), A.mult, ["P6", "T16"], ["T18"])
-            tt(pt(4, 1), tm(15), tm(16), A.add, ["T15", "T16"], ["P4"])
-            tt(pt(5, 1), fld(6, 1), tm(17), A.add, ["P6", "T17"], ["P5"])
-            tt(tm(27), pt(4, 1), tm(12), A.mult, ["P4", "T12"], ["T27"])
+            tt(pt(4, 1), tm(15), tm(16), A.add, ["T15", "T16"], pk(4, 1))
+            tt(pt(5, 1), fld(6, 1), tm(17), A.add, ["P6", "T17"], pk(5, 1))
             tt(tm(10), fld(6, 3), LS[:, 0, :], A.subtract, ["P6", "LA0"], ["T10"])
-            tt(pt(3, 1), pt(5, 1), tm(18), A.add, ["P5", "T18"], ["P3"])
+            tt(tm(27), pt(4, 1), tm(12), A.mult, pk(4, 1) + ["T12"], ["T27"])
+            tt(pt(3, 1), pt(5, 1), tm(18), A.add, pk(5, 1) + ["T18"], pk(3, 1))
             tt(tm(11), fld(6, 4), LS[:, 1, :], A.subtract, ["P6", "LA1"], ["T11"])
-            tt(pt(2, 1), tm(27), LS[:, 1, :], A.add, ["T27", "LA1"], ["P2"])
+            ts(tm(29), LS[:, 1, :], -2048.0, None, A.add, None, ["LA1"], ["T29"])
             ts(tm(14), tm(10), 4032.0, None, A.add, None, ["T10"], ["T14"])
             ts(tm(13), tm(11), -4160.0, None, A.add, None, ["T11"], ["T13"])
+            tt(pt(2, 1), tm(27), tm(29), A.add, ["T27", "T29"], pk(2, 1))
             ts(off(O_S[1], 0, 192), T.LB[:, 2:4, :], float(DUM), None, A.min, None, nk, [okey(O_S[1])])
             digits(T.LB, "LB", 2, 4)
-            tt(PS[4][:, 4:8, 0:48], fld(7, 2, 2), T.Y7[:], A.is_equal, ["P7", "Y7"], ["P4"])
-            tt(tm(24, 2), PS[4][:, 4:8, 0:48], tm(12, 2), A.mult, ["P4", "T12", "T13"], ["T24"])
-            tt(tm(28), pt(4, 2), tm(14), A.mult, ["P4", "T14"], ["T28"])
-            tt(pt(5, 2), pt(3, 1), tm(24), A.add, ["P3", "T24"], ["P5"])
-            tt(tm(30), pt(2, 1), tm(28), A.add, ["P2", "T28"], ["T30"])
-            tt(T.LB[:, 1, :], pt(5, 2), tm(25), A.add, ["P5", "T24"], ["LB1"])
-            ts(T.LB[:, 0, :], tm(30), -2048.0, None, A.add, None, ["T30"], ["LB0"])
+            tt(pt(4, 2), fld(7, 2), T.Y7[:], A.is_equal, ["P7", "Y7"], pk(4, 2))
+            tt(pt(4, 3), fld(7, 2), LS[:, 1, :], A.is_equal, ["P7", "LA1"], pk(4, 3))
+            tt(tm(28), pt(4, 2), tm(14), A.mult, pk(4, 2) + ["T14"], ["T28"])
+            tt(tm(24, 2), PS[4][:, 4:8, 0:48], tm(12, 2), A.mult, pk(4, 2) + pk(4, 3) + ["T12", "T13"], ["T24"])
+            tt(T.LB[:, 0, :], pt(2, 1), tm(28), A.add, pk(2, 1) + ["T28"], ["LB0"])
+            tt(pt(5, 2), pt(3, 1), tm(24), A.add, pk(3, 1) + ["T24"], pk(5, 2))
+            ts(T.HI[:, 0, :], T.LB[:, 0, :], 6, None, A.arith_shift_right, None, ["LB0"], ["HI0"])
+            ts(T.LO[:, 0, :], T.LB[:, 0, :], 63, None, A.bitwise_and, None, ["LB0"], ["LO0"])
+            tt(T.LB[:, 1, :], pt(5, 2), tm(25), A.add, pk(5, 2) + ["T24"], ["LB1"])
+            cp(T.XX[:, 0::8], T.HI[:, 0, :], ["HI0"], ["XX0"])
+            cp(T.XX[:, 1::8], T.LO[:, 0, :], ["LO0"], ["XX1"])
             cp(off(O_SIB[1]), T.LB[:, 1, :], ["LB1"], [okey(O_SIB[1])])
             each_bank(T.BB[:, 0], T.H1, keys("HI1", 6) + ["BB"], True)
-            digits(T.LB, "LB", 0, 1)
             turn()
-            cp(off(O_PAR[1]), tm(30), ["T30"], [okey(O_PAR[1])])
 
     for s, c in total.items():
         if waited["g"].get(s, 0) < c:

@@ -6,6 +6,8 @@ SH = 7
 DUM = NI + SH
 GH = NI + NV + SH
 WID = GH + 3 * NG
+F1 = 0
+NZ = 8
 
 SCRATCH = {
     "KI": ("sbuf", [128, 2, 96], "int32"), "SLI": ("sbuf", [128, 48], "int32"),
@@ -15,30 +17,30 @@ SCRATCH = {
     "GS0": ("sbuf", [128, 3 * NG], "bfloat16"), "GS1": ("sbuf", [128, 3 * NG], "bfloat16"),
     "W1": ("sbuf", [128, WID], "bfloat16"), "W2": ("sbuf", [128, WID], "float32"),
     "W2B": ("sbuf", [128, DUM + 1], "bfloat16"), "SRC": ("sbuf", [128, NI], "float32"),
-    "WB": ("sbuf", [128, DUM + 1], "float32"), "VV": ("sbuf", [128, DUM + 1], "float32"),
+    "WB": ("sbuf", [128, DUM + 1], "float32"), "PB": ("sbuf", [128, DUM + 1], "float32"),
     "CW": ("sbuf", [128, DUM + 1], "bfloat16"), "WD": ("sbuf", [128, DUM + 1], "bfloat16"),
     "HS": ("sbuf", [128, NI], "bfloat16"), "M1": ("sbuf", [128, NI], "bfloat16"), "M2": ("sbuf", [128, NI], "bfloat16"),
     "TB": ("sbuf", [128, NI], "float32"), "GB": ("sbuf", [128, NI], "bfloat16"), "DP": ("sbuf", [128, NI], "bfloat16"),
     "OUT": ("sbuf", [128, NI + NV], "float32"),
-    "LA": ("sbuf", [128, 4, 96], "int32"), "LB": ("sbuf", [128, 4, 96], "int32"), "LC": ("sbuf", [128, 2, 96], "int32"),
-    "HI": ("sbuf", [128, 4, 96], "int32"), "LO": ("sbuf", [128, 4, 96], "int32"),
-    "Y7": ("sbuf", [128, 96], "int32"), "IO": ("sbuf", [128, 96], "int32"),
-    "TM": ("sbuf", [128, 32, 96], "float32"),
-    "OF": ("sbuf", [128, 16 * 96], "uint16"),
-    "LI": ("sbuf", [128, 2], "int32"), "COL": ("sbuf", [128, 5], "float32"),
-    "XX": ("sbuf", [128, 768], "bfloat16"), "YY": ("sbuf", [128, 24, 32], "bfloat16"),
+    "N0": ("sbuf", [128, 96, 3], "float32"), "LC": ("sbuf", [128, 2, 96], "int32"),
+    "TI": ("sbuf", [128, 8, 96], "int32"), "TM": ("sbuf", [128, 16, 96], "float32"),
+    "OF": ("sbuf", [128, 15 * 96], "uint16"),
+    "TC": ("sbuf", [128, 3, 2, 16], "float32"), "COL": ("sbuf", [128, 3, 32], "float32"),
+    "TZ": ("sbuf", [128, NZ + 1, 4, 4, 2], "bfloat16"), "TY": ("sbuf", [128, NZ + 1, 32], "bfloat16"),
+    "YS": ("sbuf", [128, NV], "float32"),
+    "XX": ("sbuf", [128, 96, 8], "bfloat16"), "YY": ("sbuf", [128, 24, 32], "bfloat16"),
     "XT": ("sbuf", [128, 192], "float32"), "YK": ("sbuf", [128, 6, 32], "float32"), "YC": ("sbuf", [128, 192], "float32"),
-    "UU": ("sbuf", [128, 8, 10, 16], "bfloat16"), "BB": ("sbuf", [128, 2, 8, 16], "bfloat16"),
-    "FF": ("sbuf", [128, 8, 8, 2], "float32"), "MC": ("sbuf", [128, 2, 8, 16], "bfloat16"),
-    "AW": ("sbuf", [128, 3, 8, 16], "bfloat16"),
-    "ID": ("sbuf", [128, 128], "bfloat16"), "ZZ": ("sbuf", [128, 7, 144], "bfloat16"),
+    "UU": ("sbuf", [128, 12, 10, 16], "bfloat16"),
+    "CB": ("sbuf", [128, 6, 16, 4, 2], "bfloat16"), "FF": ("sbuf", [128, 16, 4, 2], "float32"),
+    "CODE": ("sbuf", [128, 8, 8], "float32"),
+    "ID": ("sbuf", [128, 128], "bfloat16"), "IF": ("sbuf", [128, 128], "float32"), "ZZ": ("sbuf", [128, NZ, 144], "bfloat16"),
 }
 for _k in range(6):
     SCRATCH["P%d" % _k] = ("psum", [128, 8, 64], "float32")
-SCRATCH["P6"] = ("psum", [128, 512], "float32")
-SCRATCH["P7"] = ("psum", [128, 512], "float32")
+SCRATCH["P6"] = ("psum", [128, 128, 4], "float32")
+SCRATCH["P7"] = ("psum", [128, 128, 4], "float32")
 
-SEMAPHORES = ["sv", "sa", "st", "sg", "arr0", "arr1", "sent"] + ["d%d" % _k for _k in range(16)]
+SEMAPHORES = ["sv", "sa", "st", "sg", "arr0", "arr1", "sent"] + ["d%d" % _k for _k in range(28)]
 
 
 def rank_program(g, core, T, topo):
@@ -87,11 +89,11 @@ def rank_program(g, core, T, topo):
         total[s] = total.get(s, 0) + 1
         done((s, total[s]), reads, writes)
 
-    def dma(q, out, in_, reads, writes):
+    def dma(q, out, in_, reads, writes, add=False):
         sync(q, reads, writes)
         s = "d%d" % ndma[0]
         ndma[0] += 1
-        eng[q].dma_start(out, in_).then_inc(T.sem[s], 16)
+        eng[q].dma_start(out, in_, **({"accum_op": A.add} if add else {})).then_inc(T.sem[s], 16)
         total[s] = 16
         done((s, 16), reads, writes)
 
@@ -112,6 +114,9 @@ def rank_program(g, core, T, topo):
     def fill(ap, val, writes):
         op("v", lambda: V.memset(ap, val), [], writes)
 
+    def turn(out, in_, reads, writes):
+        op("v", lambda: V.transpose(out, in_), reads, writes)
+
     def act(out, in_, func, reads, writes, bias=None, scale=None):
         kw = {}
         if bias is not None:
@@ -128,20 +133,33 @@ def rank_program(g, core, T, topo):
             return ins
         op("t", run, reads, writes)
 
-    def aff(ap, pattern, base, val, key, cmp=None, mult=1):
-        ks = key if isinstance(key, list) else [key]
-        op("g", lambda: g.affine_select(ap, ap, pattern, cmp or A.not_equal, float(val), base, mult), ks, ks)
+    parts = {}
 
-    def gfill(ap, n, val, writes):
-        op("g", lambda: g.iota(ap, [[0, n]], val, 0, allow_small_or_imprecise_dtypes=True), [], writes)
+    def aff(ap, pattern, base, val, key, cells):
+        mine = parts.setdefault(key, [])
+        ks = ["%s.%s" % (key, c) for c in cells]
+        op("g", lambda: g.affine_select(ap, ap, pattern, A.not_equal, float(val), base, 1), [key] + ks, ks)
+        mine += [k for k in ks if k not in mine]
+
+    def gfill(ap, n, val, key):
+        mine = parts.setdefault(key, [])
+        k = "%s.%d" % (key, len(mine))
+        op("g", lambda: g.iota(ap, [[0, n]], val, 0, allow_small_or_imprecise_dtypes=True), [key], [k])
+        mine.append(k)
+
+    def const(key):
+        return [key] + parts.get(key, [])
+
+    def in_group(out, in_, lead, tail, reads, key):
+        op("g", lambda: g.affine_select(out, in_, lead + [[-16, 8]] + tail, A.is_ge, 0.0, 0, 1), reads, [key])
+        op("g", lambda: g.affine_select(out, out, lead + [[16, 8]] + tail, A.is_ge, 0.0, 15, -1), [key], [key])
 
     def keys(name, n):
         return ["%s_%d" % (name, i) for i in range(n)]
 
     PS = [T["P%d" % k] for k in range(8)]
     O_H = [0, 2, 4]
-    O_S = [6, 8]
-    O_SIB, O_PAR, O_GP, O_SL = [10, 11], [12, 13], 14, 15
+    O_SIB, O_SIC, O_PAR, O_IC, O_SL = [6, 7], [8, 9], [10, 11], [12, 13], 14
 
     def off(slot, c0=0, c1=96):
         return T.OF[:, slot * 96 + c0: slot * 96 + c1]
@@ -149,41 +167,34 @@ def rank_program(g, core, T, topo):
     def okey(slot):
         return "OF%d" % slot
 
-    def fld(b, f, n=1):
-        return PS[b][:, 96 * f: 96 * (f + n)]
+    def fld(b, f, a=0, e=96):
+        if b >= 6:
+            return PS[b][:, 24 * f + a // 4:24 * f + e // 4, :]
+        return PS[b][:, 2 * f + a // 48:2 * f + e // 48, 0:48]
+
+    Z_W1, Z_W2, Z_GP, Z_OWN, Z_KID, Z_Z, Z_ISW, Z_T = range(NZ)
 
     def extract(b, f, zset, src, c0, reads, first=True, last=True, part=(0, 96)):
         a, e = part
-        mms([(PS[b][:, 96 * f + a:96 * f + e], T.ZZ[:, zset, 15 - r:143 - r], src[:, c0 + 16 * a + r:c0 + 16 * e:16],
-              first and r == 0, last and r == 15) for r in range(16)], reads + ["ZZ%d" % zset], ["P%d" % b])
+        mms([(fld(b, f, a, e), T.ZZ[:, zset, 15 - r:143 - r], src[:, c0 + 16 * a + r:c0 + 16 * e:16],
+              first and r == 0, last and r == 15) for r in range(16)], reads + ["ZZ%d" % (zset >= Z_GP)], ["P%d" % b])
 
-    def from_y(b, k, t, mode):
-        return [(PS[b][:, :, 16 * cl:16 * cl + 16], T.UU[:, 4 * t + cl, 1 - g0:9 - g0, :],
+    def plus(b, f, lists, reads, first=False, last=True):
+        mms([(fld(b, f), T.IF[:], x, first and i == 0, last and i == len(lists) - 1) for i, x in enumerate(lists)],
+            reads + const("IF"), ["P%d" % b])
+
+    def from_y(b, k, U, t, mode):
+        return [(PS[b][:, :, 16 * cl:16 * cl + 16], U[:, 4 * t + cl, 1 - g0:9 - g0, :],
                  T.YY[:, 8 * k:8 * k + 8, 16 * g0:16 * g0 + 16],
                  (mode == "alone" and g0 == 0) or (mode == "open" and cl + g0 == 0), mode == "alone" and g0 == 1)
                 for cl in range(4) for g0 in range(2)]
-
-    def digits(LS, lname, l0, l1):
-        rk = ["%s%d" % (lname, l) for l in range(l0, l1)]
-        ts(T.HI[:, l0:l1, :], LS[:, l0:l1, :], 6, None, A.arith_shift_right, None, rk, ["HI%d" % l0])
-        ts(T.LO[:, l0:l1, :], LS[:, l0:l1, :], 63, None, A.bitwise_and, None, rk, ["LO%d" % l0])
-        for l in range(l0, l1):
-            cp(T.XX[:, 2 * l::8], T.HI[:, l, :], ["HI%d" % l0], ["XX%d" % (2 * l)])
-        for l in range(l0, l1):
-            cp(T.XX[:, 2 * l + 1::8], T.LO[:, l, :], ["LO%d" % l0], ["XX%d" % (2 * l + 1)])
-
-    XK = ["XX%d" % f for f in range(8)]
-
-    def turn():
-        op("v", lambda: V.transpose(T.YY[:], T.XX[:]), XK, ["YY"])
 
     def engines_of(src, dst, d):
         e = topo.engines(src, dst)
         h = len(e) // 2
         return [e[:h], e[h:], e][d - 1]
 
-    def send(src, skey, dst, sem):
-        sync("g", [skey], [])
+    def send(src, skeys, dst, sem):
         trs = []
         for d in range(1, n_ranks):
             peer = T.cores[(rank + d) % n_ranks]
@@ -193,17 +204,15 @@ def rank_program(g, core, T, topo):
                                          remote_sem=T.sem[sem], src=src[:, (d - 1) * NG:d * NG],
                                          dst=dst[:, GH + (d - 1) * NG:GH + d * NG]))
             total["sent"] = total.get("sent", 0) + len(e)
-        g.remote_dma_fused(trs[:2], local_sem=T.sem.sent)
-        g.remote_dma_fused(trs[2:], local_sem=T.sem.sent)
+        for key, some in zip(skeys, (trs[:2], trs[2:])):
+            sync("g", [key], [])
+            g.remote_dma_fused(some, local_sem=T.sem.sent)
 
-    def tm(i, n=1):
-        return T.TM[:, i, :] if n == 1 else T.TM[:, i:i + n, :]
+    def tm(i):
+        return T.TM[:, i, :]
 
-    def pt(b, i):
-        return PS[b][:, 2 * i:2 * i + 2, 0:48]
-
-    def pk(b, i):
-        return ["P%d" % b, "Q%d%d" % (b, i)]
+    def ti(i):
+        return T.TI[:, i, :]
 
     arrive = sum(len(engines_of(T.cores[(rank - d) % n_ranks], core, d)) for d in range(1, n_ranks))
     for r in range(2):
@@ -217,316 +226,514 @@ def rank_program(g, core, T, topo):
     dma("s", T.HII[:], T.h0[:, 0:NI], [], ["HII"])
     dma("s", T.VI[:], T.vel[:], [], ["VI"])
 
-    op("g", lambda: g.iota(T.LI[:, 0:1], [[0, 1]], 0, 1), [], ["LI0"])
-    op("g", lambda: g.iota(T.IO[:], [[16, 96]], SH, 0), [], ["IO"])
-    fill(T.UU[:], 0.0, ["UU0", "UU1"])
-    fill(T.W1[:, 0:DUM + 1], 0.0, ["W1"])
+    LANE, BA, BW, BD = T.COL[:, 0, 0:1], T.COL[:, 1, 0:1], T.COL[:, 2, 0:1], T.TY[:, NZ, 0:1]
+    WB, PB, CW, WD = T.WB, T.PB, T.CW, T.WD
+    AW, BB, MC = T.CB, [T.CB[:, 2], T.CB[:, 3]], [T.CB[:, 4], T.CB[:, 5]]
+    fill(T.W1[:, 0:16], 0.0, ["W1a"])
+    act(T.W2[:, 0:16], T.W1[:, 0:16], F.Silu, ["W1a"], ["W2a"])
+    fill(T.UU[:], 0.0, ["US", "UU"])
+    fill(T.W1[:, 16:DUM + 1], 0.0, ["W1"])
+    act(T.W2[:, 16:DUM + 1], T.W1[:, 16:DUM + 1], F.Copy, ["W1", "W2a"], ["W2"])
+    act(T.ZZ[:, 0:4], T.W1[:, 16:16 + 4 * 144], F.Copy, ["W1"], ["ZZ0"])
+    op("g", lambda: g.iota(T.TC[:, 0], [[0, 2], [1, 16]], 0, 0, allow_small_or_imprecise_dtypes=True), [], ["TC0"])
+    op("g", lambda: g.iota(tm(0), [[16, 96]], SH + 8192, 0, allow_small_or_imprecise_dtypes=True), [], ["T0"])
+    op("g", lambda: g.iota(T.CODE[:], [[-16, 8], [0, 8]], 0, 1, allow_small_or_imprecise_dtypes=True), [], ["CODE"])
     pu = [[-8, 4], [-32, 4]]
-    aff(T.UU[:, 0:4, 1:9:2, 8:12], pu + [[-1, 4]], -4, 1 / 256, "UU0")
-    aff(T.UU[:, 0:4, 1:9:2, 1], pu, -1, 1 / 256, "UU0")
-    aff(T.UU[:, 0:4, 1:9:2, 0], pu, 0, -1 / 256, "UU0")
-    act(T.W2[:, 0:DUM + 1], T.W1[:, 0:DUM + 1], F.Silu, ["W1"], ["W2"])
-    ts(T.LI[:, 1:2], T.LI[:, 0:1], 15, None, A.bitwise_and, None, ["LI0"], ["LI1"])
-    fill(T.XX[:, 2::8], 0.0, ["XX2"])
-    cp(T.COL[:, 0:1], T.LI[:, 1:2], ["LI1"], ["LANE"])
-    fill(T.XX[:, 3::8], 0.0, ["XX3"])
-    ts(T.Y7[:], T.IO[:], T.COL[:, 0:1], None, A.add, None, ["IO", "LANE"], ["Y7"])
-    ts(T.COL[:, 1:2], T.COL[:, 0:1], 7.0, 0.25, A.is_ge, A.mult, ["LANE"], ["BA"])
-    ts(T.COL[:, 2:3], T.COL[:, 0:1], 6.0, 0.5, A.is_ge, A.mult, ["LANE"], ["BBI"])
-    ts(T.HI[:, 0, :], T.Y7[:], 6, None, A.arith_shift_right, None, ["Y7"], ["HI0"])
-    ts(T.LO[:, 0, :], T.Y7[:], 63, None, A.bitwise_and, None, ["Y7"], ["LO0"])
-    ts(T.COL[:, 4:5], T.COL[:, 0:1], 8.0, 256.0, A.is_ge, A.mult, ["LANE"], ["B8"])
-    cp(T.XX[:, 0::8], T.HI[:, 0, :], ["HI0"], ["XX0"])
-    cp(T.XX[:, 1::8], T.LO[:, 0, :], ["LO0"], ["XX1"])
-    pz = [[-16, 8]]
-    zk = ["ZZ%d" % s for s in range(7)]
+    aff(T.UU[:, 8:12, 1:9:2, 0:3], pu + [[-1, 3]], 0, 1 / 64, "US", "h")
+    aff(T.UU[:, 8:12, 1:9:2, 3:6], pu + [[-1, 3]], -3, 1, "US", "l")
+    aff(T.UU[:, 8:12, 1:9:2, 0:3], pu + [[0, 3]], -7, -248, "US", "h")
+    turn(T.COL[:, 0], T.TC[:, 0], ["TC0"], ["LANE"])
+    fill(T.XX[:, :, 6], 0.0, ["XX6"])
+    ts(T.N0[:, :, 0], tm(0), LANE, None, A.add, None, ["T0", "LANE"], ["N00"])
+    fill(T.XX[:, :, 7], 1.0, ["XX7"])
+    cp(T.XX[:, :, 0], T.N0[:, :, 0], ["N00"], ["XX0"])
 
-    def affz(s0, s1, step, lane, val):
-        aff(T.ZZ[:, s0:s1, 15:128:16], [[step, s1 - s0]] + pz, -lane, val, zk[s0:s1])
-    aff(T.UU[:, 4:8, 1:9:2, 10:12], pu + [[-1, 2]], -4, 1 / 256, "UU1")
-    aff(T.UU[:, 4:8, 1:9:2, 8:10], pu + [[-1, 2]], -6, 1 / 256, "UU1")
-    gfill(T.ZZ[:, 0:4, :], 4 * 144, 0, zk[0:4])
-    affz(2, 4, -2, 8, 64)
-    affz(2, 4, -2, 9, 1)
-    gfill(T.H0[:, 0:SH], SH, 0, ["HZ0"])
-
-    ts(T.LA[:, 2:4, :], T.KI[:], float(SH), None, A.add, None, ["KI0", "KI1"], ["LA2", "LA3"])
-    ts(off(O_H[0], 0, 192), T.KI[:], float(SH), None, A.add, None, ["KI0", "KI1"], [okey(O_H[0]), okey(O_H[0] + 1)])
-    digits(T.LA, "LA", 2, 4)
-    cp(off(O_SL, 0, 48), T.SLI[:], ["SLI"], [okey(O_SL)])
-    turn()
+    for s in range(2):
+        ts(T.N0[:, :, 1 + s], T.KI[:, s, :], SH + 8192.0, None, A.add, None, ["KI%d" % s], ["N0%d" % (1 + s)])
+    nk0 = ["N01", "N02"]
+    tt(T.XX[:, :, 3], T.N0[:, :, 0], T.XX[:, :, 0], A.subtract, ["N00", "XX0"], ["XX3"])
+    cp(T.XX[:, :, 1:3], T.N0[:, :, 1:3], nk0, ["XXh"])
+    tt(T.XX[:, :, 4:6], T.N0[:, :, 1:3], T.XX[:, :, 1:3], A.subtract, nk0 + ["XXh"], ["XXl"])
+    XK = ["XXh", "XXl", "XX6", "XX7", "XX0", "XX3"]
+    turn(T.YY[:], T.XX[:], XK, ["YY"])
     for k in range(3):
-        mms(from_y(k, k, 0, "alone"), ["YY", "UU0"], ["P%d" % k])
-    cp(T.GS0[:], T.HLI[:].indirect(off(O_SL, 0, 48)), ["HLI", okey(O_SL)], ["GS0"])
-    send(T.GS0, "GS0", T.H0, "arr0")
+        mms(from_y(k, k, T.UU, 2, "alone"), ["YY"] + const("US"), ["P%d" % k])
+    cp(off(O_SL, 0, 48), T.SLI[:], ["SLI"], [okey(O_SL)])
+    ts(off(O_H[0], 0, 192), T.KI[:], float(SH), None, A.add, None, ["KI0", "KI1"], [okey(O_H[0]), okey(O_H[0] + 1)])
+    fill(T.CB[:], 0.0, ["AW", "BB", "MC", "SM"])
+    BLOCKS = ((0, 32), (32, 48))
+    for j, (c0, c1) in enumerate(BLOCKS):
+        cp(T.GS0[:, 16 * c0:16 * c1], T.HLI[:].indirect(off(O_SL, c0, c1)), ["HLI", okey(O_SL)], ["GS0_%d" % j])
+    for s in range(2):
+        ts(T.CB[:, 2 + s, 0::2], T.CODE[:], LANE, 1.0 - 2 * s, A.is_equal, A.mult, ["CODE", "LANE", "BB"], ["BB%d" % s])
+    for s in range(2):
+        ts(T.CB[:, 2 + s, 1::2, 0, 0], T.CODE[:, :, 0], LANE, 1.0 - 2 * s, A.is_equal, A.mult, ["CODE", "LANE", "BB%d" % s], ["BB%d" % s])
     third = [slice(512 * k, 512 * k + 512) for k in range(3)]
     third7 = [slice(SH + 512 * k, SH + 512 * k + 512) for k in range(3)]
+    pz = [[-16, 8]]
+
+    def affu(U, key, lane, f, step, val):
+        aff(U[:, 0:8, 1:9:2, lane], [[step, 2]] + pu, -f, val, key, [lane])
+    for lane, f, step, val in ((4, 1, -1, 2.0 ** -16), (5, 4, -1, 2.0 ** -10), (4, 4, -1, 2.0 ** -10), (6, 2, 1, 2.0 ** -16),
+                               (7, 5, 1, 2.0 ** -10), (0, 7, 0, -21 / 16), (4, 7, 0, 134 / 1024), (5, 7, 0, 0.25),
+                               (6, 7, 0, -0.125), (7, 7, 0, 33 / 1024)):
+        affu(T.UU, "UU", lane, f, step, val)
+    gfill(T.H0[:, 0:SH], SH, 255, "HZ0")
+    send(T.GS0, keys("GS0", 2), T.H0, "arr0")
     QC = [0, 32, 64, 84, 96]
     quarter = [slice(SH + 16 * QC[b], SH + 16 * QC[b + 1]) for b in range(4)]
     PQ = [PS[b][:, 0:(QC[b + 1] - QC[b]) // 4, :] for b in range(4)]
     for k in range(3):
-        act(T.SRC[:, third[k]], PS[k][:], F.Identity, ["P%d" % k], ["SRC_%d" % k], bias=64.0, scale=256.0)
+        act(T.SRC[:, third[k]], PS[k][:], F.Identity, ["P%d" % k], ["SRC_%d" % k], bias=128.0)
     act(T.W2[:].indirect(off(O_H[0] + 1)), T.SRC[:], F.Silu, keys("SRC", 3) + [okey(O_H[0] + 1)], ["W2"])
-    act(T.W2B[:, SH:SH + 1024], T.W2[:, SH:SH + 1024], F.Copy, ["W2"], ["W2B"])
+    for j in range(2):
+        c = slice(SH + 768 * j, SH + 768 * j + 768)
+        act(T.W2B[:, c], T.W2[:, c], F.Copy, ["W2"], ["W2B_%d" % j])
+    for c0, c1 in ((0, 64), (64, 96)):
+        cp(T.W1[:].indirect(off(O_H[0], c0, c1)), T.SRC[:, 16 * c0:16 * c1], keys("SRC", c1 // 32) + [okey(O_H[0])], ["W1", "W1a"])
     cp(T.H0[:, DUM:GH], T.HLI[:], ["HLI"], ["HL0"])
-    cp(T.W1[:].indirect(off(O_H[0])), T.SRC[:], keys("SRC", 3) + [okey(O_H[0])], ["W1"])
-    cp(T.W2B[:, SH + 1024:DUM], T.W2[:, SH + 1024:DUM], ["W2"], ["W2C"])
     cp(T.H0[:, SH:DUM], T.HII[:], ["HII"], keys("HI0", 6))
-    w2b = ["W2B", "W2C"]
+    w2b = keys("W2B", 2)
+
+    def gcopy(out, in_, n, reads, writes):
+        op("g", lambda: g.affine_select(out, in_, [[0, n]], A.is_ge, 0.0, 0, 0), reads, writes)
+
     for t in (1, 0):
         for k in range(3):
-            mms(from_y(3 * t + k, k, t, "open"), ["YY", "UU0", "UU1"], ["P%d" % (3 * t + k)])
-    gfill(T.AW[:], 384, 0, ["AW0", "AW1"])
-    aff(T.AW[:, 0, :, 4], pz, 0, -1 / 32, "AW0")
-    aff(T.AW[:, 0, :, 4], pz, -1, 1 / 2048, "AW0")
-    aff(T.AW[:, 0, :, 4], pz, -5, 31 / 2048, "AW0")
-    gfill(T.BB[:], 256, 0, ["BB"])
-    gfill(T.BB[:, 0, :, 4:12], 64, 1, ["BB"])
-    gfill(T.BB[:, 1, :, 4:12], 64, -1, ["BB"])
-    aff(T.BB[:, :, :, 4:12], [[0, 2], [-16, 8], [0, 8]], 0, 0, "BB", A.is_ge)
-    aff(T.BB[:, :, :, 4:12], [[0, 2], [16, 8], [0, 8]], 15, 0, "BB", A.is_ge, -1)
-    affz(0, 2, -2, 1, 1)
-    affz(0, 1, 0, 0, -64)
-    affz(1, 2, 0, 2, 64)
-    gfill(T.H1[:, 0:SH], SH, 0, ["HZ1"])
-    gfill(T.H1[:, NI:DUM], SH, 0, ["HI1_5"])
-    for W, wn in ((T.WB, "WB"), (T.VV, "VV"), (T.CW, "CW"), (T.WD, "WD")):
-        gfill(W[:, 0:SH], SH, 0, [wn + "z"])
-        gfill(W[:, DUM:DUM + 1], 1, 0, [wn + "y"])
-    aff(T.AW[:, 1:3, :, 0:2], [[0, 2]] + pz + [[-1, 2]], 0, 1, "AW1")
-    aff(T.AW[:, 1:3, :, 2:4], [[2, 2]] + pz + [[-1, 2]], -10, 1, "AW1")
-    gfill(T.ID[:], 128, 0, ["ID"])
-    aff(T.ID[:], [[-1, 128]], 0, 1, "ID")
-    gfill(T.FF[:], 128, 0, ["FF"])
-    aff(T.FF[:, :, 3:6, :], pz + [[0, 6]], -7, -256, "FF")
-    aff(T.FF[:, :, 4:6, :], pz + [[-1, 4]], -8, 256, "FF")
-    aff(T.FF[:, :, 3, :], pz + [[-1, 2]], -8, 256, "FF")
-    aff(T.FF[:, :, 3:5, :], pz + [[1, 2], [0, 2]], -6, 512, "FF")
-    aff(T.FF[:, :, 3:5, :], pz + [[-1, 2], [0, 2]], -5, -512, "FF")
-    gfill(T.MC[:], 256, 0, ["MC0", "MC1"])
-    aff(T.MC[:, 0, :, 6:12], pz + [[0, 6]], -4, -256, "MC0")
-    aff(T.MC[:, 1, :, 6:12], pz + [[0, 6]], -4, 256, "MC1")
-    gfill(T.ZZ[:, 4:7, :], 3 * 144, 0, zk[4:7])
-    affz(4, 7, 0, 8, 64)
-    affz(4, 7, 0, 9, 1)
-    affz(4, 6, 0, 6, 64)
-    affz(4, 6, 0, 7, 1)
-    affz(5, 7, 4, 10, -64)
-    affz(5, 7, 4, 11, -1)
-    for f, w in ((0, 1 / 32), (1, 1 / 2048)):
-        aff(T.UU[:, :, 1:9:2, 4], [[0, 2]] + pu, -f, w, ["UU0", "UU1"])
+            mms(from_y(3 * t + k, k, T.UU, t, "open"), ["YY"] + const("UU"), ["P%d" % (3 * t + k)])
+    both = [[0, 2]] + pz
+    zs = [(T.ZZ[:, z0:z1, 15:128:16], [[step, z1 - z0]] + pz, -lane, val, "ZZ0", "z")
+          for z0, z1, step, lane, val in ((0, 2, 1, 2, 2.0 ** 18), (0, 2, 1, 5, 4096), (0, 2, 0, 0, 64), (0, 2, 0, 3, 1), (0, 1, 0, 7, 16))]
+    ZOFF = 640.0 * 4097
+    ws = [(AW[:, 0:2, 0::2, 0, 0], both, 0, 1 / 32, "AW", "k"), (AW[:, 0, 0::2, 1:4, :], pz + [[0, 6]], -6, 1 / 256, "AW", "d"),
+          (AW[:, 0:2, 0::2, 0, 0], both, -3, 1 / 2048, "AW", "k"), (AW[:, 0:2, 0::2, 2, 0], [[1, 2]] + pz, -2, -1 / 1024, "AW", "d"),
+          (AW[:, 0, 1::2, 1, 0], pz, -6, 1, "AW", "s"), (AW[:, 0:2, 0::2, 2, :], [[1, 2]] + pz + [[0, 2]], -5, -1 / 1024, "AW", "d"),
+          (AW[:, 0:2, 1::2, 2, :], both + [[-3, 2]], 0, 1, "AW", "p"), (AW[:, 0, 1::2, 0, 0], pz, -6, 1 / 256, "AW", "o")]
+    gfill(T.TC[:, 1:3], 64, 0, "TCz")
+    lastw["TC"] = lastw["TCz.0"]
+    for z, w in zip(zs, ws):
+        aff(*z)
+        aff(*w)
+    for w in ws[len(zs):]:
+        aff(*w)
+    zz0 = const("ZZ0")
+    for l0, l1, val in ((3, 9, 0.25), (7, 8, 0.25 + 1 / 2048)):
+        op("g", lambda: g.affine_select(T.TC[:, 1, :, l0:l1], T.TC[:, 1, :, l0:l1], [[0, 2 * (l1 - l0)]], A.is_gt, val, 0, 0),
+           ["TC"], ["TC"])
+    for l0, l1, val in ((8, 10, 4096), (10, 11, 256)):
+        gfill(T.TC[:, 2, :, l0:l1], 2 * (l1 - l0), val, "TC")
+    gfill(T.ID[:], 128, 0, "IDz")
+    gfill(T.FF[:], 128, 0, "FFz")
+    lastw["FF"], lastw["ID"] = lastw["FFz.0"], lastw["IDz.0"]
+    aff(T.ID[:], [[-1, 128]], 0, 1, "ID", "i")
 
-    def each_bank(lhs, src, reads, start, ks=(0, 1, 2)):
+    def no_node(Ws, key):
+        for W in Ws:
+            gfill(W[:, 0:SH], SH, 0, key)
+            gfill(W[:, DUM:DUM + 1], 1, 0, key)
+    no_node((WB, PB), "WPz")
+    evens, one, two = slice(0, 3, 2), slice(1, 2), slice(2, 3)
+    for s, k, lane, val in ((None, slice(0, 3), 3, -1024), (0, evens, 1, -512), (1, evens, 1, 512), (0, one, 2, -1024), (1, one, 2, 1024),
+                            (0, evens, 2, 512), (1, evens, 2, -512), (1, one, 3, -3072), (None, one, 8, 1024), (0, two, 10, -2),
+                            (None, one, 9, -1024), (1, two, 10, 2)):
+        ss, kk = ([0, 1] if s is None else [s]), range(4)[k]
+        aff(T.FF[:, ss[0]::3 - len(ss), k, :], pz + [[0, 2 * len(ss) * len(kk)]], -lane, val, "FF", [(a, b) for a in ss for b in kk])
+    aff(T.FF[:, 0::2, 3, 0], pz, -1, 64, "FF", [(0, 3)])
+    aff(T.FF[:, :, 2, :], pz + [[0, 2], [-1, 2]], -6, 1024, "FF", [(0, 2), (1, 2)])
+    aff(T.FF[:, 0::2, 3, 0], pz, -2, -64, "FF", [(0, 3)])
+    aff(T.FF[:, :, 0:2, 0], pz + [[0, 4]], -4, 1024, "FF", [(a, b) for a in range(2) for b in range(2)])
+    aff(T.FF[:, 0::2, 3, :], pz + [[-1, 2]], -12, 1, "FF", [(0, 3)])
+    aff(T.FF[:, :, 0:2, 1], pz + [[0, 4]], -5, 1024, "FF", [(a, b) for a in range(2) for b in range(2)])
+
+    def verdict_weights():
+        no_node((CW, WD), "CDz")
+        for m in range(2):
+            aff(T.CB[:, 4 + m, :, 0:3, :], pz + [[0, 12]], 0, 1024 * m - 512, "MC", [m])
+        gcopy(T.IF[:], T.ID[:], 128, const("ID"), ["IF"])
+
+    def list_weights():
+        for z, s, k0, k1, d, base, step in (
+                (Z_OWN, 0, 1, 2, 0, -64 * 4096, 0), (Z_OWN, 0, 1, 2, 1, 63 * 4096, 0), (Z_OWN, 1, 1, 2, None, -64, 127),
+                (Z_KID, 0, 0, 1, None, 64, -127), (Z_KID, 1, 0, 1, 0, 64 * 4096, 0), (Z_KID, 1, 0, 1, 1, -63 * 4096, 0),
+                (Z_Z, None, 1, 3, 0, 64 * 4096, 0), (Z_Z, None, 1, 2, 1, -63 * 4096, 0), (Z_Z, None, 2, 3, 1, 4096, 0),
+                (Z_ISW, None, 2, 3, 1, -7 * 2 ** 21, 0), (Z_T, None, 1, 2, 1, 1, -2), (Z_GP, 0, 3, 4, None, 64, -63),
+                (NZ, None, 0, 2, None, -768, 256), (NZ, None, 2, 3, None, -256, -1024), (NZ, 0, 3, 4, 0, 32, 0)):
+            n = (k1 - k0) * (2 if d is None else 1)
+            ap = T.TZ[:, z, slice(0, 4) if s is None else slice(s, 4, 2), k0:k1, slice(0, 2) if d is None else d]
+            pattern = [[0, 2], [step, 2], [0, n]] if s is None else [[0, 2], [step, n]]
+            key = "TZ1.%d" % len(parts.setdefault("TZ1", []))
+            op("g", lambda: g.iota(ap, pattern, base, 0, allow_small_or_imprecise_dtypes=True), ["TZ1"], [key])
+            parts["TZ1"].append(key)
+
+    def place_weights():
+        turn(T.TY[:, Z_GP:], T.TZ[:, Z_GP:], const("TZ1"), ["TY"])
+        in_group(T.ZZ[:, Z_GP:NZ, 15:128:16], T.TY[:, Z_GP:NZ, 0:8], [[0, NZ - Z_GP]], [], ["TY", "ZZ1"], "ZZ1")
+
+    def late_weights():
+        for lane, f, val in ((0, 0, 2.0 ** -11), (4, 7, -66 / 1024), (0, 3, 2.0 ** -11), (5, 7, 0.125), (0, 6, -1), (8, 6, 0.5), (0, 7, -5)):
+            affu(T.UU, "UU", lane, f, 0, val)
+        for t in range(2):
+            aff(T.UU[:, 4 * t:4 * t + 4, 1:9:2, 2:6], pu + [[0, 4]], -6, 0.5, "UU", [2, 3, 4, 5])
+
+    def each_bank(lhs, src, reads, start, ks=(0, 1, 2), sides=(0, 1)):
         for k in ks:
-            for t in range(2):
+            for t in sides:
                 mms([(PS[3 * t + k][:], lhs, src[:, third7[k]], start, False)], reads, ["P%d" % (3 * t + k)])
-    extract(7, 0, 3, T.W1, SH, ["W1"], True, False)
-    each_bank(T.AW[:, 0], T.W1, ["W1", "AW0"], False, (0,))
-    extract(7, 0, 2, T.W2B, SH, w2b, False, True)
-    ts(off(O_SIB[0]), fld(7, 0), -4160.0, None, A.add, None, ["P7"], [okey(O_SIB[0])])
-    ts(T.LA[:, 1, :], fld(7, 0), -4160.0, 0.0, A.add, A.max, ["P7"], ["LA1"])
-    ts(off(O_S[0], 0, 192), T.LA[:, 2:4, :], float(DUM), None, A.min, None, ["LA2", "LA3"], [okey(O_S[0])])
-    ts(T.COL[:, 3:4], T.COL[:, 2:3], -1024.0, T.COL[:, 4:5], A.mult, A.add, ["BBI", "B8"], ["BD"])
 
-    def sib_less_child(LS, ln):
-        for s in range(2):
-            tt(tm(6 + s), LS[:, 1, :], LS[:, 2 + s, :], A.subtract, [ln + "1", ln + str(2 + s)], ["T6_%d" % s])
-    sib_less_child(T.LA, "LA")
-    HALVES = ((7, (0, 512)), (6, (512, NV)))
+    def unpack_late(r):
+        ts(ti(1), ti(0), 2047, None, A.bitwise_and, None, ["I0"], ["I1"])
+        if r == 0:
+            ts(ti(2), ti(0), 12, None, A.arith_shift_right, None, ["I0"], ["I2"])
+        cp(off(O_PAR[r]), ti(1), ["I1"], [okey(O_PAR[r])])
+        if r == 0:
+            ts(off(O_SIC[r]), ti(2), float(DUM), None, A.min, None, ["I2"], [okey(O_SIC[r])])
+        else:
+            ts(off(O_SIC[r]), ti(6), 12288.0, float(DUM), A.add, A.min, ["I6"], [okey(O_SIC[r])])
 
-    def leaves_sum(H, r):
-        for b, (c0, c1) in HALVES:
-            o = PS[b][:, 0:c1 - c0]
-            mms([(o, T.ID[:], H[:, DUM + c0:DUM + c1], True, False), (o, T.ID[:], T.VB[:, c0:c1], False, True)],
-                ["ID", "VB", "HL%d" % r], ["P%d" % b])
+    LEAVES = ((6, PS[6][:], 0, 512), (7, PS[7][:, 0:64, :], 512, 768), (7, PS[7][:, 64, 0:1], 768, NV))
+    extract(7, 4, Z_W1, T.W1, SH, ["W1"] + zz0, True, False)
+    each_bank(AW[:, 0], T.W1, ["W1"] + const("AW"), False, (0,), (0,))
+    each_bank(AW[:, 0], T.W1, ["W1"] + const("AW"), False, (0,), (1,))
+    extract(7, 4, Z_W2, T.W2B, SH, w2b[:1] + zz0, False, False, part=(0, 48))
+    each_bank(AW[:, 0], T.W1, ["W1"] + const("AW"), False, (1,), (0,))
+    extract(7, 4, Z_W2, T.W2B, SH, w2b + zz0, False, True, part=(48, 96))
+    act(T.TZ[:, Z_GP:], T.W2B[:, SH:SH + 32 * (NZ + 1 - Z_GP)], F.Copy, w2b[:1], ["TZ1"], scale=0.0)
+    cp(T.VB[:], T.VI[:], ["VI"], ["VB"])
+    ts(off(O_SIB[0]), fld(7, 4), 1 / 4096, -0.44 - ZOFF / 4096, A.mult, A.add, ["P7"], [okey(O_SIB[0])])
+    ts(ti(0), fld(7, 4), -ZOFF, 0.0, A.add, A.max, ["P7"], ["I0"])
+    turn(T.COL[:, 1:3], T.TC[:, 1:3], const("TC"), ["BA"])
+    unpack_late(0)
 
     def leaves_cap():
-        for b, (c0, c1) in HALVES:
-            act(T.YT[:, c0:c1], PS[b][:, 0:c1 - c0], F.Relu, ["P%d" % b], ["YT%d" % b], bias=255.0, scale=-1.0)
+        act(T.YT[:], T.YS[:], F.Relu, ["YS"], ["YT"], bias=255.0, scale=-1.0)
 
     def leaves_out(out, key):
-        act(out, T.YT[:], F.Relu, ["YT6", "YT7"], [key], bias=255.0, scale=-1.0)
+        act(out, T.YT[:], F.Relu, ["YT"], [key], bias=255.0, scale=-1.0)
+    dma("g", T.YS[:], T.VB[:], ["VB"], ["YS"])
+    verdict_weights()
+    list_weights()
+    op("g", lambda: g.iota(T.ZZ[:, 4:NZ], [[0, 144 * (NZ - 4)]], 0, 0, allow_small_or_imprecise_dtypes=True), [], ["ZZ1"])
 
     for r in range(2):
         H = [T.H0, T.H1][r]
-        LS, ln = [(T.LA, "LA"), (T.LB, "LB")][r]
-        hk = keys("HI%d" % r, 6) + ["HL%d" % r, "HG%d" % r, "HZ%d" % r]
-        oh, os_, osib, opar = O_H[r], O_S[r], O_SIB[r], O_PAR[r]
-        for i, (c0, c1) in enumerate(((0, 16), (16, 32), (32, 64), (64, 96))):
+        hk = keys("HI%d" % r, 6) + ["HL%d" % r, "HG%d" % r] + const("HZ%d" % r)
+        oh, osib, osic, opar, oic = O_H[r], O_SIB[r], O_SIC[r], O_PAR[r], O_IC[r]
+        def siblings(i):
+            c0, c1 = ((0, 16), (16, 32), (32, 64), (64, 96))[i]
             act(T.HS[:, 16 * c0:16 * c1], H[:].indirect(off(osib, c0, c1)), F.Copy, hk + [okey(osib)], ["HS_%d" % i])
 
-        def ids(k):
+        def ids(k, t):
             if r == 1:
-                for t in range(2):
-                    mms(from_y(3 * t + k, k, t, "part"), ["YY", "UU0", "UU1"], ["P%d" % (3 * t + k)])
+                mms(from_y(3 * t + k, k, T.UU, t, "part"), ["YY"] + const("UU"), ["P%d" % (3 * t + k)])
                 return
-            each_bank(T.BB[:, 0], T.H0, keys("HI0", 6) + ["BB"], False, (k,))
-            each_bank(T.AW[:, 0], T.W2B, w2b + ["AW0"], False, (k,))
-            if k > 0:
-                each_bank(T.AW[:, 0], T.W1, ["W1", "AW0"], False, (k,))
-        ids(0)
-        for k in range(3):
-            pieces = ((0, 16, 0), (16, 32, 1)) if k == 0 else ((32 * k, 32 * k + 32, k + 1),)
-            if k < 2:
-                ids(k + 1)
-            for t, M, mn in ((0, T.M1, "M1"), (1, T.M2, "M2")):
-                for c0, c1, i in pieces:
-                    tt(M[:, 16 * c0:16 * c1], H[:].indirect(off(oh + 1 - t, c0, c1)), T.HS[:, 16 * c0:16 * c1], A.max,
-                       hk + [okey(oh + 1 - t), "HS_%d" % i], ["%s_%d" % (mn, i)])
-                mms([(PS[3 * t + k][:], T.BB[:, 1], M[:, third[k]], False, True)],
-                    ["%s_%d" % (mn, i) for c0, c1, i in pieces] + ["BB"], ["P%d" % (3 * t + k)])
-            act(T.TB[:, third[k]], PS[k][:], F.Relu, ["P%d" % k, "BA"], ["TA_%d" % k], bias=T.COL[:, 1:2])
-        if r == 0:
-            extract(6, 0, 0, T.W1, SH, ["W1"], True, False)
-            extract(6, 0, 0, T.W2B, SH, w2b, False, True)
-        for k in range(3):
-            tt(T.WB[:, third7[k]], PS[3 + k][:], T.TB[:, third[k]], A.max, ["P%d" % (3 + k), "TA_%d" % k], ["WB_%d" % k])
-        wb = keys("WB", 3) + ["WBz", "WBy"]
-        if r == 0:
-            cp(T.VB[:], T.VI[:], ["VI"], ["VB"])
-            for b in range(4):
-                mms([(PQ[b], T.AW[:, 1], T.W1[:, quarter[b]], True, False),
-                     (PQ[b], T.AW[:, 2], T.W2B[:, quarter[b]], False, False)], ["AW1", "W1"] + w2b, ["P%d" % b])
+            if 2 * k + t > 2:
+                each_bank(AW[:, 0], T.W1, ["W1"] + const("AW"), False, (k,), (t,))
+            each_bank(AW[:, 1], T.W2B, w2b + const("AW"), False, (k,), (t,))
+            each_bank(BB[0], T.H0, keys("HI0", 6) + ["BB0"], False, (k,), (t,))
+
+        def best(k):
+            tt(WB[:, third7[k]], PS[3 + k][:], T.TB[:, third[k]], A.max, ["P%d" % (3 + k), "TA_%d" % k], ["WB_%d" % k])
+            if (r, k) == (1, 1):
+                act(PS[4][:], WB[:, third7[k]], F.Identity, ["WB_%d" % k], ["P4"], bias=BW)
+            else:
+                act(T.SRC[:, third[k]], WB[:, third7[k]], F.Identity, ["WB_%d" % k], ["SRC_%d" % k], bias=BW)
+
+        def digits():
+            N1 = PS[7][:, 0:96, 0:3]
+            tt(PS[7][:, 0:96, 1], T.LC[:, 0, :], ti(6), A.subtract, ["LC0", "I6"], ["P7", "N10"])
+            ts(ti(4), ti(0), 4095, None, A.bitwise_and, None, ["I0"], ["I4"])
+            tt(PS[7][:, 0:96, 2], T.LC[:, 1, :], ti(6), A.subtract, ["LC1_1", "I6"], ["P7", "N11"])
+            ts(PS[7][:, 0:96, 0], ti(4), 8192.0, None, A.add, None, ["I4"], ["P7", "N12"])
+            ts(T.XX[:, :, 6], ti(4), 2048.0, None, A.is_ge, None, ["I4"], ["XX6"])
+            nk1 = ["P7", "N10", "N11", "N12"]
+            cp(T.XX[:, :, 0:3], N1, nk1, ["XXh"])
+            tt(T.XX[:, :, 3:6], N1, T.XX[:, :, 0:3], A.subtract, nk1 + ["XXh"], ["XXl"])
+            turn(T.YY[:], T.XX[:], XK, ["YY"])
+        def larger(k, t):
+            M, mn = ((T.M1, "M1"), (T.M2, "M2"))[t]
+            pieces = ((0, 16, 0), (16, 32, 1)) if k + t == 0 else ((32 * k, 32 * k + 32, k + 1),)
+            if r == 1 and k == 0:
+                pieces = ((0, 32, 1),)
+            for c0, c1, i in pieces:
+                tt(M[:, 16 * c0:16 * c1], H[:].indirect(off(oh + 1 - t, c0, c1)), T.HS[:, 16 * c0:16 * c1], A.max,
+                   hk + [okey(oh + 1 - t), "HS_%d" % i], ["%s_%d" % (mn, i)])
+            mms([(PS[3 * t + k][:], BB[1], M[:, third[k]], False, True)],
+                ["%s_%d" % (mn, i) for c0, c1, i in pieces] + ["BB1"], ["P%d" % (3 * t + k)])
+
+        def first(k):
+            act(T.TB[:, third[k]], PS[k][:], F.Relu, ["P%d" % k, "BA"], ["TA_%d" % k], bias=BA)
+
+        def other():
+            act(T.DP[:, third[1]], H[:].indirect(off(oh, 32, 64)), F.Copy, hk + [okey(oh)], ["HK"], scale=-1.0)
+
+        def less():
+            mms([(PS[6][:], T.ID[:], T.DP[:, third[1]], True, False), (PS[6][:], T.ID[:], T.HS[:, third[1]], False, True)],
+                const("ID") + ["HK", "HS_2"], ["P6"])
+
+        def over():
+            act(T.M2[:, third[1]], PS[6][:], F.Relu, ["P6"], ["M2_2"])
+
+        def summed(src, key, stop):
+            mms([(PS[4][:], BB[stop], src[:, third[1]], False, stop)], [key, "BB0", "BB1"], ["P4"])
+        if r == 0 and not F1:
+            for i in range(4):
+                siblings(i)
+            ids(0, 0)
+            ids(0, 1)
+            ids(1, 0)
+            larger(0, 0)
+            first(0)
+            act(tm(1), fld(7, 4), F.Relu, ["P7"], ["T1"], bias=-ZOFF)
+            ids(1, 1)
+            larger(0, 1)
+            ids(2, 0)
+            larger(1, 0)
+            first(1)
+            for b, o, c0, c1 in LEAVES:
+                mms([(o, T.ID[:], T.H0[:, DUM + c0:DUM + c1], True, False), (o, T.ID[:], T.VB[:, c0:c1], False, True)],
+                    const("ID") + ["VB", "HL0"], ["P%d" % b])
+            best(0)
+            larger(1, 1)
+            for b, o, c0, c1 in LEAVES:
+                act(T.YT[:, c0:c1], o, F.Relu, ["P%d" % b], ["YT"], bias=255.0, scale=-1.0)
+            ids(2, 1)
+            larger(2, 0)
+            first(2)
+            best(1)
+            larger(2, 1)
+            tt(ti(3), T.KI[:, 0, :], T.KI[:, 1, :], A.min, ["KI0", "KI1"], ["I3"])
+            ts(tm(5), ti(1), 4096.0, 33.0 * 4096 - 640, A.mult, A.add, ["I1"], ["T5"])
+            best(2)
+            ts(off(oic), ti(3), float(SH), float(DUM), A.add, A.min, ["I3"], [okey(oic)])
+        elif r == 0:
+            for i in range(4):
+                siblings(i)
+            ids(0, 0)
+            ids(0, 1)
+            ids(1, 0)
+            ids(1, 1)
+            larger(0, 0)
+            first(0)
+            other()
+            ids(2, 0)
+            larger(0, 1)
+            ids(2, 1)
+            larger(1, 0)
+            first(1)
+            less()
+            over()
+            larger(2, 0)
+            first(2)
+            best(0)
+            summed(T.DP, "HK", False)
+            summed(T.M2, "M2_2", True)
+            larger(2, 1)
+            act(tm(1), fld(7, 4), F.Relu, ["P7"], ["T1"], bias=-ZOFF)
+            for b, o, c0, c1 in LEAVES:
+                mms([(o, T.ID[:], T.H0[:, DUM + c0:DUM + c1], True, False), (o, T.ID[:], T.VB[:, c0:c1], False, True)],
+                    const("ID") + ["VB", "HL0"], ["P%d" % b])
+            tt(ti(3), T.KI[:, 0, :], T.KI[:, 1, :], A.min, ["KI0", "KI1"], ["I3"])
+            ts(tm(5), ti(1), 4096.0, 33.0 * 4096 - 640, A.mult, A.add, ["I1"], ["T5"])
+            best(1)
+            ts(off(oic), ti(3), float(SH), float(DUM), A.add, A.min, ["I3"], [okey(oic)])
+            best(2)
+            act(T.YT[:, 0:512], PS[6][:], F.Relu, ["P6"], ["YT"], bias=255.0, scale=-1.0)
         else:
-            ts(off(opar), T.LB[:, 0, :], 2048.0, None, A.add, None, ["LB0"], [okey(opar)])
-            sib_less_child(LS, ln)
-        for i in range(6):
-            act(T.TB[:, 256 * i:256 * i + 256], T.WB[:].indirect(off(os_, 16 * i, 16 * i + 16)), F.Identity,
-                wb + [okey(os_), "BBI"], ["TB_%d" % i], bias=T.COL[:, 2:3])
-        for i in range(6):
-            tt(T.VV[:, SH + 256 * i:SH + 256 * i + 256], T.WB[:].indirect(off(os_ + 1, 16 * i, 16 * i + 16)),
-               T.TB[:, 256 * i:256 * i + 256], A.max, wb + [okey(os_), "TB_%d" % i], ["VV_%d" % i])
-            if i == 1:
-                if r == 0:
-                    ts(T.LA[:, 0, :], fld(6, 0), 4032.0, float(DUM), A.add, A.min, ["P6"], ["LA0"])
-                    ts(off(opar), fld(6, 0), 4032.0, float(DUM), A.add, A.min, ["P6"], [okey(opar)])
-                leaves_sum(H, r)
-        for k in range(3):
-            act(T.SRC[:, third[k]], T.VV[:, third7[k]], F.Copy, ["VV_%d" % (2 * k), "VV_%d" % (2 * k + 1)], ["VC_%d" % k])
-        vk = keys("VV", 6) + ["VVz", "VVy"]
-        for b in range(4):
-            mms([(PQ[b], T.FF[:], T.VV[:, quarter[b]], r == 1, False)],
-                ["VV_%d" % i for i in range(QC[b] // 16, (QC[b + 1] - 1) // 16 + 1)] + ["FF"], ["P%d" % b])
-        leaves_cap()
+            siblings(2)
+            other()
+            less()
+            summed(T.DP, "HK", False)
+            for i in (0, 1, 3):
+                siblings(i)
+            over()
+            digits()
+            ids(1, 0)
+            larger(1, 0)
+            first(1)
+            ids(0, 0)
+            ids(1, 1)
+            summed(T.M2, "M2_2", True)
+            larger(0, 0)
+            first(0)
+            ids(0, 1)
+            larger(0, 1)
+            best(1)
+            ids(2, 0)
+            larger(2, 0)
+            first(2)
+            ids(2, 1)
+            best(0)
+            larger(2, 1)
+            unpack_late(1)
+            best(2)
+        wb = keys("WB", 3) + const("WPz")
+        banks = ((0,), (1,), (2, 3))
+        RAW = T.OUT[:, third[1]]
+        if r == 1:
+            act(RAW, WB[:].indirect(off(osic, 32, 64)), F.Copy, wb + [okey(osic)], ["RAW"])
+        for k in (0, 2, 1):
+            if (r, k) == (1, 1):
+                tt(PB[:, third7[k]], PS[4][:], RAW, A.max, ["P4", "RAW"], ["PB_%d" % k])
+            else:
+                tt(PB[:, third7[k]], WB[:].indirect(off(osic, 32 * k, 32 * k + 32)), T.SRC[:, third[k]], A.max,
+                   wb + [okey(osic), "SRC_%d" % k], ["PB_%d" % k])
+            for b in banks[k]:
+                mms([(PQ[b], T.FF[:], PB[:, quarter[b]], True, False)], ["PB_%d" % k] + const("FF"), ["P%d" % b])
+            if (r, k) == (0, 0):
+                dma("s", T.TB[:, third[k]], PB[:, third7[k]], ["PB_%d" % k], ["TA_%d" % k])
+                for b, o, c0, c1 in LEAVES[1:] if F1 else ():
+                    act(T.YT[:, c0:c1], o, F.Relu, ["P%d" % b], ["YT"], bias=255.0, scale=-1.0)
+            elif (r, k) == (1, 1):
+                act(PS[5][:], PB[:, third7[k]], F.Copy, ["PB_%d" % k], ["P5"])
+                act(RAW, PB[:].indirect(off(oic, 32, 64)), F.Copy, keys("PB", 3) + const("WPz") + [okey(oic)], ["RAW"])
+            else:
+                act(T.TB[:, third[k]], PB[:, third7[k]], F.Copy, ["PB_%d" % k], ["TA_%d" % k])
+            if (r, k) == (0, 2):
+                act(tm(3), tm(1), F.Identity, ["T1"], ["T3"], scale=-1.0, bias=-33.0 * 4096)
+                act(tm(4), T.N0[:, :, 1], F.Identity, ["N01"], ["T4"], scale=4096.0, bias=-(2.0 ** 25 + 8192))
         if r == 0:
+            act(T.GS1[:], T.YT[:].indirect(off(O_SL, 0, 48)), F.Relu, ["YT", okey(O_SL)], ["GS1"], bias=255.0, scale=-1.0)
             leaves_out(T.H1[:, DUM:GH], "HL1")
+            send(T.GS1, ["GS1", "GS1"], T.H1, "arr1")
+            dma("g", T.YS[:], T.H1[:, DUM:GH], ["HL1", "YS"], ["YS"], True)
+            gfill(T.H1[:, 0:SH], SH, 255, "HZ1")
         else:
             leaves_out(T.OUT[:, NI:NI + NV], "OUTL")
             dma("s", T.yh[:, NI:NI + NV], T.OUT[:, NI:NI + NV], ["OUTL"], [])
-        for k in range(3):
-            tt(T.CW[:, third7[k]], T.VV[:].indirect(off(opar, 32 * k, 32 * k + 32)), T.SRC[:, third[k]], A.is_lt,
-               vk + [okey(opar), "VC_%d" % k], ["CW_%d" % k])
-            mms([(PQ[k], T.MC[:, 1], T.CW[:, quarter[k]], False, False)], keys("CW", k + 1) + ["MC1"], ["P%d" % k])
+        pb = keys("PB", 3) + const("WPz")
+        for k in ((2, 1, 0), (0, 2, 1))[r]:
+            if (r, k) == (1, 1):
+                tt(CW[:, third7[k]], PS[5][:], RAW, A.is_lt, ["P5", "RAW"], ["CW_%d" % k])
+            else:
+                tt(CW[:, third7[k]], PB[:].indirect(off(oic, 32 * k, 32 * k + 32)), T.TB[:, third[k]], A.is_gt,
+                   pb + [okey(oic), "TA_%d" % k], ["CW_%d" % k])
+            for b in banks[k]:
+                mms([(PQ[b], MC[0], CW[:, quarter[b]], False, False)], ["CW_%d" % k] + const("MC"), ["P%d" % b])
         cw = keys("CW", 3)
-        ck = cw + ["CWz", "CWy"]
-        mms([(PQ[3], T.MC[:, 1], T.CW[:, quarter[3]], False, False)], cw + ["MC1"], ["P3"])
+        ck = cw + const("CDz")
+        if r == 0:
+            plus(6, 0, [tm(4), T.N0[:, :, 2]], ["T4", "N02"], True, False)
+            plus(4, 2, [tm(3), tm(5)], ["T3", "T5"], True, False)
+            plus(5, 0, [tm(1)], ["T1"], True, False)
+        else:
+            for j in range(2):
+                mms([(fld(6 + j, 0, 48 * j, 48 * j + 48), T.IF[:], T.TM[:, 4, 48 * j:48 * j + 48], True, False)], ["T4", "IF"], ["P%d" % (6 + j)])
         for b in range(4):
             c0, c1 = QC[b], QC[b + 1]
-            cp(T.M2[:, 16 * c0:16 * c1], T.CW[:].indirect(off(os_ + 1, c0, c1)), ck + [okey(os_)], ["CR_%d" % b])
-            act(T.M1[:, 16 * c0:16 * c1], T.CW[:].indirect(off(os_, c0, c1)), F.Copy, ck + [okey(os_)], ["CL_%d" % b])
-            mms([(PQ[b], T.MC[:, 0], T.M2[:, 16 * c0:16 * c1], False, False),
-                 (PQ[b], T.MC[:, 0], T.M1[:, 16 * c0:16 * c1], False, True)], ["CR_%d" % b, "CL_%d" % b, "MC0"], ["P%d" % b])
+            cp(T.M2[:, 16 * c0:16 * c1], CW[:].indirect(off(osic, c0, c1)), ck + [okey(osic)], ["CR_%d" % b])
+            act(T.M1[:, 16 * c0:16 * c1], CW[:].indirect(off(opar, c0, c1)), F.Copy, ck + [okey(opar)], ["CL_%d" % b])
+            mms([(PQ[b], MC[0], T.M2[:, 16 * c0:16 * c1], False, False),
+                 (PQ[b], MC[1], T.M1[:, 16 * c0:16 * c1], False, True)], ["CR_%d" % b, "CL_%d" % b] + const("MC"), ["P%d" % b])
+            if r == 0 and b == 2:
+                place_weights()
+                late_weights()
         for b in range(4):
             if b % 2:
-                act(T.WD[:, quarter[b]], PQ[b], F.Relu, ["P%d" % b, "BD"], ["WD_%d" % b], bias=T.COL[:, 3:4])
+                act(WD[:, quarter[b]], PQ[b], F.Relu, ["P%d" % b, "TY"], ["WD_%d" % b], bias=BD)
             else:
-                ts(T.WD[:, quarter[b]], PQ[b], T.COL[:, 3:4], 0.0, A.add, A.max, ["P%d" % b, "BD"], ["WD_%d" % b])
-        wd = keys("WD", 4) + ["WDz", "WDy"]
+                ts(WD[:, quarter[b]], PQ[b], BD, 0.0, A.add, A.max, ["P%d" % b, "TY"], ["WD_%d" % b])
+        wd = keys("WD", 4) + const("CDz")
         if r == 0:
-            ts(off(O_SL, 48, 96), T.SLI[:], float(SH), None, A.add, None, ["SLI"], ["OSL1"])
+            ts(ti(4), ti(0), 4095, None, A.bitwise_and, None, ["I0"], ["I4"])
         for j in range(2):
             c0, c1, c2 = 48 * j, 48 * j + 24, 48 * j + 48
-            act(T.DP[:, 16 * c0:16 * c1], T.WD[:].indirect(off(opar, c0, c1)), F.Copy, wd + [okey(opar)], ["DP_%d" % (2 * j)])
-            cp(T.DP[:, 16 * c1:16 * c2], T.WD[:].indirect(off(opar, c1, c2)), wd + [okey(opar)], ["DP_%d" % (2 * j + 1)])
+            act(T.DP[:, 16 * c0:16 * c1], WD[:].indirect(off(oic, c0, c1)), F.Copy, wd + [okey(oic)], ["DP_%d" % (2 * j)])
+            cp(T.DP[:, 16 * c1:16 * c2], WD[:].indirect(off(oic, c1, c2)), wd + [okey(oic)], ["DP_%d" % (2 * j + 1)])
         dp = keys("DP", 4)
-        extract(6, 0, 6, T.WD, SH, wd)
-        for j in range(2):
-            extract(7, 0, 4, T.DP, 0, dp[2 * j:2 * j + 2], part=(48 * j, 48 * j + 48))
-        if r == 0:
-            act(T.GS1[:], T.H1[:, NI:GH].indirect(off(O_SL, 48, 96)), F.Copy, ["HL1", "HI1_5", "OSL1"], ["GS1"])
-            send(T.GS1, "GS1", T.H1, "arr1")
-        ts(pt(4, 0), fld(6, 0), 0.0, None, A.is_le, None, ["P6"], pk(4, 0))
-        ts(pt(5, 0), fld(6, 0), 0.0, -1.0, A.is_ge, A.mult, ["P6"], pk(5, 0))
-        for s in range(2):
-            tt(tm(2 + s), pt(4 + s, 0), LS[:, 2 + s, :], A.mult, pk(4 + s, 0) + [ln + str(2 + s)], ["T2_%d" % s])
-        for s in range(2):
-            tt(tm(4 + s), fld(6, 0), tm(2 + s), [A.max, A.min][s], ["P6", "T2_%d" % s], ["T4_%d" % s])
-        if r == 0:
-            extract(6, 3, 0, T.DP, 0, dp)
         ohn = O_H[r + 1]
-        KN = [[T.LB[:, 2, :], T.LB[:, 3, :]], [T.LC[:, 0, :], T.LC[:, 1, :]]][r]
-        nk = [["LB2", "LB3"], ["LC0", "LC1"]][r]
-        for s in range(2):
-            tt(pt(s, 0), fld(7, 0), LS[:, 2 + s, :], A.is_equal, ["P7", ln + str(2 + s)], pk(s, 0))
-        for s in range(2):
-            tt(pt(2 + s, 0), pt(s, 0), tm(6 + s), A.mult, pk(s, 0) + ["T6_%d" % s], pk(2 + s, 0))
-        for s in range(2):
-            tt(KN[s], pt(2 + s, 0), tm(4 + s), [A.add, A.subtract][s], pk(2 + s, 0) + ["T4_%d" % s], [nk[s]])
-        for s in range(2):
-            cp(off(ohn + s), KN[s], [nk[s]], [okey(ohn + s)])
-        if r == 0:
-            cp(tm(9), pt(1, 0), pk(1, 0), ["T9"])
-            ts(off(O_GP), fld(6, 3), 4032.0, float(DUM), A.add, A.min, ["P6"], [okey(O_GP)])
-            ts(tm(15), fld(7, 0), 0.0, None, A.is_equal, None, ["P7"], ["T15"])
-            extract(6, 1, 3, T.DP, 0, dp)
-            extract(6, 2, 5, T.DP, 0, dp)
-            extract(6, 4, 1, T.DP, 0, dp)
-            tt(tm(16), pt(0, 0), tm(9), A.add, pk(0, 0) + ["T9"], ["T16"])
-            tt(tm(12), T.LA[:, 0, :], LS[:, 1, :], A.subtract, ["LA0", "LA1"], ["T12"])
-        else:
+        nk = ["LC0", "LC1_0", "LC1_1"]
+
+        def children(b, a, e, js):
+            z = fld(b, 0, a, e)
+            ts(off(ohn, a, e), z, 1 / 4096, -0.38, A.mult, A.add, ["P%d" % b], ["OL%d_%d" % (r, j) for j in js])
+            cp(T.TI[:, 5, a:e], z, ["P%d" % b], ["I5_%d" % j for j in js])
+            if r == 0:
+                ts(tm(8), ti(4), -2047.5, None, A.add, None, ["I4"], ["T8"])
+            ts(T.LC[:, 1, a:e], T.TI[:, 5, a:e], 4095, None, A.bitwise_and, None, ["I5_%d" % j for j in js], ["LC1_%d" % j for j in js])
+            if r == 0:
+                lefts()
+            cp(off(ohn + 1, a, e), T.LC[:, 1, a:e], ["LC1_%d" % j for j in js], ["OR%d_%d" % (r, j) for j in js])
+
+        def lefts():
+            ts(T.LC[:, 0, :], ti(5), 12, None, A.arith_shift_right, None, keys("I5", 2), ["LC0"])
+
+        def left_values(i):
+            act(T.HS[:, 256 * i:256 * i + 256], H[:].indirect(off(ohn, 16 * i, 16 * i + 16)), F.Copy, hk + ["OL%d_%d" % (r, i // 3)],
+                ["HE_%d" % i])
+
+        def values(i):
+            o = T.H1[:, SH + 256 * i:SH + 256 * i + 256] if r == 0 else T.OUT[:, 256 * i:256 * i + 256]
+            tt(o, H[:].indirect(off(ohn + 1, 16 * i, 16 * i + 16)), T.HS[:, 256 * i:256 * i + 256], A.max,
+               hk + ["OR%d_%d" % (r, i // 3), "HE_%d" % i], ["HI1_%d" % i if r == 0 else "OUT_%d" % i])
+
+        def store(i0, i1):
+            dma("s", T.yh[:, 256 * i0:256 * i1], T.OUT[:, 256 * i0:256 * i1], ["OUT_%d" % j for j in range(i0, i1)], [])
+        if r == 1:
+            for j in range(2):
+                extract(6 + j, 0, Z_OWN, WD, SH, wd, False, False, part=(48 * j, 48 * j + 48))
+                extract(6 + j, 0, Z_KID, T.DP, 0, dp[2 * j:2 * j + 2], False, True, part=(48 * j, 48 * j + 48))
+            children(6, 0, 48, [0])
+            for i in range(3):
+                left_values(i)
+            values(0)
+            store(0, 1)
+            children(7, 48, 96, [1])
+            for i in range(3, 6):
+                left_values(i)
+            values(1)
+            values(2)
+            store(1, 3)
+            lefts()
+            values(3)
             for t in range(6):
                 ts(T.XT[:, 32 * t:32 * t + 32], T.LC[:, :, t::6], -float(SH), None, A.add, None, nk, ["XT_%d" % t])
-            op("v", lambda: V.transpose(T.YK[:], T.XT[:]), keys("XT", 6), ["YK"])
-        EC = [0, 16, 32, 48, 64, 80, 96] if r == 0 else [0, 16, 32, 48, 68, 86, 96]
-        for i in range(6):
-            act(T.HS[:, 16 * EC[i]:16 * EC[i + 1]], H[:].indirect(off(ohn, EC[i], EC[i + 1])), F.Copy, hk + [okey(ohn)],
-                ["HE_%d" % i])
-        if r == 1:
+            turn(T.YK[:], T.XT[:], keys("XT", 6), ["YK"])
+            values(4)
+            store(3, 5)
             for g0 in range(2):
                 act(T.YC[:, 96 * g0:96 * g0 + 96], T.YK[:, :, 16 * g0:16 * g0 + 16], F.Copy, ["YK"], ["YC_%d" % g0])
-            for g0 in range(2):
                 dma("a", T.yk[g0::2, :], T.YC[:, 96 * g0:96 * g0 + 96], ["YC_%d" % g0], [])
-        for i in range(6):
-            c0, c1 = 16 * EC[i], 16 * EC[i + 1]
-            o = T.H1[:, SH + c0:SH + c1] if r == 0 else T.OUT[:, c0:c1]
-            tt(o, H[:].indirect(off(ohn + 1, EC[i], EC[i + 1])), T.HS[:, c0:c1], A.max,
-               hk + [okey(ohn + 1), "HE_%d" % i], ["HI1_%d" % i if r == 0 else "OUT_%d" % i])
-            if r == 1 and i in (1, 3, 4, 5):
-                i0 = i - 1 if i < 4 else i
-                dma("s", T.yh[:, 16 * EC[i0]:c1], T.OUT[:, 16 * EC[i0]:c1], ["OUT_%d" % j for j in range(i0, i + 1)], [])
-        if r == 0:
+            values(5)
+            store(5, 6)
+        else:
+            extract(6, 0, Z_OWN, WD, SH, wd, False, False)
             for j in range(2):
-                act(T.GB[:, 768 * j:768 * j + 768], T.WD[:].indirect(off(O_GP, 48 * j, 48 * j + 48)), F.Copy,
-                    wd + [okey(O_GP)], ["GB_%d" % j])
-                extract(7, 2, 4, T.GB, 0, ["GB_%d" % j], part=(48 * j, 48 * j + 48))
-            tt(tm(17), tm(15), LS[:, 1, :], A.mult, ["T15", "LA1"], ["T17"])
-            tt(tm(18), fld(6, 2), tm(16), A.mult, ["P6", "T16"], ["T18"])
-            tt(pt(4, 1), tm(15), tm(16), A.add, ["T15", "T16"], pk(4, 1))
-            tt(pt(5, 1), fld(6, 1), tm(17), A.add, ["P6", "T17"], pk(5, 1))
-            tt(tm(10), fld(6, 3), LS[:, 0, :], A.subtract, ["P6", "LA0"], ["T10"])
-            tt(tm(27), pt(4, 1), tm(12), A.mult, pk(4, 1) + ["T12"], ["T27"])
-            tt(pt(3, 1), pt(5, 1), tm(18), A.add, pk(5, 1) + ["T18"], pk(3, 1))
-            tt(tm(11), fld(6, 4), LS[:, 1, :], A.subtract, ["P6", "LA1"], ["T11"])
-            ts(tm(29), LS[:, 1, :], -2048.0, None, A.add, None, ["LA1"], ["T29"])
-            ts(tm(14), tm(10), 4032.0, None, A.add, None, ["T10"], ["T14"])
-            ts(tm(13), tm(11), -4160.0, None, A.add, None, ["T11"], ["T13"])
-            tt(pt(2, 1), tm(27), tm(29), A.add, ["T27", "T29"], pk(2, 1))
-            ts(off(O_S[1], 0, 192), T.LB[:, 2:4, :], float(DUM), None, A.min, None, nk, [okey(O_S[1])])
-            digits(T.LB, "LB", 2, 4)
-            tt(pt(4, 2), fld(7, 2), T.Y7[:], A.is_equal, ["P7", "Y7"], pk(4, 2))
-            tt(pt(4, 3), fld(7, 2), LS[:, 1, :], A.is_equal, ["P7", "LA1"], pk(4, 3))
-            tt(tm(28), pt(4, 2), tm(14), A.mult, pk(4, 2) + ["T14"], ["T28"])
-            tt(tm(24, 2), PS[4][:, 4:8, 0:48], tm(12, 2), A.mult, pk(4, 2) + pk(4, 3) + ["T12", "T13"], ["T24"])
-            tt(T.LB[:, 0, :], pt(2, 1), tm(28), A.add, pk(2, 1) + ["T28"], ["LB0"])
-            tt(pt(5, 2), pt(3, 1), tm(24), A.add, pk(3, 1) + ["T24"], pk(5, 2))
-            ts(T.HI[:, 0, :], T.LB[:, 0, :], 6, None, A.arith_shift_right, None, ["LB0"], ["HI0"])
-            ts(T.LO[:, 0, :], T.LB[:, 0, :], 63, None, A.bitwise_and, None, ["LB0"], ["LO0"])
-            tt(T.LB[:, 1, :], pt(5, 2), tm(25), A.add, pk(5, 2) + ["T24"], ["LB1"])
-            cp(T.XX[:, 0::8], T.HI[:, 0, :], ["HI0"], ["XX0"])
-            cp(T.XX[:, 1::8], T.LO[:, 0, :], ["LO0"], ["XX1"])
-            cp(off(O_SIB[1]), T.LB[:, 1, :], ["LB1"], [okey(O_SIB[1])])
-            each_bank(T.BB[:, 0], T.H1, keys("HI1", 6) + ["BB"], True)
-            turn()
+                extract(6, 0, Z_KID, T.DP, 0, dp[2 * j:2 * j + 2], False, j == 1, part=(48 * j, 48 * j + 48))
+            act(T.GB[:, 0:768], WD[:].indirect(off(opar, 0, 48)), F.Copy, wd + [okey(opar)], ["GB_0"])
+            cp(T.GB[:, 768:NI], WD[:].indirect(off(opar, 48, 96)), wd + [okey(opar)], ["GB_1"])
+            extract(0, 0, Z_ISW, WD, SH, wd)
+            tt(tm(6), ti(2), tm(3), A.add, ["I2", "T3"], ["T6"])
+            children(6, 0, 96, [0, 1])
+            tt(tm(9), fld(0, 0), tm(6), A.max, ["P0", "T6"], ["T9"])
+            for s in range(2):
+                lastw[okey(ohn + s)] = lastw["O%s0_1" % "LR"[s]]
+            extract(1, 0, Z_T, T.GB, 0, keys("GB", 2))
+            extract(4, 2, Z_GP, T.GB, 0, keys("GB", 2), False, True)
+            extract(3, 1, Z_Z, T.GB, 0, keys("GB", 2))
+            plus(5, 0, [tm(9)], ["T9"], False, False)
+            extract(5, 0, Z_Z, WD, SH, wd, False, False)
+            for i in range(6):
+                left_values(i)
+            act(tm(4), fld(6, 0), F.Copy, ["P6"], ["T4"])
+            leaves_cap()
+            values(0)
+            values(1)
+            tt(tm(10), fld(1, 0), tm(8), A.mult, ["P1", "T8"], ["T10"])
+            values(2)
+            ts(tm(11), tm(10), 0.0, None, A.is_gt, None, ["T10"], ["T11"])
+            ts(tm(12), tm(10), 0.0, -1.0, A.is_lt, A.mult, ["T10"], ["T12"])
+            values(3)
+            tt(tm(13), fld(4, 2), tm(11), A.mult, ["T11", "P4"], ["T13"])
+            tt(tm(14), fld(3, 1), tm(12), A.mult, ["P3", "T12"], ["T14"])
+            plus(5, 0, [tm(13), tm(14)], ["T13", "T14"])
+            values(4)
+            values(5)
+            tt(ti(3), T.LC[:, 0, :], T.LC[:, 1, :], A.min, nk, ["I3"])
+            ts(off(O_IC[1]), ti(3), float(DUM), None, A.min, None, ["I3"], [okey(O_IC[1])])
+            ts(off(O_SIB[1]), fld(5, 0), 1 / 4096, -0.44, A.mult, A.add, ["P5"], [okey(O_SIB[1])])
+            ts(ti(6), fld(5, 0), 1 / 4096, -12288.44, A.mult, A.add, ["P5"], ["I6"])
+            cp(ti(0), fld(5, 0), ["P5"], ["I0"])
+            each_bank(BB[0], T.H1, keys("HI1", 6) + ["BB0"], True)
 
     for s, c in total.items():
         if waited["g"].get(s, 0) < c:

@@ -6,13 +6,13 @@ SH = 7
 DUM = NI + SH
 GH = NI + NV + SH
 WID = GH + 3 * NG
-F1 = 0
+D1, E1, G1, G2, HV = 64, 16, 48, 80, 1088
 NZ = 8
 
 SCRATCH = {
     "KI": ("sbuf", [128, 2, 96], "int32"), "SLI": ("sbuf", [128, 48], "int32"),
     "HLI": ("sbuf", [128, NV], "int32"), "HII": ("sbuf", [128, NI], "int32"), "VI": ("sbuf", [128, NV], "int32"),
-    "VB": ("sbuf", [128, NV], "bfloat16"), "YT": ("sbuf", [128, NV], "float32"),
+    "YT": ("sbuf", [128, NV], "float32"),
     "H0": ("sbuf", [128, WID], "bfloat16"), "H1": ("sbuf", [128, WID], "bfloat16"),
     "GS0": ("sbuf", [128, 3 * NG], "bfloat16"), "GS1": ("sbuf", [128, 3 * NG], "bfloat16"),
     "W1": ("sbuf", [128, WID], "bfloat16"), "W2": ("sbuf", [128, WID], "float32"),
@@ -27,7 +27,6 @@ SCRATCH = {
     "OF": ("sbuf", [128, 15 * 96], "uint16"),
     "TC": ("sbuf", [128, 3, 2, 16], "float32"), "COL": ("sbuf", [128, 3, 32], "float32"),
     "TZ": ("sbuf", [128, NZ + 1, 4, 4, 2], "bfloat16"), "TY": ("sbuf", [128, NZ + 1, 32], "bfloat16"),
-    "YS": ("sbuf", [128, NV], "float32"),
     "XX": ("sbuf", [128, 96, 8], "bfloat16"), "YY": ("sbuf", [128, 24, 32], "bfloat16"),
     "XT": ("sbuf", [128, 192], "float32"), "YK": ("sbuf", [128, 6, 32], "float32"), "YC": ("sbuf", [128, 192], "float32"),
     "UU": ("sbuf", [128, 12, 10, 16], "bfloat16"),
@@ -192,7 +191,7 @@ def rank_program(g, core, T, topo):
     def engines_of(src, dst, d):
         e = topo.engines(src, dst)
         h = len(e) // 2
-        return [e[:h], e[h:], e][d - 1]
+        return [e, e[:h], e[h:]][d - 1]
 
     def send(src, skeys, dst, sem):
         trs = []
@@ -204,7 +203,7 @@ def rank_program(g, core, T, topo):
                                          remote_sem=T.sem[sem], src=src[:, (d - 1) * NG:d * NG],
                                          dst=dst[:, GH + (d - 1) * NG:GH + d * NG]))
             total["sent"] = total.get("sent", 0) + len(e)
-        for key, some in zip(skeys, (trs[:2], trs[2:])):
+        for key, some in zip(skeys, (trs[:1], trs[1:])):
             sync("g", [key], [])
             g.remote_dma_fused(some, local_sem=T.sem.sent)
 
@@ -224,7 +223,6 @@ def rank_program(g, core, T, topo):
     dma("s", T.HLI[:], T.h0[:, NI:NI + NV], [], ["HLI"])
     dma("a", T.SLI[:], T.sl[:], [], ["SLI"])
     dma("s", T.HII[:], T.h0[:, 0:NI], [], ["HII"])
-    dma("s", T.VI[:], T.vel[:], [], ["VI"])
 
     LANE, BA, BW, BD = T.COL[:, 0, 0:1], T.COL[:, 1, 0:1], T.COL[:, 2, 0:1], T.TY[:, NZ, 0:1]
     WB, PB, CW, WD = T.WB, T.PB, T.CW, T.WD
@@ -245,29 +243,26 @@ def rank_program(g, core, T, topo):
     turn(T.COL[:, 0], T.TC[:, 0], ["TC0"], ["LANE"])
     fill(T.XX[:, :, 6], 0.0, ["XX6"])
     ts(T.N0[:, :, 0], tm(0), LANE, None, A.add, None, ["T0", "LANE"], ["N00"])
-    fill(T.XX[:, :, 7], 1.0, ["XX7"])
-    cp(T.XX[:, :, 0], T.N0[:, :, 0], ["N00"], ["XX0"])
 
-    for s in range(2):
+    for s in (1, 0):
         ts(T.N0[:, :, 1 + s], T.KI[:, s, :], SH + 8192.0, None, A.add, None, ["KI%d" % s], ["N0%d" % (1 + s)])
-    nk0 = ["N01", "N02"]
-    tt(T.XX[:, :, 3], T.N0[:, :, 0], T.XX[:, :, 0], A.subtract, ["N00", "XX0"], ["XX3"])
-    cp(T.XX[:, :, 1:3], T.N0[:, :, 1:3], nk0, ["XXh"])
-    tt(T.XX[:, :, 4:6], T.N0[:, :, 1:3], T.XX[:, :, 1:3], A.subtract, nk0 + ["XXh"], ["XXl"])
-    XK = ["XXh", "XXl", "XX6", "XX7", "XX0", "XX3"]
-    turn(T.YY[:], T.XX[:], XK, ["YY"])
-    for k in range(3):
-        mms(from_y(k, k, T.UU, 2, "alone"), ["YY"] + const("US"), ["P%d" % k])
+    nk0 = ["N00", "N01", "N02"]
+    fill(T.XX[:, :, 7], 1.0, ["XX7"])
+    cp(T.XX[:, :, 0:3], T.N0[:], nk0, ["XXh"])
     cp(off(O_SL, 0, 48), T.SLI[:], ["SLI"], [okey(O_SL)])
+    XK = ["XXh", "XXl", "XX6", "XX7"]
+    for c0, c1, ks in ((0, 32, (0,)), (32, 96, (1, 2))):
+        tt(T.XX[:, c0:c1, 3:6], T.N0[:, c0:c1], T.XX[:, c0:c1, 0:3], A.subtract, nk0 + ["XXh"], ["XXl%d" % c0])
+    for c0, c1, ks in ((0, 32, (0,)), (32, 96, (1, 2))):
+        turn(T.YY[:, c0 // 4:c1 // 4], T.XX[:, c0:c1], ["XXh", "XXl%d" % c0, "XX6", "XX7"], ["YY%d" % c0])
+        for k in ks:
+            mms(from_y(k, k, T.UU, 2, "alone"), ["YY%d" % c0] + const("US"), ["P%d" % k])
+    lastw["YY"], lastw["XXl"] = lastw["YY32"], lastw["XXl32"]
     ts(off(O_H[0], 0, 192), T.KI[:], float(SH), None, A.add, None, ["KI0", "KI1"], [okey(O_H[0]), okey(O_H[0] + 1)])
     fill(T.CB[:], 0.0, ["AW", "BB", "MC", "SM"])
-    BLOCKS = ((0, 32), (32, 48))
+    BLOCKS = ((0, 16), (16, 48))
     for j, (c0, c1) in enumerate(BLOCKS):
         cp(T.GS0[:, 16 * c0:16 * c1], T.HLI[:].indirect(off(O_SL, c0, c1)), ["HLI", okey(O_SL)], ["GS0_%d" % j])
-    for s in range(2):
-        ts(T.CB[:, 2 + s, 0::2], T.CODE[:], LANE, 1.0 - 2 * s, A.is_equal, A.mult, ["CODE", "LANE", "BB"], ["BB%d" % s])
-    for s in range(2):
-        ts(T.CB[:, 2 + s, 1::2, 0, 0], T.CODE[:, :, 0], LANE, 1.0 - 2 * s, A.is_equal, A.mult, ["CODE", "LANE", "BB%d" % s], ["BB%d" % s])
     third = [slice(512 * k, 512 * k + 512) for k in range(3)]
     third7 = [slice(SH + 512 * k, SH + 512 * k + 512) for k in range(3)]
     pz = [[-16, 8]]
@@ -283,16 +278,21 @@ def rank_program(g, core, T, topo):
     QC = [0, 32, 64, 84, 96]
     quarter = [slice(SH + 16 * QC[b], SH + 16 * QC[b + 1]) for b in range(4)]
     PQ = [PS[b][:, 0:(QC[b + 1] - QC[b]) // 4, :] for b in range(4)]
-    for k in range(3):
+    for k in range(2):
         act(T.SRC[:, third[k]], PS[k][:], F.Identity, ["P%d" % k], ["SRC_%d" % k], bias=128.0)
-    act(T.W2[:].indirect(off(O_H[0] + 1)), T.SRC[:], F.Silu, keys("SRC", 3) + [okey(O_H[0] + 1)], ["W2"])
-    for j in range(2):
-        c = slice(SH + 768 * j, SH + 768 * j + 768)
-        act(T.W2B[:, c], T.W2[:, c], F.Copy, ["W2"], ["W2B_%d" % j])
+    ts(T.SRC[:, third[2]], PS[2][:], 128.0, None, A.add, None, ["P2"], ["SRC_2"])
     for c0, c1 in ((0, 64), (64, 96)):
-        cp(T.W1[:].indirect(off(O_H[0], c0, c1)), T.SRC[:, 16 * c0:16 * c1], keys("SRC", c1 // 32) + [okey(O_H[0])], ["W1", "W1a"])
-    cp(T.H0[:, DUM:GH], T.HLI[:], ["HLI"], ["HL0"])
-    cp(T.H0[:, SH:DUM], T.HII[:], ["HII"], keys("HI0", 6))
+        act(T.W2[:].indirect(off(O_H[0] + 1, c0, c1)), T.SRC[:, 16 * c0:16 * c1], F.Silu, keys("SRC", c1 // 32) + [okey(O_H[0] + 1)], ["W2"])
+    act(T.W2B[:, SH:SH + 1024], T.W2[:, SH:SH + 1024], F.Copy, ["W2"], ["W2B_0"])
+    act(T.H0[:, DUM:GH], T.HLI[:], F.Copy, ["HLI"], ["HL0"])
+    act(T.H0[:, SH + HV:DUM], T.HII[:, HV:NI], F.Copy, ["HII"], keys("HI0", 6)[3:])
+    cp(T.W1[:].indirect(off(O_H[0])), T.SRC[:], keys("SRC", 3) + [okey(O_H[0])], ["W1", "W1a"])
+    cp(T.W2B[:, SH + 1024:DUM], T.W2[:, SH + 1024:DUM], ["W2"], ["W2B_1"])
+    for s in range(2):
+        ts(T.CB[:, 2 + s, 0::2], T.CODE[:], LANE, 1.0 - 2 * s, A.is_equal, A.mult, ["CODE", "LANE", "BB"], ["BB%d" % s])
+    for s in range(2):
+        ts(T.CB[:, 2 + s, 1::2, 0, 0], T.CODE[:, :, 0], LANE, 1.0 - 2 * s, A.is_equal, A.mult, ["CODE", "LANE", "BB%d" % s], ["BB%d" % s])
+    cp(T.H0[:, SH:SH + HV], T.HII[:, 0:HV], ["HII"], keys("HI0", 3))
     w2b = keys("W2B", 2)
 
     def gcopy(out, in_, n, reads, writes):
@@ -317,25 +317,30 @@ def rank_program(g, core, T, topo):
     for w in ws[len(zs):]:
         aff(*w)
     zz0 = const("ZZ0")
+    OUTL = T.OUT[:, NI:NI + NV]
     for l0, l1, val in ((3, 9, 0.25), (7, 8, 0.25 + 1 / 2048)):
         op("g", lambda: g.affine_select(T.TC[:, 1, :, l0:l1], T.TC[:, 1, :, l0:l1], [[0, 2 * (l1 - l0)]], A.is_gt, val, 0, 0),
            ["TC"], ["TC"])
     for l0, l1, val in ((8, 10, 4096), (10, 11, 256)):
         gfill(T.TC[:, 2, :, l0:l1], 2 * (l1 - l0), val, "TC")
-    gfill(T.ID[:], 128, 0, "IDz")
+    gfill(T.IF[:], 128, 0, "IFz")
+    lastw["IF"] = lastw["IFz.0"]
     gfill(T.FF[:], 128, 0, "FFz")
-    lastw["FF"], lastw["ID"] = lastw["FFz.0"], lastw["IDz.0"]
-    aff(T.ID[:], [[-1, 128]], 0, 1, "ID", "i")
+    lastw["FF"] = lastw["FFz.0"]
 
     def no_node(Ws, key):
         for W in Ws:
             gfill(W[:, 0:SH], SH, 0, key)
             gfill(W[:, DUM:DUM + 1], 1, 0, key)
     no_node((WB, PB), "WPz")
+    aff(T.IF[:], [[-1, 128]], 0, 1, "IF", "i")
     evens, one, two = slice(0, 3, 2), slice(1, 2), slice(2, 3)
     for s, k, lane, val in ((None, slice(0, 3), 3, -1024), (0, evens, 1, -512), (1, evens, 1, 512), (0, one, 2, -1024), (1, one, 2, 1024),
                             (0, evens, 2, 512), (1, evens, 2, -512), (1, one, 3, -3072), (None, one, 8, 1024), (0, two, 10, -2),
                             (None, one, 9, -1024), (1, two, 10, 2)):
+        if (s, lane) == (1, 2) and k == one:
+            dma("g", T.HLI[:], T.vel[:], ["HLI"], ["HLI"], True)
+            dma("s", T.VI[:], T.vel[:], ["HL0", okey(O_H[0])] + keys("HI0", 6), ["VI"])
         ss, kk = ([0, 1] if s is None else [s]), range(4)[k]
         aff(T.FF[:, ss[0]::3 - len(ss), k, :], pz + [[0, 2 * len(ss) * len(kk)]], -lane, val, "FF", [(a, b) for a in ss for b in kk])
     aff(T.FF[:, 0::2, 3, 0], pz, -1, 64, "FF", [(0, 3)])
@@ -349,7 +354,6 @@ def rank_program(g, core, T, topo):
         no_node((CW, WD), "CDz")
         for m in range(2):
             aff(T.CB[:, 4 + m, :, 0:3, :], pz + [[0, 12]], 0, 1024 * m - 512, "MC", [m])
-        gcopy(T.IF[:], T.ID[:], 128, const("ID"), ["IF"])
 
     def list_weights():
         for z, s, k0, k1, d, base, step in (
@@ -390,29 +394,24 @@ def rank_program(g, core, T, topo):
         else:
             ts(off(O_SIC[r]), ti(6), 12288.0, float(DUM), A.add, A.min, ["I6"], [okey(O_SIC[r])])
 
-    LEAVES = ((6, PS[6][:], 0, 512), (7, PS[7][:, 0:64, :], 512, 768), (7, PS[7][:, 64, 0:1], 768, NV))
     extract(7, 4, Z_W1, T.W1, SH, ["W1"] + zz0, True, False)
-    each_bank(AW[:, 0], T.W1, ["W1"] + const("AW"), False, (0,), (0,))
-    each_bank(AW[:, 0], T.W1, ["W1"] + const("AW"), False, (0,), (1,))
-    extract(7, 4, Z_W2, T.W2B, SH, w2b[:1] + zz0, False, False, part=(0, 48))
-    each_bank(AW[:, 0], T.W1, ["W1"] + const("AW"), False, (1,), (0,))
-    extract(7, 4, Z_W2, T.W2B, SH, w2b + zz0, False, True, part=(48, 96))
-    act(T.TZ[:, Z_GP:], T.W2B[:, SH:SH + 32 * (NZ + 1 - Z_GP)], F.Copy, w2b[:1], ["TZ1"], scale=0.0)
-    cp(T.VB[:], T.VI[:], ["VI"], ["VB"])
+    extract(7, 4, Z_W2, T.W2B, SH, w2b + zz0, False, True)
+    each_bank(AW[:, 0], T.W1, ["W1"] + const("AW"), False, (0, 1, 2), (0,))
     ts(off(O_SIB[0]), fld(7, 4), 1 / 4096, -0.44 - ZOFF / 4096, A.mult, A.add, ["P7"], [okey(O_SIB[0])])
     ts(ti(0), fld(7, 4), -ZOFF, 0.0, A.add, A.max, ["P7"], ["I0"])
-    turn(T.COL[:, 1:3], T.TC[:, 1:3], const("TC"), ["BA"])
     unpack_late(0)
+    turn(T.COL[:, 1:3], T.TC[:, 1:3], const("TC"), ["BA"])
+    tt(ti(3), T.KI[:, 0, :], T.KI[:, 1, :], A.min, ["KI0", "KI1"], ["I3"])
 
-    def leaves_cap():
-        act(T.YT[:], T.YS[:], F.Relu, ["YS"], ["YT"], bias=255.0, scale=-1.0)
+    def leaves_cap(moved, key):
+        act(T.YT[:], moved, F.Relu, [key], ["YT"], bias=255.0, scale=-1.0)
 
     def leaves_out(out, key):
         act(out, T.YT[:], F.Relu, ["YT"], [key], bias=255.0, scale=-1.0)
-    dma("g", T.YS[:], T.VB[:], ["VB"], ["YS"])
     verdict_weights()
+    op("g", lambda: g.iota(T.TZ[:, Z_GP:], [[0, 32 * (NZ + 1 - Z_GP)]], 0, 0, allow_small_or_imprecise_dtypes=True), [], ["TZ1"])
     list_weights()
-    op("g", lambda: g.iota(T.ZZ[:, 4:NZ], [[0, 144 * (NZ - 4)]], 0, 0, allow_small_or_imprecise_dtypes=True), [], ["ZZ1"])
+    gcopy(OUTL, T.VI[:], NV, ["VI"], ["OUTL"])
 
     for r in range(2):
         H = [T.H0, T.H1][r]
@@ -424,9 +423,9 @@ def rank_program(g, core, T, topo):
 
         def ids(k, t):
             if r == 1:
-                mms(from_y(3 * t + k, k, T.UU, t, "part"), ["YY"] + const("UU"), ["P%d" % (3 * t + k)])
+                mms(from_y(3 * t + k, k, T.UU, t, "part"), ["YY_%d" % k] + const("UU"), ["P%d" % (3 * t + k)])
                 return
-            if 2 * k + t > 2:
+            if t == 1:
                 each_bank(AW[:, 0], T.W1, ["W1"] + const("AW"), False, (k,), (t,))
             each_bank(AW[:, 1], T.W2B, w2b + const("AW"), False, (k,), (t,))
             each_bank(BB[0], T.H0, keys("HI0", 6) + ["BB0"], False, (k,), (t,))
@@ -444,16 +443,15 @@ def rank_program(g, core, T, topo):
             ts(ti(4), ti(0), 4095, None, A.bitwise_and, None, ["I0"], ["I4"])
             tt(PS[7][:, 0:96, 2], T.LC[:, 1, :], ti(6), A.subtract, ["LC1_1", "I6"], ["P7", "N11"])
             ts(PS[7][:, 0:96, 0], ti(4), 8192.0, None, A.add, None, ["I4"], ["P7", "N12"])
-            ts(T.XX[:, :, 6], ti(4), 2048.0, None, A.is_ge, None, ["I4"], ["XX6"])
             nk1 = ["P7", "N10", "N11", "N12"]
+            ts(T.XX[:, :, 6], ti(4), 2048.0, None, A.is_ge, None, ["I4"], ["XX6"])
             cp(T.XX[:, :, 0:3], N1, nk1, ["XXh"])
             tt(T.XX[:, :, 3:6], N1, T.XX[:, :, 0:3], A.subtract, nk1 + ["XXh"], ["XXl"])
-            turn(T.YY[:], T.XX[:], XK, ["YY"])
+            for k in (1, 0, 2):
+                turn(T.YY[:, 8 * k:8 * k + 8], T.XX[:, 32 * k:32 * k + 32], XK, ["YY", "YY_%d" % k] if k == 1 else ["YY_%d" % k])
         def larger(k, t):
             M, mn = ((T.M1, "M1"), (T.M2, "M2"))[t]
             pieces = ((0, 16, 0), (16, 32, 1)) if k + t == 0 else ((32 * k, 32 * k + 32, k + 1),)
-            if r == 1 and k == 0:
-                pieces = ((0, 32, 1),)
             for c0, c1, i in pieces:
                 tt(M[:, 16 * c0:16 * c1], H[:].indirect(off(oh + 1 - t, c0, c1)), T.HS[:, 16 * c0:16 * c1], A.max,
                    hk + [okey(oh + 1 - t), "HS_%d" % i], ["%s_%d" % (mn, i)])
@@ -469,80 +467,51 @@ def rank_program(g, core, T, topo):
         def less():
             mms([(PS[6][:], T.ID[:], T.DP[:, third[1]], True, False), (PS[6][:], T.ID[:], T.HS[:, third[1]], False, True)],
                 const("ID") + ["HK", "HS_2"], ["P6"])
+            mms([(PS[4][:], BB[0], T.DP[:, third[1]], False, False)], ["HK", "BB0"], ["P4"])
 
         def over():
             act(T.M2[:, third[1]], PS[6][:], F.Relu, ["P6"], ["M2_2"])
 
-        def summed(src, key, stop):
-            mms([(PS[4][:], BB[stop], src[:, third[1]], False, stop)], [key, "BB0", "BB1"], ["P4"])
-        if r == 0 and not F1:
+        def summed():
+            mms([(PS[4][:], BB[1], T.M2[:, third[1]], False, True)], ["M2_2", "BB1"], ["P4"])
+        if r == 0:
             for i in range(4):
                 siblings(i)
             ids(0, 0)
-            ids(0, 1)
             ids(1, 0)
+            ids(0, 1)
             larger(0, 0)
             first(0)
+            act(T.ZZ[:, 4:NZ], T.W2B[:, SH:SH + 144 * (NZ - 4)], F.Copy, w2b, ["ZZ1"], scale=0.0)
             act(tm(1), fld(7, 4), F.Relu, ["P7"], ["T1"], bias=-ZOFF)
-            ids(1, 1)
-            larger(0, 1)
+            act(tm(4), T.N0[:, :, 1], F.Identity, ["N01"], ["T4"], scale=4096.0, bias=-(2.0 ** 25 + 8192))
             ids(2, 0)
+            larger(0, 1)
             larger(1, 0)
             first(1)
-            for b, o, c0, c1 in LEAVES:
-                mms([(o, T.ID[:], T.H0[:, DUM + c0:DUM + c1], True, False), (o, T.ID[:], T.VB[:, c0:c1], False, True)],
-                    const("ID") + ["VB", "HL0"], ["P%d" % b])
-            best(0)
+            ids(1, 1)
+            larger(2, 0)
+            first(2)
+            ids(2, 1)
             larger(1, 1)
-            for b, o, c0, c1 in LEAVES:
-                act(T.YT[:, c0:c1], o, F.Relu, ["P%d" % b], ["YT"], bias=255.0, scale=-1.0)
-            ids(2, 1)
-            larger(2, 0)
-            first(2)
-            best(1)
-            larger(2, 1)
-            tt(ti(3), T.KI[:, 0, :], T.KI[:, 1, :], A.min, ["KI0", "KI1"], ["I3"])
-            ts(tm(5), ti(1), 4096.0, 33.0 * 4096 - 640, A.mult, A.add, ["I1"], ["T5"])
-            best(2)
-            ts(off(oic), ti(3), float(SH), float(DUM), A.add, A.min, ["I3"], [okey(oic)])
-        elif r == 0:
-            for i in range(4):
-                siblings(i)
-            ids(0, 0)
-            ids(0, 1)
-            ids(1, 0)
-            ids(1, 1)
-            larger(0, 0)
-            first(0)
-            other()
-            ids(2, 0)
-            larger(0, 1)
-            ids(2, 1)
-            larger(1, 0)
-            first(1)
-            less()
-            over()
-            larger(2, 0)
-            first(2)
+            act(tm(5), ti(1), F.Identity, ["I1"], ["T5"], scale=4096.0, bias=33.0 * 4096 - 640)
+            act(tm(6), ti(2), F.Identity, ["I2"], ["T6"], bias=-33.0 * 4096)
+            act(tm(7), ti(2), F.Identity, ["I2"], ["T7"], scale=-1.0, bias=33.0 * 4096)
+            act(tm(3), tm(1), F.Identity, ["T1"], ["T3"], scale=-1.0, bias=-33.0 * 4096)
             best(0)
-            summed(T.DP, "HK", False)
-            summed(T.M2, "M2_2", True)
             larger(2, 1)
-            act(tm(1), fld(7, 4), F.Relu, ["P7"], ["T1"], bias=-ZOFF)
-            for b, o, c0, c1 in LEAVES:
-                mms([(o, T.ID[:], T.H0[:, DUM + c0:DUM + c1], True, False), (o, T.ID[:], T.VB[:, c0:c1], False, True)],
-                    const("ID") + ["VB", "HL0"], ["P%d" % b])
-            tt(ti(3), T.KI[:, 0, :], T.KI[:, 1, :], A.min, ["KI0", "KI1"], ["I3"])
-            ts(tm(5), ti(1), 4096.0, 33.0 * 4096 - 640, A.mult, A.add, ["I1"], ["T5"])
             best(1)
-            ts(off(oic), ti(3), float(SH), float(DUM), A.add, A.min, ["I3"], [okey(oic)])
+            ts(ti(4), ti(0), 4095, None, A.bitwise_and, None, ["I0"], ["I4"])
+            plus(7, 3, [tm(1), tm(7)], ["T1", "T7"], True, False)
+            plus(6, 0, [T.N0[:, :, 2], tm(4)], ["N02", "T4"], True, False)
+            plus(4, 2, [tm(3), tm(5)], ["T3", "T5"], True, False)
             best(2)
-            act(T.YT[:, 0:512], PS[6][:], F.Relu, ["P6"], ["YT"], bias=255.0, scale=-1.0)
+            ts(off(oic), ti(3), float(SH), float(DUM), A.add, A.min, ["I3"], [okey(oic)])
+            plus(5, 0, [tm(6)], ["T6"], True, False)
         else:
             siblings(2)
             other()
             less()
-            summed(T.DP, "HK", False)
             for i in (0, 1, 3):
                 siblings(i)
             over()
@@ -551,19 +520,21 @@ def rank_program(g, core, T, topo):
             larger(1, 0)
             first(1)
             ids(0, 0)
-            ids(1, 1)
-            summed(T.M2, "M2_2", True)
             larger(0, 0)
             first(0)
+            leaves_out(OUTL, "OUTL")
+            dma("s", T.yh[:, NI:NI + NV], OUTL, ["OUTL"], [])
+            ids(1, 1)
+            summed()
+            ids(2, 0)
+            larger(2, 0)
             ids(0, 1)
             larger(0, 1)
             best(1)
-            ids(2, 0)
-            larger(2, 0)
             first(2)
             ids(2, 1)
-            best(0)
             larger(2, 1)
+            best(0)
             unpack_late(1)
             best(2)
         wb = keys("WB", 3) + const("WPz")
@@ -581,25 +552,19 @@ def rank_program(g, core, T, topo):
                 mms([(PQ[b], T.FF[:], PB[:, quarter[b]], True, False)], ["PB_%d" % k] + const("FF"), ["P%d" % b])
             if (r, k) == (0, 0):
                 dma("s", T.TB[:, third[k]], PB[:, third7[k]], ["PB_%d" % k], ["TA_%d" % k])
-                for b, o, c0, c1 in LEAVES[1:] if F1 else ():
-                    act(T.YT[:, c0:c1], o, F.Relu, ["P%d" % b], ["YT"], bias=255.0, scale=-1.0)
             elif (r, k) == (1, 1):
                 act(PS[5][:], PB[:, third7[k]], F.Copy, ["PB_%d" % k], ["P5"])
                 act(RAW, PB[:].indirect(off(oic, 32, 64)), F.Copy, keys("PB", 3) + const("WPz") + [okey(oic)], ["RAW"])
             else:
                 act(T.TB[:, third[k]], PB[:, third7[k]], F.Copy, ["PB_%d" % k], ["TA_%d" % k])
-            if (r, k) == (0, 2):
-                act(tm(3), tm(1), F.Identity, ["T1"], ["T3"], scale=-1.0, bias=-33.0 * 4096)
-                act(tm(4), T.N0[:, :, 1], F.Identity, ["N01"], ["T4"], scale=4096.0, bias=-(2.0 ** 25 + 8192))
+            if (r, k) == (0, 0):
+                leaves_cap(T.HLI[:], "HLI")
+                act(tm(8), ti(4), F.Identity, ["I4"], ["T8"], bias=-2047.5)
         if r == 0:
             act(T.GS1[:], T.YT[:].indirect(off(O_SL, 0, 48)), F.Relu, ["YT", okey(O_SL)], ["GS1"], bias=255.0, scale=-1.0)
             leaves_out(T.H1[:, DUM:GH], "HL1")
             send(T.GS1, ["GS1", "GS1"], T.H1, "arr1")
-            dma("g", T.YS[:], T.H1[:, DUM:GH], ["HL1", "YS"], ["YS"], True)
-            gfill(T.H1[:, 0:SH], SH, 255, "HZ1")
-        else:
-            leaves_out(T.OUT[:, NI:NI + NV], "OUTL")
-            dma("s", T.yh[:, NI:NI + NV], T.OUT[:, NI:NI + NV], ["OUTL"], [])
+            dma("g", OUTL, T.H1[:, DUM:GH], ["HL1", "OUTL"], ["OUTL"], True)
         pb = keys("PB", 3) + const("WPz")
         for k in ((2, 1, 0), (0, 2, 1))[r]:
             if (r, k) == (1, 1):
@@ -611,13 +576,9 @@ def rank_program(g, core, T, topo):
                 mms([(PQ[b], MC[0], CW[:, quarter[b]], False, False)], ["CW_%d" % k] + const("MC"), ["P%d" % b])
         cw = keys("CW", 3)
         ck = cw + const("CDz")
-        if r == 0:
-            plus(6, 0, [tm(4), T.N0[:, :, 2]], ["T4", "N02"], True, False)
-            plus(4, 2, [tm(3), tm(5)], ["T3", "T5"], True, False)
-            plus(5, 0, [tm(1)], ["T1"], True, False)
-        else:
-            for j in range(2):
-                mms([(fld(6 + j, 0, 48 * j, 48 * j + 48), T.IF[:], T.TM[:, 4, 48 * j:48 * j + 48], True, False)], ["T4", "IF"], ["P%d" % (6 + j)])
+        if r == 1:
+            for b, a, e in ((6, 0, 32), (7, 32, 96)):
+                mms([(fld(b, 0, a, e), T.IF[:], T.TM[:, 4, a:e], True, False)], ["T4"] + const("IF"), ["P%d" % b])
         for b in range(4):
             c0, c1 = QC[b], QC[b + 1]
             cp(T.M2[:, 16 * c0:16 * c1], CW[:].indirect(off(osic, c0, c1)), ck + [okey(osic)], ["CR_%d" % b])
@@ -626,6 +587,8 @@ def rank_program(g, core, T, topo):
                  (PQ[b], MC[1], T.M1[:, 16 * c0:16 * c1], False, True)], ["CR_%d" % b, "CL_%d" % b] + const("MC"), ["P%d" % b])
             if r == 0 and b == 2:
                 place_weights()
+                gfill(T.H1[:, 0:SH], SH, 255, "HZ1")
+                gcopy(T.ID[:], T.IF[:], 128, const("IF"), ["ID"])
                 late_weights()
         for b in range(4):
             if b % 2:
@@ -633,101 +596,113 @@ def rank_program(g, core, T, topo):
             else:
                 ts(WD[:, quarter[b]], PQ[b], BD, 0.0, A.add, A.max, ["P%d" % b, "TY"], ["WD_%d" % b])
         wd = keys("WD", 4) + const("CDz")
-        if r == 0:
-            ts(ti(4), ti(0), 4095, None, A.bitwise_and, None, ["I0"], ["I4"])
-        for j in range(2):
-            c0, c1, c2 = 48 * j, 48 * j + 24, 48 * j + 48
-            act(T.DP[:, 16 * c0:16 * c1], WD[:].indirect(off(oic, c0, c1)), F.Copy, wd + [okey(oic)], ["DP_%d" % (2 * j)])
-            cp(T.DP[:, 16 * c1:16 * c2], WD[:].indirect(off(oic, c1, c2)), wd + [okey(oic)], ["DP_%d" % (2 * j + 1)])
+        PARTS = (((0, 48), (48, 96)), ((0, 32), (32, 96)))[r]
+
+        def verdicts(engine, out, slot, c0, c1, key):
+            if engine == "a":
+                act(out[:, 16 * c0:16 * c1], WD[:].indirect(off(slot, c0, c1)), F.Copy, wd + [okey(slot)], [key])
+            else:
+                cp(out[:, 16 * c0:16 * c1], WD[:].indirect(off(slot, c0, c1)), wd + [okey(slot)], [key])
+        DC = ((0, 24, 48, 72, 96), (0, 16, 32, D1, 96))[r]
+        for j in range(4):
+            verdicts("av"[j % 2], T.DP, oic, DC[j], DC[j + 1], "DP_%d" % j)
         dp = keys("DP", 4)
+        EC = (0, E1, 32, 48, 64, 80, 96)
         ohn = O_H[r + 1]
         nk = ["LC0", "LC1_0", "LC1_1"]
 
         def children(b, a, e, js):
             z = fld(b, 0, a, e)
+            new, nw = T.TI[:, 5 + 2 * r, a:e], ["IN%d_%d" % (r, j) for j in js]
             ts(off(ohn, a, e), z, 1 / 4096, -0.38, A.mult, A.add, ["P%d" % b], ["OL%d_%d" % (r, j) for j in js])
-            cp(T.TI[:, 5, a:e], z, ["P%d" % b], ["I5_%d" % j for j in js])
-            if r == 0:
-                ts(tm(8), ti(4), -2047.5, None, A.add, None, ["I4"], ["T8"])
-            ts(T.LC[:, 1, a:e], T.TI[:, 5, a:e], 4095, None, A.bitwise_and, None, ["I5_%d" % j for j in js], ["LC1_%d" % j for j in js])
+            cp(new, z, ["P%d" % b], nw)
+            ts(T.LC[:, 1, a:e], new, 4095, None, A.bitwise_and, None, nw, ["LC1_%d" % j for j in js])
             if r == 0:
                 lefts()
             cp(off(ohn + 1, a, e), T.LC[:, 1, a:e], ["LC1_%d" % j for j in js], ["OR%d_%d" % (r, j) for j in js])
 
         def lefts():
-            ts(T.LC[:, 0, :], ti(5), 12, None, A.arith_shift_right, None, keys("I5", 2), ["LC0"])
+            ts(T.LC[:, 0, :], ti(5 + 2 * r), 12, None, A.arith_shift_right, None, keys("IN%d" % r, 2), ["LC0"])
 
         def left_values(i):
-            act(T.HS[:, 256 * i:256 * i + 256], H[:].indirect(off(ohn, 16 * i, 16 * i + 16)), F.Copy, hk + ["OL%d_%d" % (r, i // 3)],
+            act(T.HS[:, 16 * EC[i]:16 * EC[i + 1]], H[:].indirect(off(ohn, EC[i], EC[i + 1])), F.Copy, hk + ["OL%d_%d" % (r, i > 1)],
                 ["HE_%d" % i])
 
         def values(i):
-            o = T.H1[:, SH + 256 * i:SH + 256 * i + 256] if r == 0 else T.OUT[:, 256 * i:256 * i + 256]
-            tt(o, H[:].indirect(off(ohn + 1, 16 * i, 16 * i + 16)), T.HS[:, 256 * i:256 * i + 256], A.max,
-               hk + ["OR%d_%d" % (r, i // 3), "HE_%d" % i], ["HI1_%d" % i if r == 0 else "OUT_%d" % i])
+            c0, c1 = 16 * EC[i], 16 * EC[i + 1]
+            o = T.H1[:, SH + c0:SH + c1] if r == 0 else T.OUT[:, c0:c1]
+            tt(o, H[:].indirect(off(ohn + 1, EC[i], EC[i + 1])), T.HS[:, c0:c1], A.max,
+               hk + ["OR%d_%d" % (r, i > 1), "HE_%d" % i], ["HI1_%d" % i if r == 0 else "OUT_%d" % i])
 
         def store(i0, i1):
-            dma("s", T.yh[:, 256 * i0:256 * i1], T.OUT[:, 256 * i0:256 * i1], ["OUT_%d" % j for j in range(i0, i1)], [])
+            c = slice(16 * EC[i0], 16 * EC[i1])
+            dma("s", T.yh[:, c], T.OUT[:, c], ["OUT_%d" % j for j in range(i0, i1)], [])
         if r == 1:
-            for j in range(2):
-                extract(6 + j, 0, Z_OWN, WD, SH, wd, False, False, part=(48 * j, 48 * j + 48))
-                extract(6 + j, 0, Z_KID, T.DP, 0, dp[2 * j:2 * j + 2], False, True, part=(48 * j, 48 * j + 48))
-            children(6, 0, 48, [0])
-            for i in range(3):
+            extract(6, 0, Z_OWN, WD, SH, wd, False, False, part=PARTS[0])
+            extract(6, 0, Z_KID, T.DP, 0, dp[:2], False, True, part=PARTS[0])
+            extract(7, 0, Z_OWN, WD, SH, wd, False, False, part=PARTS[1])
+            extract(7, 0, Z_KID, T.DP, 0, dp[2:], False, True, part=PARTS[1])
+            children(6, 0, 32, [0])
+            for i in range(2):
                 left_values(i)
             values(0)
             store(0, 1)
-            children(7, 48, 96, [1])
-            for i in range(3, 6):
-                left_values(i)
-            values(1)
-            values(2)
-            store(1, 3)
+            children(7, 32, 96, [1])
             lefts()
+            for t in range(3):
+                gcopy(T.XT[:, 32 * t:32 * t + 32], T.LC[:, :, t::6], 32, nk, ["XT_%d" % t])
+            for i in range(2, 6):
+                left_values(i)
+            for t in range(3, 6):
+                act(T.XT[:, 32 * t:32 * t + 32], T.LC[:, :, t::6], F.Copy, nk, ["XT_%d" % t])
+            values(1)
+            store(1, 2)
+            values(2)
             values(3)
-            for t in range(6):
-                ts(T.XT[:, 32 * t:32 * t + 32], T.LC[:, :, t::6], -float(SH), None, A.add, None, nk, ["XT_%d" % t])
-            turn(T.YK[:], T.XT[:], keys("XT", 6), ["YK"])
+            store(2, 4)
             values(4)
-            store(3, 5)
+            turn(T.YK[:], T.XT[:], keys("XT", 6), ["YK"])
             for g0 in range(2):
-                act(T.YC[:, 96 * g0:96 * g0 + 96], T.YK[:, :, 16 * g0:16 * g0 + 16], F.Copy, ["YK"], ["YC_%d" % g0])
+                act(T.YC[:, 96 * g0:96 * g0 + 96], T.YK[:, :, 16 * g0:16 * g0 + 16], F.Identity, ["YK"], ["YC_%d" % g0], bias=-float(SH))
                 dma("a", T.yk[g0::2, :], T.YC[:, 96 * g0:96 * g0 + 96], ["YC_%d" % g0], [])
             values(5)
-            store(5, 6)
+            store(4, 6)
         else:
             extract(6, 0, Z_OWN, WD, SH, wd, False, False)
             for j in range(2):
                 extract(6, 0, Z_KID, T.DP, 0, dp[2 * j:2 * j + 2], False, j == 1, part=(48 * j, 48 * j + 48))
-            act(T.GB[:, 0:768], WD[:].indirect(off(opar, 0, 48)), F.Copy, wd + [okey(opar)], ["GB_0"])
-            cp(T.GB[:, 768:NI], WD[:].indirect(off(opar, 48, 96)), wd + [okey(opar)], ["GB_1"])
-            extract(0, 0, Z_ISW, WD, SH, wd)
-            tt(tm(6), ti(2), tm(3), A.add, ["I2", "T3"], ["T6"])
+            verdicts("a", T.GB, opar, 0, G1, "GB_0")
+            verdicts("v", T.GB, opar, G1, G2, "GB_1")
+            extract(7, 3, Z_ISW, WD, SH, wd, False, True)
+            extract(5, 0, Z_Z, WD, SH, wd, False, False)
             children(6, 0, 96, [0, 1])
-            tt(tm(9), fld(0, 0), tm(6), A.max, ["P0", "T6"], ["T9"])
+            verdicts("v", T.GB, opar, G2, 96, "GB_2")
             for s in range(2):
                 lastw[okey(ohn + s)] = lastw["O%s0_1" % "LR"[s]]
-            extract(1, 0, Z_T, T.GB, 0, keys("GB", 2))
-            extract(4, 2, Z_GP, T.GB, 0, keys("GB", 2), False, True)
-            extract(3, 1, Z_Z, T.GB, 0, keys("GB", 2))
-            plus(5, 0, [tm(9)], ["T9"], False, False)
-            extract(5, 0, Z_Z, WD, SH, wd, False, False)
-            for i in range(6):
+            for i in range(3):
                 left_values(i)
-            act(tm(4), fld(6, 0), F.Copy, ["P6"], ["T4"])
-            leaves_cap()
+            act(tm(9), fld(7, 3), F.Relu, ["P7"], ["T9"])
+            extract(1, 0, Z_T, T.GB, 0, keys("GB", 3))
+            extract(4, 2, Z_GP, T.GB, 0, keys("GB", 3), False, True)
+            extract(3, 1, Z_Z, T.GB, 0, keys("GB", 3))
+            plus(5, 0, [tm(9)], ["T9"], False, False)
+            for i in range(3, 6):
+                left_values(i)
+            act(tm(4), ti(5), F.Copy, keys("IN0", 2), ["T4"])
+            leaves_cap(OUTL, "OUTL")
             values(0)
             values(1)
-            tt(tm(10), fld(1, 0), tm(8), A.mult, ["P1", "T8"], ["T10"])
             values(2)
+            tt(tm(10), fld(1, 0), tm(8), A.mult, ["P1", "T8"], ["T10"])
+            values(3)
             ts(tm(11), tm(10), 0.0, None, A.is_gt, None, ["T10"], ["T11"])
             ts(tm(12), tm(10), 0.0, -1.0, A.is_lt, A.mult, ["T10"], ["T12"])
-            values(3)
-            tt(tm(13), fld(4, 2), tm(11), A.mult, ["T11", "P4"], ["T13"])
-            tt(tm(14), fld(3, 1), tm(12), A.mult, ["P3", "T12"], ["T14"])
-            plus(5, 0, [tm(13), tm(14)], ["T13", "T14"])
             values(4)
+            tt(tm(13), fld(4, 2), tm(11), A.mult, ["T11", "P4"], ["T13"])
+            plus(5, 0, [tm(13)], ["T13"], False, False)
             values(5)
+            tt(tm(14), fld(3, 1), tm(12), A.mult, ["P3", "T12"], ["T14"])
+            plus(5, 0, [tm(14)], ["T14"])
             tt(ti(3), T.LC[:, 0, :], T.LC[:, 1, :], A.min, nk, ["I3"])
             ts(off(O_IC[1]), ti(3), float(DUM), None, A.min, None, ["I3"], [okey(O_IC[1])])
             ts(off(O_SIB[1]), fld(5, 0), 1 / 4096, -0.44, A.mult, A.add, ["P5"], [okey(O_SIB[1])])

from concourse.bass import DstId, RemoteDMATransfer
from concourse.mybir import AluOpType, ActivationFunctionType

NI, NV, NG = 1536, 769, 256
SH = 7
DUM = NI + SH
GH = NI + NV + SH
WID = GH + 3 * NG
D1, E1, G1, G2, HV = 64, 16, 48, 80, 1088
NZ = 8

SCRATCH = {
    "KI": ("sbuf", [128, 2, 96], "int32"), "SLI": ("sbuf", [128, 48], "int32"),
    "HLI": ("sbuf", [128, NV], "int32"), "HII": ("sbuf", [128, NI], "int32"), "VI": ("sbuf", [128, NV], "int32"),
    "YT": ("sbuf", [128, NV], "float32"),
    "H0": ("sbuf", [128, WID], "bfloat16"), "H1": ("sbuf", [128, WID], "bfloat16"),
    "GS0": ("sbuf", [128, 3 * NG], "bfloat16"), "GS1": ("sbuf", [128, 3 * NG], "bfloat16"),
    "W1": ("sbuf", [128, WID], "bfloat16"), "W2": ("sbuf", [128, WID], "float32"),
    "W2B": ("sbuf", [128, DUM + 1], "bfloat16"), "SRC": ("sbuf", [128, NI], "float32"),
    "WB": ("sbuf", [128, DUM + 1], "float32"), "PB": ("sbuf", [128, DUM + 1], "float32"),
    "CW": ("sbuf", [128, DUM + 1], "bfloat16"), "WD": ("sbuf", [128, DUM + 1], "bfloat16"),
    "HS": ("sbuf", [128, NI], "bfloat16"), "M1": ("sbuf", [128, NI], "bfloat16"), "M2": ("sbuf", [128, NI], "bfloat16"),
    "TB": ("sbuf", [128, NI], "float32"), "GB": ("sbuf", [128, NI], "bfloat16"), "DP": ("sbuf", [128, NI], "bfloat16"),
    "OUT": ("sbuf", [128, NI + NV], "float32"),
    "N0": ("sbuf", [128, 96, 3], "float32"), "LC": ("sbuf", [128, 2, 96], "int32"),
    "TI": ("sbuf", [128, 8, 96], "int32"), "TM": ("sbuf", [128, 16, 96], "float32"),
    "OF": ("sbuf", [128, 15 * 96], "uint16"),
    "TC": ("sbuf", [128, 3, 2, 16], "float32"), "COL": ("sbuf", [128, 3, 32], "float32"),
    "TZ": ("sbuf", [128, NZ + 1, 4, 4, 2], "bfloat16"), "TY": ("sbuf", [128, NZ + 1, 32], "bfloat16"),
    "XX": ("sbuf", [128, 96, 8], "bfloat16"), "YY": ("sbuf", [128, 24, 32], "bfloat16"),
    "XT": ("sbuf", [128, 192], "float32"), "YK": ("sbuf", [128, 6, 32], "float32"), "YC": ("sbuf", [128, 192], "float32"),
    "UU": ("sbuf", [128, 12, 10, 16], "bfloat16"),
    "CB": ("sbuf", [128, 6, 16, 4, 2], "bfloat16"), "FF": ("sbuf", [128, 16, 4, 2], "float32"),
    "CODE": ("sbuf", [128, 8, 8], "float32"),
    "ID": ("sbuf", [128, 128], "bfloat16"), "IF": ("sbuf", [128, 128], "float32"), "ZZ": ("sbuf", [128, NZ, 144], "bfloat16"),
}
for _k in range(6):
    SCRATCH["P%d" % _k] = ("psum", [128, 8, 64], "float32")
SCRATCH["P6"] = ("psum", [128, 128, 4], "float32")
SCRATCH["P7"] = ("psum", [128, 128, 4], "float32")

SEMAPHORES = ["sv", "sa", "st", "sg", "arr0", "arr1", "sent"] + ["d%d" % _k for _k in range(28)]


def rank_program(g, core, T, topo):
    rank = T.rank_of(core)
    if rank is None:
        return
    A = AluOpType
    F = ActivationFunctionType
    n_ranks = len(T.cores)
    eng = {"v": g.vector, "a": g.scalar, "t": g.tensor, "g": g, "s": g.sync}
    qsem = {"v": "sv", "a": "sa", "t": "st", "g": "sg"}
    total = {}
    waited = {q: {} for q in eng}
    lastw, readers = {}, {}
    ndma = [0]

    def bank(k):
        return k[0] == "P" and k[1:].isdigit()

    def sync(q, reads, writes):
        need = {}
        deps = [lastw[k] for k in list(reads) + list(writes) if k in lastw and not (bank(k) and lastw[k][0] == qsem.get(q))]
        for k in writes:
            deps += readers.get(k, [])
        for s, c in deps:
            if q == "t" and s == "st":
                continue
            need[s] = max(need.get(s, 0), c)
        for s, c in need.items():
            if waited[q].get(s, 0) < c:
                eng[q].wait_ge(T.sem[s], c)
                waited[q][s] = c

    def done(tok, reads, writes):
        for k in reads:
            readers.setdefault(k, []).append(tok)
        for k in writes:
            lastw[k] = tok
            readers[k] = []

    def op(q, call, reads, writes):
        writes = list(writes) + [k for k in reads if bank(k)]
        sync(q, reads, writes)
        s = qsem[q]
        call().then_inc(T.sem[s], 1)
        total[s] = total.get(s, 0) + 1
        done((s, total[s]), reads, writes)

    def dma(q, out, in_, reads, writes, add=False):
        sync(q, reads, writes)
        s = "d%d" % ndma[0]
        ndma[0] += 1
        eng[q].dma_start(out, in_, **({"accum_op": A.add} if add else {})).then_inc(T.sem[s], 16)
        total[s] = 16
        done((s, 16), reads, writes)

    V, S_, PE = g.vector, g.scalar, g.tensor

    def ts(out, in0, s1, s2, o0, o1, reads, writes):
        if o1 is None:
            op("v", lambda: V.tensor_scalar(out, in0, s1, None, o0), reads, writes)
        else:
            op("v", lambda: V.tensor_scalar(out, in0, s1, s2, o0, o1), reads, writes)

    def tt(out, a, b, o, reads, writes):
        op("v", lambda: V.tensor_tensor(out, a, b, o), reads, writes)

    def cp(out, in_, reads, writes):
        op("v", lambda: V.tensor_copy(out, in_), reads, writes)

    def fill(ap, val, writes):
        op("v", lambda: V.memset(ap, val), [], writes)

    def turn(out, in_, reads, writes):
        op("v", lambda: V.transpose(out, in_), reads, writes)

    def act(out, in_, func, reads, writes, bias=None, scale=None):
        kw = {}
        if bias is not None:
            kw["bias"] = bias
        if scale is not None:
            kw["scale"] = scale
        op("a", lambda: S_.activation(out, in_, func, **kw), reads, writes)

    def mms(lst, reads, writes):
        def run():
            ins = None
            for out, lhs, rhs, st, sp in lst:
                ins = PE.matmul(out, lhs, rhs, st, sp)
            return ins
        op("t", run, reads, writes)

    parts = {}

    def aff(ap, pattern, base, val, key, cells):
        mine = parts.setdefault(key, [])
        ks = ["%s.%s" % (key, c) for c in cells]
        op("g", lambda: g.affine_select(ap, ap, pattern, A.not_equal, float(val), base, 1), [key] + ks, ks)
        mine += [k for k in ks if k not in mine]

    def gfill(ap, n, val, key):
        mine = parts.setdefault(key, [])
        k = "%s.%d" % (key, len(mine))
        op("g", lambda: g.iota(ap, [[0, n]], val, 0, allow_small_or_imprecise_dtypes=True), [key], [k])
        mine.append(k)

    def const(key):
        return [key] + parts.get(key, [])

    def in_group(out, in_, lead, tail, reads, key):
        op("g", lambda: g.affine_select(out, in_, lead + [[-16, 8]] + tail, A.is_ge, 0.0, 0, 1), reads, [key])
        op("g", lambda: g.affine_select(out, out, lead + [[16, 8]] + tail, A.is_ge, 0.0, 15, -1), [key], [key])

    def keys(name, n):
        return ["%s_%d" % (name, i) for i in range(n)]

    PS = [T["P%d" % k] for k in range(8)]
    O_H = [0, 2, 4]
    O_SIB, O_SIC, O_PAR, O_IC, O_SL = [6, 7], [8, 9], [10, 11], [12, 13], 14

    def off(slot, c0=0, c1=96):
        return T.OF[:, slot * 96 + c0: slot * 96 + c1]

    def okey(slot):
        return "OF%d" % slot

    def fld(b, f, a=0, e=96):
        if b >= 6:
            return PS[b][:, 24 * f + a // 4:24 * f + e // 4, :]
        return PS[b][:, 2 * f + a // 48:2 * f + e // 48, 0:48]

    Z_W1, Z_W2, Z_GP, Z_OWN, Z_KID, Z_Z, Z_ISW, Z_T = range(NZ)

    def extract(b, f, zset, src, c0, reads, first=True, last=True, part=(0, 96)):
        a, e = part
        mms([(fld(b, f, a, e), T.ZZ[:, zset, 15 - r:143 - r], src[:, c0 + 16 * a + r:c0 + 16 * e:16],
              first and r == 0, last and r == 15) for r in range(16)], reads + ["ZZ%d" % (zset >= Z_GP)], ["P%d" % b])

    def plus(b, f, lists, reads, first=False, last=True):
        mms([(fld(b, f), T.IF[:], x, first and i == 0, last and i == len(lists) - 1) for i, x in enumerate(lists)],
            reads + const("IF"), ["P%d" % b])

    def from_y(b, k, U, t, mode):
        return [(PS[b][:, :, 16 * cl:16 * cl + 16], U[:, 4 * t + cl, 1 - g0:9 - g0, :],
                 T.YY[:, 8 * k:8 * k + 8, 16 * g0:16 * g0 + 16],
                 (mode == "alone" and g0 == 0) or (mode == "open" and cl + g0 == 0), mode == "alone" and g0 == 1)
                for cl in range(4) for g0 in range(2)]

    def engines_of(src, dst, d):
        e = topo.engines(src, dst)
        h = len(e) // 2
        return [e, e[:h], e[h:]][d - 1]

    def send(src, skeys, dst, sem):
        trs = []
        for d in range(1, n_ranks):
            peer = T.cores[(rank + d) % n_ranks]
            e = engines_of(core, peer, d)
            rid, pid, _ = topo.addr(peer)
            trs.append(RemoteDMATransfer(dst_ids=[DstId(rid=rid, pnc=pid)], dma_engine_mask=sum(1 << x for x in e),
                                         remote_sem=T.sem[sem], src=src[:, (d - 1) * NG:d * NG],
                                         dst=dst[:, GH + (d - 1) * NG:GH + d * NG]))
            total["sent"] = total.get("sent", 0) + len(e)
        for key, some in zip(skeys, (trs[:1], trs[1:])):
            sync("g", [key], [])
            g.remote_dma_fused(some, local_sem=T.sem.sent)

    def tm(i):
        return T.TM[:, i, :]

    def ti(i):
        return T.TI[:, i, :]

    arrive = sum(len(engines_of(T.cores[(rank - d) % n_ranks], core, d)) for d in range(1, n_ranks))
    for r in range(2):
        total["arr%d" % r] = arrive
        lastw["HG%d" % r] = ("arr%d" % r, arrive)

    dma("s", T.KI[:, 0, :], T.kl[:], [], ["KI0"])
    dma("a", T.KI[:, 1, :], T.kr[:], [], ["KI1"])
    dma("s", T.HLI[:], T.h0[:, NI:NI + NV], [], ["HLI"])
    dma("a", T.SLI[:], T.sl[:], [], ["SLI"])
    dma("s", T.HII[:], T.h0[:, 0:NI], [], ["HII"])

    LANE, BA, BW, BD = T.COL[:, 0, 0:1], T.COL[:, 1, 0:1], T.COL[:, 2, 0:1], T.TY[:, NZ, 0:1]
    WB, PB, CW, WD = T.WB, T.PB, T.CW, T.WD
    AW, BB, MC = T.CB, [T.CB[:, 2], T.CB[:, 3]], [T.CB[:, 4], T.CB[:, 5]]
    fill(T.W1[:, 0:16], 0.0, ["W1a"])
    act(T.W2[:, 0:16], T.W1[:, 0:16], F.Silu, ["W1a"], ["W2a"])
    fill(T.UU[:], 0.0, ["US", "UU"])
    fill(T.W1[:, 16:DUM + 1], 0.0, ["W1"])
    act(T.W2[:, 16:DUM + 1], T.W1[:, 16:DUM + 1], F.Copy, ["W1", "W2a"], ["W2"])
    act(T.ZZ[:, 0:4], T.W1[:, 16:16 + 4 * 144], F.Copy, ["W1"], ["ZZ0"])
    op("g", lambda: g.iota(T.TC[:, 0], [[0, 2], [1, 16]], 0, 0, allow_small_or_imprecise_dtypes=True), [], ["TC0"])
    op("g", lambda: g.iota(tm(0), [[16, 96]], SH + 8192, 0, allow_small_or_imprecise_dtypes=True), [], ["T0"])
    op("g", lambda: g.iota(T.CODE[:], [[-16, 8], [0, 8]], 0, 1, allow_small_or_imprecise_dtypes=True), [], ["CODE"])
    pu = [[-8, 4], [-32, 4]]
    aff(T.UU[:, 8:12, 1:9:2, 0:3], pu + [[-1, 3]], 0, 1 / 64, "US", "h")
    aff(T.UU[:, 8:12, 1:9:2, 3:6], pu + [[-1, 3]], -3, 1, "US", "l")
    aff(T.UU[:, 8:12, 1:9:2, 0:3], pu + [[0, 3]], -7, -248, "US", "h")
    turn(T.COL[:, 0], T.TC[:, 0], ["TC0"], ["LANE"])
    fill(T.XX[:, :, 6], 0.0, ["XX6"])
    ts(T.N0[:, :, 0], tm(0), LANE, None, A.add, None, ["T0", "LANE"], ["N00"])

    for s in (1, 0):
        ts(T.N0[:, :, 1 + s], T.KI[:, s, :], SH + 8192.0, None, A.add, None, ["KI%d" % s], ["N0%d" % (1 + s)])
    nk0 = ["N00", "N01", "N02"]
    fill(T.XX[:, :, 7], 1.0, ["XX7"])
    cp(T.XX[:, :, 0:3], T.N0[:], nk0, ["XXh"])
    cp(off(O_SL, 0, 48), T.SLI[:], ["SLI"], [okey(O_SL)])
    XK = ["XXh", "XXl", "XX6", "XX7"]
    for c0, c1, ks in ((0, 32, (0,)), (32, 96, (1, 2))):
        tt(T.XX[:, c0:c1, 3:6], T.N0[:, c0:c1], T.XX[:, c0:c1, 0:3], A.subtract, nk0 + ["XXh"], ["XXl%d" % c0])
    for c0, c1, ks in ((0, 32, (0,)), (32, 96, (1, 2))):
        turn(T.YY[:, c0 // 4:c1 // 4], T.XX[:, c0:c1], ["XXh", "XXl%d" % c0, "XX6", "XX7"], ["YY%d" % c0])
        for k in ks:
            mms(from_y(k, k, T.UU, 2, "alone"), ["YY%d" % c0] + const("US"), ["P%d" % k])
    lastw["YY"], lastw["XXl"] = lastw["YY32"], lastw["XXl32"]
    ts(off(O_H[0], 0, 192), T.KI[:], float(SH), None, A.add, None, ["KI0", "KI1"], [okey(O_H[0]), okey(O_H[0] + 1)])
    fill(T.CB[:], 0.0, ["AW", "BB", "MC", "SM"])
    BLOCKS = ((0, 16), (16, 48))
    for j, (c0, c1) in enumerate(BLOCKS):
        cp(T.GS0[:, 16 * c0:16 * c1], T.HLI[:].indirect(off(O_SL, c0, c1)), ["HLI", okey(O_SL)], ["GS0_%d" % j])
    third = [slice(512 * k, 512 * k + 512) for k in range(3)]
    third7 = [slice(SH + 512 * k, SH + 512 * k + 512) for k in range(3)]
    pz = [[-16, 8]]

    def affu(U, key, lane, f, step, val):
        aff(U[:, 0:8, 1:9:2, lane], [[step, 2]] + pu, -f, val, key, [lane])
    for lane, f, step, val in ((4, 1, -1, 2.0 ** -16), (5, 4, -1, 2.0 ** -10), (4, 4, -1, 2.0 ** -10), (6, 2, 1, 2.0 ** -16),
                               (7, 5, 1, 2.0 ** -10), (0, 7, 0, -21 / 16), (4, 7, 0, 134 / 1024), (5, 7, 0, 0.25),
                               (6, 7, 0, -0.125), (7, 7, 0, 33 / 1024)):
        affu(T.UU, "UU", lane, f, step, val)
    gfill(T.H0[:, 0:SH], SH, 255, "HZ0")
    send(T.GS0, keys("GS0", 2), T.H0, "arr0")
    QC = [0, 32, 64, 84, 96]
    quarter = [slice(SH + 16 * QC[b], SH + 16 * QC[b + 1]) for b in range(4)]
    PQ = [PS[b][:, 0:(QC[b + 1] - QC[b]) // 4, :] for b in range(4)]
    for k in range(2):
        act(T.SRC[:, third[k]], PS[k][:], F.Identity, ["P%d" % k], ["SRC_%d" % k], bias=128.0)
    ts(T.SRC[:, third[2]], PS[2][:], 128.0, None, A.add, None, ["P2"], ["SRC_2"])
    for c0, c1 in ((0, 64), (64, 96)):
        act(T.W2[:].indirect(off(O_H[0] + 1, c0, c1)), T.SRC[:, 16 * c0:16 * c1], F.Silu, keys("SRC", c1 // 32) + [okey(O_H[0] + 1)], ["W2"])
    act(T.W2B[:, SH:SH + 1024], T.W2[:, SH:SH + 1024], F.Copy, ["W2"], ["W2B_0"])
    act(T.H0[:, DUM:GH], T.HLI[:], F.Copy, ["HLI"], ["HL0"])
    act(T.H0[:, SH + HV:DUM], T.HII[:, HV:NI], F.Copy, ["HII"], keys("HI0", 6)[3:])
    cp(T.W1[:].indirect(off(O_H[0])), T.SRC[:], keys("SRC", 3) + [okey(O_H[0])], ["W1", "W1a"])
    cp(T.W2B[:, SH + 1024:DUM], T.W2[:, SH + 1024:DUM], ["W2"], ["W2B_1"])
    for s in range(2):
        ts(T.CB[:, 2 + s, 0::2], T.CODE[:], LANE, 1.0 - 2 * s, A.is_equal, A.mult, ["CODE", "LANE", "BB"], ["BB%d" % s])
    for s in range(2):
        ts(T.CB[:, 2 + s, 1::2, 0, 0], T.CODE[:, :, 0], LANE, 1.0 - 2 * s, A.is_equal, A.mult, ["CODE", "LANE", "BB%d" % s], ["BB%d" % s])
    cp(T.H0[:, SH:SH + HV], T.HII[:, 0:HV], ["HII"], keys("HI0", 3))
    w2b = keys("W2B", 2)

    def gcopy(out, in_, n, reads, writes):
        op("g", lambda: g.affine_select(out, in_, [[0, n]], A.is_ge, 0.0, 0, 0), reads, writes)

    for t in (1, 0):
        for k in range(3):
            mms(from_y(3 * t + k, k, T.UU, t, "open"), ["YY"] + const("UU"), ["P%d" % (3 * t + k)])
    both = [[0, 2]] + pz
    zs = [(T.ZZ[:, z0:z1, 15:128:16], [[step, z1 - z0]] + pz, -lane, val, "ZZ0", "z")
          for z0, z1, step, lane, val in ((0, 2, 1, 2, 2.0 ** 18), (0, 2, 1, 5, 4096), (0, 2, 0, 0, 64), (0, 2, 0, 3, 1), (0, 1, 0, 7, 16))]
    ZOFF = 640.0 * 4097
    ws = [(AW[:, 0:2, 0::2, 0, 0], both, 0, 1 / 32, "AW", "k"), (AW[:, 0, 0::2, 1:4, :], pz + [[0, 6]], -6, 1 / 256, "AW", "d"),
          (AW[:, 0:2, 0::2, 0, 0], both, -3, 1 / 2048, "AW", "k"), (AW[:, 0:2, 0::2, 2, 0], [[1, 2]] + pz, -2, -1 / 1024, "AW", "d"),
          (AW[:, 0, 1::2, 1, 0], pz, -6, 1, "AW", "s"), (AW[:, 0:2, 0::2, 2, :], [[1, 2]] + pz + [[0, 2]], -5, -1 / 1024, "AW", "d"),
          (AW[:, 0:2, 1::2, 2, :], both + [[-3, 2]], 0, 1, "AW", "p"), (AW[:, 0, 1::2, 0, 0], pz, -6, 1 / 256, "AW", "o")]
    gfill(T.TC[:, 1:3], 64, 0, "TCz")
    lastw["TC"] = lastw["TCz.0"]
    for z, w in zip(zs, ws):
        aff(*z)
        aff(*w)
    for w in ws[len(zs):]:
        aff(*w)
    zz0 = const("ZZ0")
    OUTL = T.OUT[:, NI:NI + NV]
    for l0, l1, val in ((3, 9, 0.25), (7, 8, 0.25 + 1 / 2048)):
        op("g", lambda: g.affine_select(T.TC[:, 1, :, l0:l1], T.TC[:, 1, :, l0:l1], [[0, 2 * (l1 - l0)]], A.is_gt, val, 0, 0),
           ["TC"], ["TC"])
    for l0, l1, val in ((8, 10, 4096), (10, 11, 256)):
        gfill(T.TC[:, 2, :, l0:l1], 2 * (l1 - l0), val, "TC")
    gfill(T.IF[:], 128, 0, "IFz")
    lastw["IF"] = lastw["IFz.0"]
    gfill(T.FF[:], 128, 0, "FFz")
    lastw["FF"] = lastw["FFz.0"]

    def no_node(Ws, key):
        for W in Ws:
            gfill(W[:, 0:SH], SH, 0, key)
            gfill(W[:, DUM:DUM + 1], 1, 0, key)
    no_node((WB, PB), "WPz")
    aff(T.IF[:], [[-1, 128]], 0, 1, "IF", "i")
    evens, one, two = slice(0, 3, 2), slice(1, 2), slice(2, 3)
    for s, k, lane, val in ((None, slice(0, 3), 3, -1024), (0, evens, 1, -512), (1, evens, 1, 512), (0, one, 2, -1024), (1, one, 2, 1024),
                            (0, evens, 2, 512), (1, evens, 2, -512), (1, one, 3, -3072), (None, one, 8, 1024), (0, two, 10, -2),
                            (None, one, 9, -1024), (1, two, 10, 2)):
        if (s, lane) == (1, 2) and k == one:
            dma("g", T.HLI[:], T.vel[:], ["HLI"], ["HLI"], True)
            dma("s", T.VI[:], T.vel[:], ["HL0", okey(O_H[0])] + keys("HI0", 6), ["VI"])
        ss, kk = ([0, 1] if s is None else [s]), range(4)[k]
        aff(T.FF[:, ss[0]::3 - len(ss), k, :], pz + [[0, 2 * len(ss) * len(kk)]], -lane, val, "FF", [(a, b) for a in ss for b in kk])
    aff(T.FF[:, 0::2, 3, 0], pz, -1, 64, "FF", [(0, 3)])
    aff(T.FF[:, :, 2, :], pz + [[0, 2], [-1, 2]], -6, 1024, "FF", [(0, 2), (1, 2)])
    aff(T.FF[:, 0::2, 3, 0], pz, -2, -64, "FF", [(0, 3)])
    aff(T.FF[:, :, 0:2, 0], pz + [[0, 4]], -4, 1024, "FF", [(a, b) for a in range(2) for b in range(2)])
    aff(T.FF[:, 0::2, 3, :], pz + [[-1, 2]], -12, 1, "FF", [(0, 3)])
    aff(T.FF[:, :, 0:2, 1], pz + [[0, 4]], -5, 1024, "FF", [(a, b) for a in range(2) for b in range(2)])

    def verdict_weights():
        no_node((CW, WD), "CDz")
        for m in range(2):
            aff(T.CB[:, 4 + m, :, 0:3, :], pz + [[0, 12]], 0, 1024 * m - 512, "MC", [m])

    def list_weights():
        for z, s, k0, k1, d, base, step in (
                (Z_OWN, 0, 1, 2, 0, -64 * 4096, 0), (Z_OWN, 0, 1, 2, 1, 63 * 4096, 0), (Z_OWN, 1, 1, 2, None, -64, 127),
                (Z_KID, 0, 0, 1, None, 64, -127), (Z_KID, 1, 0, 1, 0, 64 * 4096, 0), (Z_KID, 1, 0, 1, 1, -63 * 4096, 0),
                (Z_Z, None, 1, 3, 0, 64 * 4096, 0), (Z_Z, None, 1, 2, 1, -63 * 4096, 0), (Z_Z, None, 2, 3, 1, 4096, 0),
                (Z_ISW, None, 2, 3, 1, -7 * 2 ** 21, 0), (Z_T, None, 1, 2, 1, 1, -2), (Z_GP, 0, 3, 4, None, 64, -63),
                (NZ, None, 0, 2, None, -768, 256), (NZ, None, 2, 3, None, -256, -1024), (NZ, 0, 3, 4, 0, 32, 0)):
            n = (k1 - k0) * (2 if d is None else 1)
            ap = T.TZ[:, z, slice(0, 4) if s is None else slice(s, 4, 2), k0:k1, slice(0, 2) if d is None else d]
            pattern = [[0, 2], [step, 2], [0, n]] if s is None else [[0, 2], [step, n]]
            key = "TZ1.%d" % len(parts.setdefault("TZ1", []))
            op("g", lambda: g.iota(ap, pattern, base, 0, allow_small_or_imprecise_dtypes=True), ["TZ1"], [key])
            parts["TZ1"].append(key)

    def place_weights():
        turn(T.TY[:, Z_GP:], T.TZ[:, Z_GP:], const("TZ1"), ["TY"])
        in_group(T.ZZ[:, Z_GP:NZ, 15:128:16], T.TY[:, Z_GP:NZ, 0:8], [[0, NZ - Z_GP]], [], ["TY", "ZZ1"], "ZZ1")

    def late_weights():
        for lane, f, val in ((0, 0, 2.0 ** -11), (4, 7, -66 / 1024), (0, 3, 2.0 ** -11), (5, 7, 0.125), (0, 6, -1), (8, 6, 0.5), (0, 7, -5)):
            affu(T.UU, "UU", lane, f, 0, val)
        for t in range(2):
            aff(T.UU[:, 4 * t:4 * t + 4, 1:9:2, 2:6], pu + [[0, 4]], -6, 0.5, "UU", [2, 3, 4, 5])

    def each_bank(lhs, src, reads, start, ks=(0, 1, 2), sides=(0, 1)):
        for k in ks:
            for t in sides:
                mms([(PS[3 * t + k][:], lhs, src[:, third7[k]], start, False)], reads, ["P%d" % (3 * t + k)])

    def unpack_late(r):
        ts(ti(1), ti(0), 2047, None, A.bitwise_and, None, ["I0"], ["I1"])
        if r == 0:
            ts(ti(2), ti(0), 12, None, A.arith_shift_right, None, ["I0"], ["I2"])
        cp(off(O_PAR[r]), ti(1), ["I1"], [okey(O_PAR[r])])
        if r == 0:
            ts(off(O_SIC[r]), ti(2), float(DUM), None, A.min, None, ["I2"], [okey(O_SIC[r])])
        else:
            ts(off(O_SIC[r]), ti(6), 12288.0, float(DUM), A.add, A.min, ["I6"], [okey(O_SIC[r])])

    extract(7, 4, Z_W1, T.W1, SH, ["W1"] + zz0, True, False)
    extract(7, 4, Z_W2, T.W2B, SH, w2b + zz0, False, True)
    each_bank(AW[:, 0], T.W1, ["W1"] + const("AW"), False, (0, 1, 2), (0,))
    ts(off(O_SIB[0]), fld(7, 4), 1 / 4096, -0.44 - ZOFF / 4096, A.mult, A.add, ["P7"], [okey(O_SIB[0])])
    ts(ti(0), fld(7, 4), -ZOFF, 0.0, A.add, A.max, ["P7"], ["I0"])
    unpack_late(0)
    turn(T.COL[:, 1:3], T.TC[:, 1:3], const("TC"), ["BA"])
    tt(ti(3), T.KI[:, 0, :], T.KI[:, 1, :], A.min, ["KI0", "KI1"], ["I3"])

    def leaves_cap(moved, key):
        act(T.YT[:], moved, F.Relu, [key], ["YT"], bias=255.0, scale=-1.0)

    def leaves_out(out, key):
        act(out, T.YT[:], F.Relu, ["YT"], [key], bias=255.0, scale=-1.0)
    verdict_weights()
    op("g", lambda: g.iota(T.TZ[:, Z_GP:], [[0, 32 * (NZ + 1 - Z_GP)]], 0, 0, allow_small_or_imprecise_dtypes=True), [], ["TZ1"])
    list_weights()
    gcopy(OUTL, T.VI[:], NV, ["VI"], ["OUTL"])

    for r in range(2):
        H = [T.H0, T.H1][r]
        hk = keys("HI%d" % r, 6) + ["HL%d" % r, "HG%d" % r] + const("HZ%d" % r)
        oh, osib, osic, opar, oic = O_H[r], O_SIB[r], O_SIC[r], O_PAR[r], O_IC[r]
        def siblings(i):
            c0, c1 = ((0, 16), (16, 32), (32, 64), (64, 96))[i]
            act(T.HS[:, 16 * c0:16 * c1], H[:].indirect(off(osib, c0, c1)), F.Copy, hk + [okey(osib)], ["HS_%d" % i])

        def ids(k, t):
            if r == 1:
                mms(from_y(3 * t + k, k, T.UU, t, "part"), ["YY_%d" % k] + const("UU"), ["P%d" % (3 * t + k)])
                return
            if t == 1:
                each_bank(AW[:, 0], T.W1, ["W1"] + const("AW"), False, (k,), (t,))
            each_bank(AW[:, 1], T.W2B, w2b + const("AW"), False, (k,), (t,))
            each_bank(BB[0], T.H0, keys("HI0", 6) + ["BB0"], False, (k,), (t,))

        def best(k):
            tt(WB[:, third7[k]], PS[3 + k][:], T.TB[:, third[k]], A.max, ["P%d" % (3 + k), "TA_%d" % k], ["WB_%d" % k])
            if (r, k) == (1, 1):
                act(PS[4][:], WB[:, third7[k]], F.Identity, ["WB_%d" % k], ["P4"], bias=BW)
            else:
                act(T.SRC[:, third[k]], WB[:, third7[k]], F.Identity, ["WB_%d" % k], ["SRC_%d" % k], bias=BW)

        def digits():
            N1 = PS[7][:, 0:96, 0:3]
            tt(PS[7][:, 0:96, 1], T.LC[:, 0, :], ti(6), A.subtract, ["LC0", "I6"], ["P7", "N10"])
            ts(ti(4), ti(0), 4095, None, A.bitwise_and, None, ["I0"], ["I4"])
            tt(PS[7][:, 0:96, 2], T.LC[:, 1, :], ti(6), A.subtract, ["LC1_1", "I6"], ["P7", "N11"])
            ts(PS[7][:, 0:96, 0], ti(4), 8192.0, None, A.add, None, ["I4"], ["P7", "N12"])
            nk1 = ["P7", "N10", "N11", "N12"]
            ts(T.XX[:, :, 6], ti(4), 2048.0, None, A.is_ge, None, ["I4"], ["XX6"])
            cp(T.XX[:, :, 0:3], N1, nk1, ["XXh"])
            tt(T.XX[:, :, 3:6], N1, T.XX[:, :, 0:3], A.subtract, nk1 + ["XXh"], ["XXl"])
            for k in (1, 0, 2):
                turn(T.YY[:, 8 * k:8 * k + 8], T.XX[:, 32 * k:32 * k + 32], XK, ["YY", "YY_%d" % k] if k == 1 else ["YY_%d" % k])
        def larger(k, t):
            M, mn = ((T.M1, "M1"), (T.M2, "M2"))[t]
            pieces = ((0, 16, 0), (16, 32, 1)) if k + t == 0 else ((32 * k, 32 * k + 32, k + 1),)
            for c0, c1, i in pieces:
                tt(M[:, 16 * c0:16 * c1], H[:].indirect(off(oh + 1 - t, c0, c1)), T.HS[:, 16 * c0:16 * c1], A.max,
                   hk + [okey(oh + 1 - t), "HS_%d" % i], ["%s_%d" % (mn, i)])
            mms([(PS[3 * t + k][:], BB[1], M[:, third[k]], False, True)],
                ["%s_%d" % (mn, i) for c0, c1, i in pieces] + ["BB1"], ["P%d" % (3 * t + k)])

        def first(k):
            act(T.TB[:, third[k]], PS[k][:], F.Relu, ["P%d" % k, "BA"], ["TA_%d" % k], bias=BA)

        def other():
            act(T.DP[:, third[1]], H[:].indirect(off(oh, 32, 64)), F.Copy, hk + [okey(oh)], ["HK"], scale=-1.0)

        def less():
            mms([(PS[6][:], T.ID[:], T.DP[:, third[1]], True, False), (PS[6][:], T.ID[:], T.HS[:, third[1]], False, True)],
                const("ID") + ["HK", "HS_2"], ["P6"])
            mms([(PS[4][:], BB[0], T.DP[:, third[1]], False, False)], ["HK", "BB0"], ["P4"])

        def over():
            act(T.M2[:, third[1]], PS[6][:], F.Relu, ["P6"], ["M2_2"])

        def summed():
            mms([(PS[4][:], BB[1], T.M2[:, third[1]], False, True)], ["M2_2", "BB1"], ["P4"])
        if r == 0:
            for i in range(4):
                siblings(i)
            ids(0, 0)
            ids(1, 0)
            ids(0, 1)
            larger(0, 0)
            first(0)
            act(T.ZZ[:, 4:NZ], T.W2B[:, SH:SH + 144 * (NZ - 4)], F.Copy, w2b, ["ZZ1"], scale=0.0)
            act(tm(1), fld(7, 4), F.Relu, ["P7"], ["T1"], bias=-ZOFF)
            act(tm(4), T.N0[:, :, 1], F.Identity, ["N01"], ["T4"], scale=4096.0, bias=-(2.0 ** 25 + 8192))
            ids(2, 0)
            larger(0, 1)
            larger(1, 0)
            first(1)
            ids(1, 1)
            larger(2, 0)
            first(2)
            ids(2, 1)
            larger(1, 1)
            act(tm(5), ti(1), F.Identity, ["I1"], ["T5"], scale=4096.0, bias=33.0 * 4096 - 640)
            act(tm(6), ti(2), F.Identity, ["I2"], ["T6"], bias=-33.0 * 4096)
            act(tm(7), ti(2), F.Identity, ["I2"], ["T7"], scale=-1.0, bias=33.0 * 4096)
            act(tm(3), tm(1), F.Identity, ["T1"], ["T3"], scale=-1.0, bias=-33.0 * 4096)
            best(0)
            larger(2, 1)
            best(1)
            ts(ti(4), ti(0), 4095, None, A.bitwise_and, None, ["I0"], ["I4"])
            plus(7, 3, [tm(1), tm(7)], ["T1", "T7"], True, False)
            plus(6, 0, [T.N0[:, :, 2], tm(4)], ["N02", "T4"], True, False)
            plus(4, 2, [tm(3), tm(5)], ["T3", "T5"], True, False)
            best(2)
            ts(off(oic), ti(3), float(SH), float(DUM), A.add, A.min, ["I3"], [okey(oic)])
            plus(5, 0, [tm(6)], ["T6"], True, False)
        else:
            siblings(2)
            other()
            less()
            for i in (0, 1, 3):
                siblings(i)
            over()
            digits()
            ids(1, 0)
            larger(1, 0)
            first(1)
            ids(0, 0)
            larger(0, 0)
            first(0)
            leaves_out(OUTL, "OUTL")
            dma("s", T.yh[:, NI:NI + NV], OUTL, ["OUTL"], [])
            ids(1, 1)
            summed()
            ids(2, 0)
            larger(2, 0)
            ids(0, 1)
            larger(0, 1)
            best(1)
            first(2)
            ids(2, 1)
            larger(2, 1)
            best(0)
            unpack_late(1)
            best(2)
        wb = keys("WB", 3) + const("WPz")
        banks = ((0,), (1,), (2, 3))
        RAW = T.OUT[:, third[1]]
        if r == 1:
            act(RAW, WB[:].indirect(off(osic, 32, 64)), F.Copy, wb + [okey(osic)], ["RAW"])
        for k in (0, 2, 1):
            if (r, k) == (1, 1):
                tt(PB[:, third7[k]], PS[4][:], RAW, A.max, ["P4", "RAW"], ["PB_%d" % k])
            else:
                tt(PB[:, third7[k]], WB[:].indirect(off(osic, 32 * k, 32 * k + 32)), T.SRC[:, third[k]], A.max,
                   wb + [okey(osic), "SRC_%d" % k], ["PB_%d" % k])
            for b in banks[k]:
                mms([(PQ[b], T.FF[:], PB[:, quarter[b]], True, False)], ["PB_%d" % k] + const("FF"), ["P%d" % b])
            if (r, k) == (0, 0):
                dma("s", T.TB[:, third[k]], PB[:, third7[k]], ["PB_%d" % k], ["TA_%d" % k])
            elif (r, k) == (1, 1):
                act(PS[5][:], PB[:, third7[k]], F.Copy, ["PB_%d" % k], ["P5"])
                act(RAW, PB[:].indirect(off(oic, 32, 64)), F.Copy, keys("PB", 3) + const("WPz") + [okey(oic)], ["RAW"])
            else:
                act(T.TB[:, third[k]], PB[:, third7[k]], F.Copy, ["PB_%d" % k], ["TA_%d" % k])
            if (r, k) == (0, 0):
                leaves_cap(T.HLI[:], "HLI")
                act(tm(8), ti(4), F.Identity, ["I4"], ["T8"], bias=-2047.5)
        if r == 0:
            act(T.GS1[:], T.YT[:].indirect(off(O_SL, 0, 48)), F.Relu, ["YT", okey(O_SL)], ["GS1"], bias=255.0, scale=-1.0)
            leaves_out(T.H1[:, DUM:GH], "HL1")
            send(T.GS1, ["GS1", "GS1"], T.H1, "arr1")
            dma("g", OUTL, T.H1[:, DUM:GH], ["HL1", "OUTL"], ["OUTL"], True)
        pb = keys("PB", 3) + const("WPz")
        for k in ((2, 1, 0), (0, 2, 1))[r]:
            if (r, k) == (1, 1):
                tt(CW[:, third7[k]], PS[5][:], RAW, A.is_lt, ["P5", "RAW"], ["CW_%d" % k])
            else:
                tt(CW[:, third7[k]], PB[:].indirect(off(oic, 32 * k, 32 * k + 32)), T.TB[:, third[k]], A.is_gt,
                   pb + [okey(oic), "TA_%d" % k], ["CW_%d" % k])
            for b in banks[k]:
                mms([(PQ[b], MC[0], CW[:, quarter[b]], False, False)], ["CW_%d" % k] + const("MC"), ["P%d" % b])
        cw = keys("CW", 3)
        ck = cw + const("CDz")
        if r == 1:
            for b, a, e in ((6, 0, 32), (7, 32, 96)):
                mms([(fld(b, 0, a, e), T.IF[:], T.TM[:, 4, a:e], True, False)], ["T4"] + const("IF"), ["P%d" % b])
        for b in range(4):
            c0, c1 = QC[b], QC[b + 1]
            cp(T.M2[:, 16 * c0:16 * c1], CW[:].indirect(off(osic, c0, c1)), ck + [okey(osic)], ["CR_%d" % b])
            act(T.M1[:, 16 * c0:16 * c1], CW[:].indirect(off(opar, c0, c1)), F.Copy, ck + [okey(opar)], ["CL_%d" % b])
            mms([(PQ[b], MC[0], T.M2[:, 16 * c0:16 * c1], False, False),
                 (PQ[b], MC[1], T.M1[:, 16 * c0:16 * c1], False, True)], ["CR_%d" % b, "CL_%d" % b] + const("MC"), ["P%d" % b])
            if r == 0 and b == 2:
                place_weights()
                gfill(T.H1[:, 0:SH], SH, 255, "HZ1")
                gcopy(T.ID[:], T.IF[:], 128, const("IF"), ["ID"])
                late_weights()
        for b in range(4):
            if b % 2:
                act(WD[:, quarter[b]], PQ[b], F.Relu, ["P%d" % b, "TY"], ["WD_%d" % b], bias=BD)
            else:
                ts(WD[:, quarter[b]], PQ[b], BD, 0.0, A.add, A.max, ["P%d" % b, "TY"], ["WD_%d" % b])
        wd = keys("WD", 4) + const("CDz")
        PARTS = (((0, 48), (48, 96)), ((0, 32), (32, 96)))[r]

        def verdicts(engine, out, slot, c0, c1, key):
            if engine == "a":
                act(out[:, 16 * c0:16 * c1], WD[:].indirect(off(slot, c0, c1)), F.Copy, wd + [okey(slot)], [key])
            else:
                cp(out[:, 16 * c0:16 * c1], WD[:].indirect(off(slot, c0, c1)), wd + [okey(slot)], [key])
        DC = ((0, 24, 48, 72, 96), (0, 16, 32, D1, 96))[r]
        for j in range(4):
            verdicts("av"[j % 2], T.DP, oic, DC[j], DC[j + 1], "DP_%d" % j)
        dp = keys("DP", 4)
        EC = (0, E1, 32, 48, 64, 80, 96)
        ohn = O_H[r + 1]
        nk = ["LC0", "LC1_0", "LC1_1"]

        def children(b, a, e, js):
            z = fld(b, 0, a, e)
            new, nw = T.TI[:, 5 + 2 * r, a:e], ["IN%d_%d" % (r, j) for j in js]
            ts(off(ohn, a, e), z, 1 / 4096, -0.38, A.mult, A.add, ["P%d" % b], ["OL%d_%d" % (r, j) for j in js])
            cp(new, z, ["P%d" % b], nw)
            ts(T.LC[:, 1, a:e], new, 4095, None, A.bitwise_and, None, nw, ["LC1_%d" % j for j in js])
            if r == 0:
                lefts()
            cp(off(ohn + 1, a, e), T.LC[:, 1, a:e], ["LC1_%d" % j for j in js], ["OR%d_%d" % (r, j) for j in js])

        def lefts():
            ts(T.LC[:, 0, :], ti(5 + 2 * r), 12, None, A.arith_shift_right, None, keys("IN%d" % r, 2), ["LC0"])

        def left_values(i):
            act(T.HS[:, 16 * EC[i]:16 * EC[i + 1]], H[:].indirect(off(ohn, EC[i], EC[i + 1])), F.Copy, hk + ["OL%d_%d" % (r, i > 1)],
                ["HE_%d" % i])

        def values(i):
            c0, c1 = 16 * EC[i], 16 * EC[i + 1]
            o = T.H1[:, SH + c0:SH + c1] if r == 0 else T.OUT[:, c0:c1]
            tt(o, H[:].indirect(off(ohn + 1, EC[i], EC[i + 1])), T.HS[:, c0:c1], A.max,
               hk + ["OR%d_%d" % (r, i > 1), "HE_%d" % i], ["HI1_%d" % i if r == 0 else "OUT_%d" % i])

        def store(i0, i1):
            c = slice(16 * EC[i0], 16 * EC[i1])
            dma("s", T.yh[:, c], T.OUT[:, c], ["OUT_%d" % j for j in range(i0, i1)], [])
        if r == 1:
            extract(6, 0, Z_OWN, WD, SH, wd, False, False, part=PARTS[0])
            extract(6, 0, Z_KID, T.DP, 0, dp[:2], False, True, part=PARTS[0])
            extract(7, 0, Z_OWN, WD, SH, wd, False, False, part=PARTS[1])
            extract(7, 0, Z_KID, T.DP, 0, dp[2:], False, True, part=PARTS[1])
            children(6, 0, 32, [0])
            for i in range(2):
                left_values(i)
            values(0)
            store(0, 1)
            children(7, 32, 96, [1])
            lefts()
            for t in range(3):
                gcopy(T.XT[:, 32 * t:32 * t + 32], T.LC[:, :, t::6], 32, nk, ["XT_%d" % t])
            for i in range(2, 6):
                left_values(i)
            for t in range(3, 6):
                act(T.XT[:, 32 * t:32 * t + 32], T.LC[:, :, t::6], F.Copy, nk, ["XT_%d" % t])
            values(1)
            store(1, 2)
            values(2)
            values(3)
            store(2, 4)
            values(4)
            turn(T.YK[:], T.XT[:], keys("XT", 6), ["YK"])
            for g0 in range(2):
                act(T.YC[:, 96 * g0:96 * g0 + 96], T.YK[:, :, 16 * g0:16 * g0 + 16], F.Identity, ["YK"], ["YC_%d" % g0], bias=-float(SH))
                dma("a", T.yk[g0::2, :], T.YC[:, 96 * g0:96 * g0 + 96], ["YC_%d" % g0], [])
            values(5)
            store(4, 6)
        else:
            extract(6, 0, Z_OWN, WD, SH, wd, False, False)
            for j in range(2):
                extract(6, 0, Z_KID, T.DP, 0, dp[2 * j:2 * j + 2], False, j == 1, part=(48 * j, 48 * j + 48))
            verdicts("a", T.GB, opar, 0, G1, "GB_0")
            verdicts("v", T.GB, opar, G1, G2, "GB_1")
            extract(7, 3, Z_ISW, WD, SH, wd, False, True)
            extract(5, 0, Z_Z, WD, SH, wd, False, False)
            children(6, 0, 96, [0, 1])
            verdicts("v", T.GB, opar, G2, 96, "GB_2")
            for s in range(2):
                lastw[okey(ohn + s)] = lastw["O%s0_1" % "LR"[s]]
            for i in range(3):
                left_values(i)
            act(tm(9), fld(7, 3), F.Relu, ["P7"], ["T9"])
            extract(1, 0, Z_T, T.GB, 0, keys("GB", 3))
            extract(4, 2, Z_GP, T.GB, 0, keys("GB", 3), False, True)
            extract(3, 1, Z_Z, T.GB, 0, keys("GB", 3))
            plus(5, 0, [tm(9)], ["T9"], False, False)
            for i in range(3, 6):
                left_values(i)
            act(tm(4), ti(5), F.Copy, keys("IN0", 2), ["T4"])
            leaves_cap(OUTL, "OUTL")
            values(0)
            values(1)
            values(2)
            tt(tm(10), fld(1, 0), tm(8), A.mult, ["P1", "T8"], ["T10"])
            values(3)
            ts(tm(11), tm(10), 0.0, None, A.is_gt, None, ["T10"], ["T11"])
            ts(tm(12), tm(10), 0.0, -1.0, A.is_lt, A.mult, ["T10"], ["T12"])
            values(4)
            tt(tm(13), fld(4, 2), tm(11), A.mult, ["T11", "P4"], ["T13"])
            plus(5, 0, [tm(13)], ["T13"], False, False)
            values(5)
            tt(tm(14), fld(3, 1), tm(12), A.mult, ["P3", "T12"], ["T14"])
            plus(5, 0, [tm(14)], ["T14"])
            tt(ti(3), T.LC[:, 0, :], T.LC[:, 1, :], A.min, nk, ["I3"])
            ts(off(O_IC[1]), ti(3), float(DUM), None, A.min, None, ["I3"], [okey(O_IC[1])])
            ts(off(O_SIB[1]), fld(5, 0), 1 / 4096, -0.44, A.mult, A.add, ["P5"], [okey(O_SIB[1])])
            ts(ti(6), fld(5, 0), 1 / 4096, -12288.44, A.mult, A.add, ["P5"], ["I6"])
            cp(ti(0), fld(5, 0), ["P5"], ["I0"])
            each_bank(BB[0], T.H1, keys("HI1", 6) + ["BB0"], True)

    for s, c in total.items():
        if waited["g"].get(s, 0) < c:
            g.wait_ge(T.sem[s], c)
